import numpy as np
import ml_dtypes


def mxq(x, axis, fmt="e4m3"):
    dtype, down = {"e4m3": (ml_dtypes.float8_e4m3fn, 7), "e5m2": (ml_dtypes.float8_e5m2, 14)}[fmt]
    v = np.moveaxis(np.asarray(x, np.float32).astype(ml_dtypes.bfloat16).astype(np.float64), axis, -1)
    blocks = v.reshape(v.shape[:-1] + (-1, 32))
    amax = np.abs(blocks).max(-1, keepdims=True)
    byte = np.maximum(np.where(amax > 0, np.frexp(amax)[1] - 1 + 127, 0) - down, 1)
    scale = np.exp2(byte - 127.0)
    codes = (blocks / scale).astype(np.float32).astype(dtype).astype(np.float64)
    return np.moveaxis((codes * scale).reshape(v.shape), -1, axis)


WIDE = False


def mx_kscale(k):
    if not WIDE:
        return np.ones(k)
    levels = np.array([10, -10, 5, -5, 0])
    if k % 512:
        return np.exp2(np.random.permutation(np.resize(levels, k // 32))).repeat(32)
    a = np.empty((k // 512, 16))
    for p in range(k // 512):
        a[p, :8] = np.random.permutation(np.resize(levels, 8))
        for g in range(8):
            far = levels[np.abs(levels - a[p, g]) >= 10]
            a[p, g + 8] = far[np.random.randint(len(far))]
    return np.exp2(a.ravel()).repeat(32)


def f64(x):
    return np.asarray(x).astype(np.float64)


def striped(idx):
    return np.tile(np.asarray(idx).reshape(-1, 16).T, (8, 1)).astype(np.uint16)


def unstriped(offs):
    return offs[:16].T.reshape(-1).astype(np.int64)

def softplus(v):
    return np.log(1.0 + np.exp(v))


def rot(x):
    y = x.reshape(x.shape[0], -1, 2, x.shape[2])
    return np.stack([-y[:, :, 1], y[:, :, 0]], axis=2).reshape(x.shape)


B, N, T, D, NQ = 1, 512, 2048, 512, 256


def setup_inputs():
    n = np.random.standard_normal
    idx = np.random.permutation(T)[:B * N]
    idx2 = np.random.permutation(1024)[:B * N]
    s = mx_kscale(D)[:, None]
    ph = 2 * n((D // 2, 1024))
    return {
        "qT": (n((B, D, NQ)) * s * (1.00 / np.sqrt(D))).astype(np.float32),
        "kT": (np.clip(np.round(n((D, T)) * 16), -64, 64) / 16 / s).astype(np.float32),
        "cT": (np.repeat(np.round(np.cos(ph) * 64) / 64, 2, axis=0)).astype(np.float32),
        "wT": (np.repeat(np.round(np.sin(ph) * 64) / 64, 2, axis=0)).astype(np.float32),
        "mg": (np.random.uniform(0.5, 1.5, (B, NQ, 1))).astype(np.float32),
        "offs": striped(idx),
        "offs2": striped(idx2),
    }


def reference(qT, kT, cT, wT, mg, offs, offs2):
    idx = unstriped(offs)
    idx2 = unstriped(offs2)
    pick = lambda x, which: x[:, which].reshape(x.shape[0], B, -1).transpose(1, 0, 2)
    kg = pick(f64(kT), idx)
    cg = pick(f64(cT), idx2)
    wg = pick(f64(wT), idx2)
    ug = mxq(kg * cg + rot(kg) * wg, 1, "e4m3")
    qq = mxq(f64(qT), 1, "e4m3")
    a = qq.transpose(0, 2, 1) @ ug
    y = softplus(f64(mg) - a)
    return y

@@ -1,0 +1,150 @@
+from contextlib import ExitStack
+
+import concourse.mybir as mybir
+
+F32 = mybir.dt.float32
+BF16 = mybir.dt.bfloat16
+U32 = mybir.dt.uint32
+U16 = mybir.dt.uint16
+U8 = mybir.dt.uint8
+FP8X4 = mybir.dt.float8_e4m3fn_x4
+ALU = mybir.AluOpType
+ACT = mybir.ActivationFunctionType
+
+P = 128
+PACK = 4
+D, NQ, SLOTS = 512, 256, 512
+FLOPS = 2 * D * NQ * SLOTS
+CHUNKS = [(0, 128), (128, 256), (256, 384), (384, 512)]
+LOG_FLOOR = 2.0 ** -60
+
+
+def tile_attend_pre_rotate_f_topk_kernel(tc, qT, kT, cT, wT, mg, offs, offs2, out):
+    nc = tc.nc
+    n_ent = kT.shape[1]
+    n_rel = cT.shape[1]
+    q_tiles = NQ // P
+
+    with ExitStack() as ctx:
+        sb = ctx.enter_context(tc.tile_pool(name="sb", bufs=1))
+        ps = ctx.enter_context(tc.psum_pool(name="ps", bufs=1))
+
+        ent_list = sb.tile([P, SLOTS // 16], U16, name="ent_list")
+        rel_list = sb.tile([P, SLOTS // 16], U16, name="rel_list")
+        k_pl = [sb.tile([P, n_ent], F32, name="k%d" % t) for t in range(PACK)]
+        c_pl = [sb.tile([P, n_rel], F32, name="c%d" % t) for t in range(PACK)]
+        w_pl = [sb.tile([P, n_rel], F32, name="w%d" % t) for t in range(PACK)]
+        k_rows = kT.rearrange("(p t) n -> p t n", t=PACK)
+        c_rows = cT.rearrange("(p t) n -> p t n", t=PACK)
+        w_rows = wT.rearrange("(p t) n -> p t n", t=PACK)
+        q_raw = sb.tile([P, PACK, NQ], F32, name="q_raw")
+        margin = [sb.tile([P, 1], F32, name="margin%d" % m) for m in range(q_tiles)]
+        neg_margin = [sb.tile([P, 1], F32, name="neg_margin%d" % m) for m in range(q_tiles)]
+        floor = sb.tile([P, 1], F32, name="floor")
+
+        nc.sync.dma_start(k_pl[0][:], k_rows[:, 0, :])
+        nc.sync.dma_start(ent_list[:], offs)
+        nc.sync.dma_start(rel_list[:], offs2)
+        for even in (0, 2):
+            odd = even + 1
+            if even:
+                nc.sync.dma_start(k_pl[even][:], k_rows[:, even, :])
+            nc.sync.dma_start(c_pl[even][:], c_rows[:, even, :])
+            nc.sync.dma_start(w_pl[odd][:], w_rows[:, odd, :])
+            nc.sync.dma_start(k_pl[odd][:], k_rows[:, odd, :])
+            nc.sync.dma_start(c_pl[odd][:], c_rows[:, odd, :])
+            nc.sync.dma_start(w_pl[even][:], w_rows[:, even, :])
+        nc.sync.dma_start(q_raw[:], qT[0].rearrange("(p t) n -> p t n", t=PACK))
+        for m in range(q_tiles):
+            nc.scalar.dma_start(margin[m][:], mg[0, m * P:(m + 1) * P, :])
+            nc.gpsimd.tensor_scalar(neg_margin[m][:], margin[m][:], -1.0, 0.0, ALU.mult, ALU.add)
+        nc.gpsimd.memset(floor[:], LOG_FLOOR)
+
+        u = sb.tile([P, SLOTS, PACK], BF16, name="u", align_bytes=64)
+        u_low = sb.tile([P, SLOTS, 2], BF16, name="u_low")
+        kg = [sb.tile([P, SLOTS], F32, name="kg%d" % t) for t in range(PACK)]
+        neg_kg = [sb.tile([P, SLOTS], F32, name="neg_kg%d" % h) for h in range(2)]
+        cos_part = [sb.tile([P, 2, SLOTS], F32, name="cos_part%d" % h) for h in range(2)]
+        sin_part = [sb.tile([P, 2, SLOTS], F32, name="sin_part%d" % h) for h in range(2)]
+
+        def products(h):
+            even, odd = 2 * h, 2 * h + 1
+            nc.vector.tensor_copy(kg[even][:], k_pl[even][:].indirect(ent_list[:]))
+            nc.vector.tensor_tensor(cos_part[h][:, 0, :], c_pl[even][:].indirect(rel_list[:]), kg[even][:], ALU.mult)
+            nc.vector.tensor_tensor(sin_part[h][:, 1, :], w_pl[odd][:].indirect(rel_list[:]), kg[even][:], ALU.mult)
+            nc.vector.tensor_copy(kg[odd][:], k_pl[odd][:].indirect(ent_list[:]))
+            nc.scalar.activation(neg_kg[h][:], kg[odd][:], ACT.Copy, scale=-1.0)
+            nc.vector.tensor_tensor(cos_part[h][:, 1, :], c_pl[odd][:].indirect(rel_list[:]), kg[odd][:], ALU.mult)
+
+        def last_product(h, lo, hi):
+            nc.vector.tensor_tensor(sin_part[h][:, 0, lo:hi], w_pl[2 * h][:].indirect(rel_list[:, lo // 16:hi // 16]),
+                                    neg_kg[h][:, lo:hi], ALU.mult)
+
+        def pair_sum(h, lo, hi, dst):
+            nc.vector.tensor_tensor(dst, cos_part[h][:, :, lo:hi].rearrange("p t n -> p n t"),
+                                    sin_part[h][:, :, lo:hi].rearrange("p t n -> p n t"), ALU.add)
+
+        products(0)
+        last_product(0, 0, SLOTS)
+        pair_sum(0, 0, SLOTS, u_low[:])
+        nc.scalar.copy(u[:, :, 0:2], u_low[:])
+        products(1)
+
+        q_bf = sb.tile([P, NQ, PACK], BF16, name="q_bf", align_bytes=64)
+        q_codes = sb.tile([P, NQ], U32, name="q_codes", align_bytes=64)
+        q_scales = sb.tile([P, NQ], U8, name="q_scales", align_bytes=64)
+        u_codes = sb.tile([P, SLOTS], U32, name="u_codes", align_bytes=64)
+        u_scales = sb.tile([P, SLOTS], U8, name="u_scales", align_bytes=64)
+        for m in range(q_tiles):
+            cols = slice(m * P, (m + 1) * P)
+            nc.scalar.activation(q_bf[:, cols, :].rearrange("p (c i) t -> p c t i", i=4),
+                                 q_raw[:, :, cols].rearrange("p t (c i) -> p c t i", i=4), ACT.Copy)
+
+        def quant_q(m):
+            cols = slice(m * P, (m + 1) * P)
+            nc.vector.quantize_mx(q_codes[:, cols].bitcast(FP8X4), q_scales[:, cols],
+                                  q_bf[:, cols, :].rearrange("p n t -> p (n t)"))
+
+        def quant_u(j):
+            lo, hi = CHUNKS[j]
+            nc.vector.quantize_mx(u_codes[:, lo:hi].bitcast(FP8X4), u_scales[:, lo:hi],
+                                  u[:, lo:hi, :].rearrange("p n t -> p (n t)"))
+
+        sig = sb.tile([P, q_tiles, SLOTS], F32, name="sig")
+        acc = {}
+
+        def score(j):
+            lo, hi = CHUNKS[j]
+            for m in range(q_tiles):
+                cols = slice(m * P, (m + 1) * P)
+                acc[j, m] = ps.tile([P, hi - lo], F32, name="acc%d_%d" % (j, m))
+                nc.tensor.matmul_mx(acc[j, m][:], lhsT=q_codes[:, cols].bitcast(FP8X4), lhsT_scale=q_scales[:, cols],
+                                    rhs=u_codes[:, lo:hi].bitcast(FP8X4), rhs_scale=u_scales[:, lo:hi],
+                                    start=True, stop=True)
+                nc.scalar.activation(sig[:, m, lo:hi], acc[j, m][:], ACT.Sigmoid, bias=neg_margin[m][:])
+
+        n = len(CHUNKS)
+        for step in range(n + 2):
+            if step < n:
+                last_product(1, *CHUNKS[step])
+            if 1 <= step <= n:
+                lo, hi = CHUNKS[step - 1]
+                pair_sum(1, lo, hi, u[:, lo:hi, 2:4])
+            if step == 2:
+                quant_q(0)
+                quant_q(1)
+            if step >= 2:
+                quant_u(step - 2)
+                score(step - 2)
+
+        v = sb.tile([P, q_tiles, SLOTS], F32, name="v")
+        lg = sb.tile([P, q_tiles, SLOTS], F32, name="lg")
+        res = sb.tile([P, q_tiles, SLOTS], F32, name="res")
+        for j in range(n):
+            lo, hi = CHUNKS[j]
+            for m in range(q_tiles):
+                nc.vector.tensor_scalar(v[:, m, lo:hi], acc[j, m][:], -1.0, margin[m][:], ALU.mult, ALU.add)
+        for m in (1, 0):
+            nc.scalar.activation(lg[:, m, :], sig[:, m, :], ACT.Ln, bias=floor[:])
+            nc.vector.scalar_tensor_tensor(res[:, m, :], lg[:, m, :], -1.0, v[:, m, :], ALU.mult, ALU.max)
+            nc.sync.dma_start(out[0, m * P:(m + 1) * P, :], res[:, m, :])

@@ -15,7 +15,8 @@ P = 128
 PACK = 4
 D, NQ, SLOTS = 512, 256, 512
 FLOPS = 2 * D * NQ * SLOTS
-CHUNKS = [(0, 128), (128, 256), (256, 384), (384, 512)]
+CHUNKS = [(256, 384), (384, 512), (0, 128), (128, 256)]
+PIECES = [(1, 0, 192), (1, 192, 512), (0, 192, 512), (0, 0, 192)]
 LOG_FLOOR = 2.0 ** -60
 
 
@@ -50,8 +51,8 @@ def tile_attend_pre_rotate_f_topk_kernel(tc, qT, kT, cT, wT, mg, offs, offs2, ou
             if even:
                 nc.sync.dma_start(k_pl[even][:], k_rows[:, even, :])
             nc.sync.dma_start(c_pl[even][:], c_rows[:, even, :])
-            nc.sync.dma_start(w_pl[odd][:], w_rows[:, odd, :])
             nc.sync.dma_start(k_pl[odd][:], k_rows[:, odd, :])
+            nc.sync.dma_start(w_pl[odd][:], w_rows[:, odd, :])
             nc.sync.dma_start(c_pl[odd][:], c_rows[:, odd, :])
             nc.sync.dma_start(w_pl[even][:], w_rows[:, even, :])
         nc.sync.dma_start(q_raw[:], qT[0].rearrange("(p t) n -> p t n", t=PACK))
@@ -59,20 +60,22 @@ def tile_attend_pre_rotate_f_topk_kernel(tc, qT, kT, cT, wT, mg, offs, offs2, ou
             nc.scalar.dma_start(margin[m][:], mg[0, m * P:(m + 1) * P, :])
             nc.gpsimd.tensor_scalar(neg_margin[m][:], margin[m][:], -1.0, 0.0, ALU.mult, ALU.add)
         nc.gpsimd.memset(floor[:], LOG_FLOOR)
+        warm = sb.tile([P, 1], F32, name="warm")
+        nc.scalar.activation(warm[:], floor[:], ACT.Sigmoid)
 
-        u = sb.tile([P, SLOTS, PACK], BF16, name="u", align_bytes=64)
+        u = sb.tile([P, SLOTS, PACK], BF16, name="u", tag="u", align_bytes=64)
         u_low = sb.tile([P, SLOTS, 2], BF16, name="u_low")
         kg = [sb.tile([P, SLOTS], F32, name="kg%d" % t) for t in range(PACK)]
         neg_kg = [sb.tile([P, SLOTS], F32, name="neg_kg%d" % h) for h in range(2)]
         cos_part = [sb.tile([P, 2, SLOTS], F32, name="cos_part%d" % h) for h in range(2)]
-        sin_part = [sb.tile([P, 2, SLOTS], F32, name="sin_part%d" % h) for h in range(2)]
+        sin_part = [sb.tile([P, 2, SLOTS], F32, name="sin_part%d" % h, align_bytes=64) for h in range(2)]
 
         def products(h):
             even, odd = 2 * h, 2 * h + 1
             nc.vector.tensor_copy(kg[even][:], k_pl[even][:].indirect(ent_list[:]))
             nc.vector.tensor_tensor(cos_part[h][:, 0, :], c_pl[even][:].indirect(rel_list[:]), kg[even][:], ALU.mult)
-            nc.vector.tensor_tensor(sin_part[h][:, 1, :], w_pl[odd][:].indirect(rel_list[:]), kg[even][:], ALU.mult)
             nc.vector.tensor_copy(kg[odd][:], k_pl[odd][:].indirect(ent_list[:]))
+            nc.vector.tensor_tensor(sin_part[h][:, 1, :], w_pl[odd][:].indirect(rel_list[:]), kg[even][:], ALU.mult)
             nc.scalar.activation(neg_kg[h][:], kg[odd][:], ACT.Copy, scale=-1.0)
             nc.vector.tensor_tensor(cos_part[h][:, 1, :], c_pl[odd][:].indirect(rel_list[:]), kg[odd][:], ALU.mult)
 
@@ -90,20 +93,20 @@ def tile_attend_pre_rotate_f_topk_kernel(tc, qT, kT, cT, wT, mg, offs, offs2, ou
         nc.scalar.copy(u[:, :, 0:2], u_low[:])
         products(1)
 
-        q_bf = sb.tile([P, NQ, PACK], BF16, name="q_bf", align_bytes=64)
+        q_bf1 = sb.tile([P, P * PACK], BF16, name="q_bf1", align_bytes=64)
+        q_bf = [sin_part[1][:, 0, 0:256].bitcast(BF16), q_bf1[:]]
         q_codes = sb.tile([P, NQ], U32, name="q_codes", align_bytes=64)
         q_scales = sb.tile([P, NQ], U8, name="q_scales", align_bytes=64)
         u_codes = sb.tile([P, SLOTS], U32, name="u_codes", align_bytes=64)
         u_scales = sb.tile([P, SLOTS], U8, name="u_scales", align_bytes=64)
         for m in range(q_tiles):
             cols = slice(m * P, (m + 1) * P)
-            nc.scalar.activation(q_bf[:, cols, :].rearrange("p (c i) t -> p c t i", i=4),
+            nc.scalar.activation(q_bf[m].rearrange("p (c i t) -> p c t i", i=4, t=PACK),
                                  q_raw[:, :, cols].rearrange("p t (c i) -> p c t i", i=4), ACT.Copy)
 
         def quant_q(m):
             cols = slice(m * P, (m + 1) * P)
-            nc.vector.quantize_mx(q_codes[:, cols].bitcast(FP8X4), q_scales[:, cols],
-                                  q_bf[:, cols, :].rearrange("p n t -> p (n t)"))
+            nc.vector.quantize_mx(q_codes[:, cols].bitcast(FP8X4), q_scales[:, cols], q_bf[m])
 
         def quant_u(j):
             lo, hi = CHUNKS[j]
@@ -123,28 +126,29 @@ def tile_attend_pre_rotate_f_topk_kernel(tc, qT, kT, cT, wT, mg, offs, offs2, ou
                                     start=True, stop=True)
                 nc.scalar.activation(sig[:, m, lo:hi], acc[j, m][:], ACT.Sigmoid, bias=neg_margin[m][:])
 
-        n = len(CHUNKS)
-        for step in range(n + 2):
-            if step < n:
-                last_product(1, *CHUNKS[step])
-            if 1 <= step <= n:
-                lo, hi = CHUNKS[step - 1]
-                pair_sum(1, lo, hi, u[:, lo:hi, 2:4])
-            if step == 2:
-                quant_q(0)
+        for first in (0, 2):
+            for j in (first, first + 1):
+                last_product(1, *CHUNKS[j])
+            if first:
                 quant_q(1)
-            if step >= 2:
-                quant_u(step - 2)
-                score(step - 2)
+            for j in (first, first + 1):
+                lo, hi = CHUNKS[j]
+                pair_sum(1, lo, hi, u[:, lo:hi, 2:4])
+            for j in (first, first + 1):
+                quant_u(j)
+            if not first:
+                quant_q(0)
+        for j in range(len(CHUNKS)):
+            score(j)
 
-        v = sb.tile([P, q_tiles, SLOTS], F32, name="v")
+        v = sb.tile([P, q_tiles, SLOTS], F32, name="v", tag="u", align_bytes=64)
         lg = sb.tile([P, q_tiles, SLOTS], F32, name="lg")
         res = sb.tile([P, q_tiles, SLOTS], F32, name="res")
-        for j in range(n):
-            lo, hi = CHUNKS[j]
-            for m in range(q_tiles):
-                nc.vector.tensor_scalar(v[:, m, lo:hi], acc[j, m][:], -1.0, margin[m][:], ALU.mult, ALU.add)
         for m in (1, 0):
-            nc.scalar.activation(lg[:, m, :], sig[:, m, :], ACT.Ln, bias=floor[:])
-            nc.vector.scalar_tensor_tensor(res[:, m, :], lg[:, m, :], -1.0, v[:, m, :], ALU.mult, ALU.max)
-            nc.sync.dma_start(out[0, m * P:(m + 1) * P, :], res[:, m, :])
+            for j in range(len(CHUNKS)):
+                lo, hi = CHUNKS[j]
+                nc.vector.tensor_scalar(v[:, m, lo:hi], acc[j, m][:], -1.0, margin[m][:], ALU.mult, ALU.add)
+        for m, lo, hi in PIECES:
+            nc.scalar.activation(lg[:, m, lo:hi], sig[:, m, lo:hi], ACT.Ln, bias=floor[:])
+            nc.vector.scalar_tensor_tensor(res[:, m, lo:hi], lg[:, m, lo:hi], -1.0, v[:, m, lo:hi], ALU.mult, ALU.max)
+            nc.sync.dma_start(out[0, m * P:(m + 1) * P, lo:hi], res[:, m, lo:hi])

@@ -57,14 +57,13 @@ def tile_attend_pre_rotate_f_topk_kernel(tc, qT, kT, cT, wT, mg, offs, offs2, ou
             nc.sync.dma_start(w_pl[even][:], w_rows[:, even, :])
         nc.sync.dma_start(q_raw[:], qT[0].rearrange("(p t) n -> p t n", t=PACK))
         for m in range(q_tiles):
-            nc.scalar.dma_start(margin[m][:], mg[0, m * P:(m + 1) * P, :])
-            nc.gpsimd.tensor_scalar(neg_margin[m][:], margin[m][:], -1.0, 0.0, ALU.mult, ALU.add)
+            nc.sync.dma_start(margin[m][:], mg[0, m * P:(m + 1) * P, :])
         nc.gpsimd.memset(floor[:], LOG_FLOOR)
         warm = sb.tile([P, 1], F32, name="warm")
         nc.scalar.activation(warm[:], floor[:], ACT.Sigmoid)
 
         u = sb.tile([P, SLOTS, PACK], BF16, name="u", tag="u", align_bytes=64)
-        u_low = sb.tile([P, SLOTS, 2], BF16, name="u_low")
+        pairs = sb.tile([P, 2, SLOTS, 2], BF16, name="pairs")
         kg = [sb.tile([P, SLOTS], F32, name="kg%d" % t) for t in range(PACK)]
         neg_kg = [sb.tile([P, SLOTS], F32, name="neg_kg%d" % h) for h in range(2)]
         cos_part = [sb.tile([P, 2, SLOTS], F32, name="cos_part%d" % h) for h in range(2)]
@@ -83,14 +82,17 @@ def tile_attend_pre_rotate_f_topk_kernel(tc, qT, kT, cT, wT, mg, offs, offs2, ou
             nc.vector.tensor_tensor(sin_part[h][:, 0, lo:hi], w_pl[2 * h][:].indirect(rel_list[:, lo // 16:hi // 16]),
                                     neg_kg[h][:, lo:hi], ALU.mult)
 
-        def pair_sum(h, lo, hi, dst):
-            nc.vector.tensor_tensor(dst, cos_part[h][:, :, lo:hi].rearrange("p t n -> p n t"),
+        def merge(lo, hi):
+            nc.vector.tensor_copy(u[:, lo:hi, :].rearrange("p n (h e) -> p n h e", h=2),
+                                  pairs[:, :, lo:hi, :].rearrange("p h n e -> p n h e"))
+
+        def pair_sum(h, lo, hi):
+            nc.vector.tensor_tensor(pairs[:, h, lo:hi, :], cos_part[h][:, :, lo:hi].rearrange("p t n -> p n t"),
                                     sin_part[h][:, :, lo:hi].rearrange("p t n -> p n t"), ALU.add)
 
         products(0)
         last_product(0, 0, SLOTS)
-        pair_sum(0, 0, SLOTS, u_low[:])
-        nc.scalar.copy(u[:, :, 0:2], u_low[:])
+        pair_sum(0, 0, SLOTS)
         products(1)
 
         q_bf1 = sb.tile([P, P * PACK], BF16, name="q_bf1", align_bytes=64)
@@ -103,6 +105,8 @@ def tile_attend_pre_rotate_f_topk_kernel(tc, qT, kT, cT, wT, mg, offs, offs2, ou
             cols = slice(m * P, (m + 1) * P)
             nc.scalar.activation(q_bf[m].rearrange("p (c i t) -> p c t i", i=4, t=PACK),
                                  q_raw[:, :, cols].rearrange("p t (c i) -> p c t i", i=4), ACT.Copy)
+        for m in range(q_tiles):
+            nc.scalar.activation(neg_margin[m][:], margin[m][:], ACT.Copy, scale=-1.0)
 
         def quant_q(m):
             cols = slice(m * P, (m + 1) * P)
@@ -132,8 +136,9 @@ def tile_attend_pre_rotate_f_topk_kernel(tc, qT, kT, cT, wT, mg, offs, offs2, ou
             if first:
                 quant_q(1)
             for j in (first, first + 1):
-                lo, hi = CHUNKS[j]
-                pair_sum(1, lo, hi, u[:, lo:hi, 2:4])
+                pair_sum(1, *CHUNKS[j])
+            for j in (first, first + 1):
+                merge(*CHUNKS[j])
             for j in (first, first + 1):
                 quant_u(j)
             if not first:

@@ -16,7 +16,8 @@ PACK = 4
 D, NQ, SLOTS = 512, 256, 512
 FLOPS = 2 * D * NQ * SLOTS
 CHUNKS = [(256, 384), (384, 512), (0, 128), (128, 256)]
-PIECES = [(1, 0, 192), (1, 192, 512), (0, 192, 512), (0, 0, 192)]
+GROUPS = [(256, 512), (0, 128), (128, 256)]
+PIECES = [(1, 0, 128), (1, 128, 320), (1, 320, 512), (0, 0, 192), (0, 192, 384), (0, 384, 512)]
 LOG_FLOOR = 2.0 ** -60
 
 
@@ -63,11 +64,11 @@ def tile_attend_pre_rotate_f_topk_kernel(tc, qT, kT, cT, wT, mg, offs, offs2, ou
         nc.scalar.activation(warm[:], floor[:], ACT.Sigmoid)
 
         u = sb.tile([P, SLOTS, PACK], BF16, name="u", tag="u", align_bytes=64)
-        pairs = sb.tile([P, 2, SLOTS, 2], BF16, name="pairs")
+        pairs = sb.tile([P, 2, SLOTS, 2], BF16, name="pairs", align_bytes=64)
         kg = [sb.tile([P, SLOTS], F32, name="kg%d" % t) for t in range(PACK)]
         neg_kg = [sb.tile([P, SLOTS], F32, name="neg_kg%d" % h) for h in range(2)]
         cos_part = [sb.tile([P, 2, SLOTS], F32, name="cos_part%d" % h) for h in range(2)]
-        sin_part = [sb.tile([P, 2, SLOTS], F32, name="sin_part%d" % h, align_bytes=64) for h in range(2)]
+        sin_part = [sb.tile([P, 2, SLOTS], F32, name="sin_part%d" % h) for h in range(2)]
 
         def products(h):
             even, odd = 2 * h, 2 * h + 1
@@ -96,10 +97,10 @@ def tile_attend_pre_rotate_f_topk_kernel(tc, qT, kT, cT, wT, mg, offs, offs2, ou
         products(1)
 
         q_bf1 = sb.tile([P, P * PACK], BF16, name="q_bf1", align_bytes=64)
-        q_bf = [sin_part[1][:, 0, 0:256].bitcast(BF16), q_bf1[:]]
+        q_bf = [pairs[:, 1, 0:256, :].rearrange("p n e -> p (n e)"), q_bf1[:]]
         q_codes = sb.tile([P, NQ], U32, name="q_codes", align_bytes=64)
         q_scales = sb.tile([P, NQ], U8, name="q_scales", align_bytes=64)
-        u_codes = sb.tile([P, SLOTS], U32, name="u_codes", align_bytes=64)
+        u_codes = sb.tile([P, SLOTS], U32, name="u_codes", tag="codes", align_bytes=64)
         u_scales = sb.tile([P, SLOTS], U8, name="u_scales", align_bytes=64)
         for m in range(q_tiles):
             cols = slice(m * P, (m + 1) * P)
@@ -113,7 +114,7 @@ def tile_attend_pre_rotate_f_topk_kernel(tc, qT, kT, cT, wT, mg, offs, offs2, ou
             nc.vector.quantize_mx(q_codes[:, cols].bitcast(FP8X4), q_scales[:, cols], q_bf[m])
 
         def quant_u(j):
-            lo, hi = CHUNKS[j]
+            lo, hi = GROUPS[j]
             nc.vector.quantize_mx(u_codes[:, lo:hi].bitcast(FP8X4), u_scales[:, lo:hi],
                                   u[:, lo:hi, :].rearrange("p n t -> p (n t)"))
 
@@ -121,7 +122,7 @@ def tile_attend_pre_rotate_f_topk_kernel(tc, qT, kT, cT, wT, mg, offs, offs2, ou
         acc = {}
 
         def score(j):
-            lo, hi = CHUNKS[j]
+            lo, hi = GROUPS[j]
             for m in range(q_tiles):
                 cols = slice(m * P, (m + 1) * P)
                 acc[j, m] = ps.tile([P, hi - lo], F32, name="acc%d_%d" % (j, m))
@@ -130,28 +131,31 @@ def tile_attend_pre_rotate_f_topk_kernel(tc, qT, kT, cT, wT, mg, offs, offs2, ou
                                     start=True, stop=True)
                 nc.scalar.activation(sig[:, m, lo:hi], acc[j, m][:], ACT.Sigmoid, bias=neg_margin[m][:])
 
-        for first in (0, 2):
-            for j in (first, first + 1):
-                last_product(1, *CHUNKS[j])
-            if first:
-                quant_q(1)
-            for j in (first, first + 1):
-                pair_sum(1, *CHUNKS[j])
-            for j in (first, first + 1):
-                merge(*CHUNKS[j])
-            for j in (first, first + 1):
-                quant_u(j)
-            if not first:
-                quant_q(0)
-        for j in range(len(CHUNKS)):
+        for j in (0, 1):
+            last_product(1, *CHUNKS[j])
+        for j in (0, 1):
+            pair_sum(1, *CHUNKS[j])
+        last_product(1, *CHUNKS[2])
+        merge(*GROUPS[0])
+        last_product(1, *CHUNKS[3])
+        quant_u(0)
+        quant_q(0)
+        for j in (2, 3):
+            pair_sum(1, *CHUNKS[j])
+        quant_q(1)
+        for j in (2, 3):
+            merge(*CHUNKS[j])
+        quant_u(1)
+        quant_u(2)
+        for j in range(len(GROUPS)):
             score(j)
 
         v = sb.tile([P, q_tiles, SLOTS], F32, name="v", tag="u", align_bytes=64)
-        lg = sb.tile([P, q_tiles, SLOTS], F32, name="lg")
+        lg = sb.tile([P, q_tiles, SLOTS], F32, name="lg", tag="codes", align_bytes=64)
         res = sb.tile([P, q_tiles, SLOTS], F32, name="res")
         for m in (1, 0):
-            for j in range(len(CHUNKS)):
-                lo, hi = CHUNKS[j]
+            for j in range(len(GROUPS)):
+                lo, hi = GROUPS[j]
                 nc.vector.tensor_scalar(v[:, m, lo:hi], acc[j, m][:], -1.0, margin[m][:], ALU.mult, ALU.add)
         for m, lo, hi in PIECES:
             nc.scalar.activation(lg[:, m, lo:hi], sig[:, m, lo:hi], ACT.Ln, bias=floor[:])

@@ -84,17 +84,19 @@ def tile_attend_pre_rotate_f_topk_kernel(tc, qT, kT, cT, wT, mg, offs, offs2, ou
                                     neg_kg[h][:, lo:hi], ALU.mult)
 
         def merge(lo, hi):
-            nc.vector.tensor_copy(u[:, lo:hi, :].rearrange("p n (h e) -> p n h e", h=2),
-                                  pairs[:, :, lo:hi, :].rearrange("p h n e -> p n h e"))
+            nc.vector.tensor_copy(u[:, lo:hi, :].rearrange("p (c i) (h e) -> p c h i e", i=4, h=2),
+                                  pairs[:, :, lo:hi, :].rearrange("p h (c i) e -> p c h i e", i=4))
 
         def pair_sum(h, lo, hi):
-            nc.vector.tensor_tensor(pairs[:, h, lo:hi, :], cos_part[h][:, :, lo:hi].rearrange("p t n -> p n t"),
-                                    sin_part[h][:, :, lo:hi].rearrange("p t n -> p n t"), ALU.add)
+            nc.vector.tensor_tensor(pairs[:, h, lo:hi, :].rearrange("p (c i) e -> p c e i", i=4),
+                                    cos_part[h][:, :, lo:hi].rearrange("p e (c i) -> p c e i", i=4),
+                                    sin_part[h][:, :, lo:hi].rearrange("p e (c i) -> p c e i", i=4), ALU.add)
 
         products(0)
         last_product(0, 0, SLOTS)
-        pair_sum(0, 0, SLOTS)
         products(1)
+        pair_sum(0, 0, SLOTS // 2)
+        pair_sum(0, SLOTS // 2, SLOTS)
 
         q_bf1 = sb.tile([P, P * PACK], BF16, name="q_bf1", align_bytes=64)
         q_bf = [pairs[:, 1, 0:256, :].rearrange("p n e -> p (n e)"), q_bf1[:]]

@@ -15,8 +15,7 @@ P = 128
 PACK = 4
 D, NQ, SLOTS = 512, 256, 512
 FLOPS = 2 * D * NQ * SLOTS
-CHUNKS = [(256, 384), (384, 512), (0, 128), (128, 256)]
-GROUPS = [(256, 512), (0, 128), (128, 256)]
+GROUP = 128
 PIECES = [(1, 0, 128), (1, 128, 320), (1, 320, 512), (0, 0, 192), (0, 192, 384), (0, 384, 512)]
 LOG_FLOOR = 2.0 ** -60
 
@@ -26,6 +25,7 @@ def tile_attend_pre_rotate_f_topk_kernel(tc, qT, kT, cT, wT, mg, offs, offs2, ou
     n_ent = kT.shape[1]
     n_rel = cT.shape[1]
     q_tiles = NQ // P
+    groups = SLOTS // GROUP
 
     with ExitStack() as ctx:
         sb = ctx.enter_context(tc.tile_pool(name="sb", bufs=1))
@@ -34,8 +34,8 @@ def tile_attend_pre_rotate_f_topk_kernel(tc, qT, kT, cT, wT, mg, offs, offs2, ou
         ent_list = sb.tile([P, SLOTS // 16], U16, name="ent_list")
         rel_list = sb.tile([P, SLOTS // 16], U16, name="rel_list")
         k_pl = [sb.tile([P, n_ent], F32, name="k%d" % t) for t in range(PACK)]
-        c_pl = [sb.tile([P, n_rel], F32, name="c%d" % t) for t in range(PACK)]
-        w_pl = [sb.tile([P, n_rel], F32, name="w%d" % t) for t in range(PACK)]
+        c_pl = [sb.tile([P, n_rel], F32, name="c%d" % h) for h in range(2)]
+        w_pl = [sb.tile([P, n_rel], F32, name="w%d" % h) for h in range(2)]
         k_rows = kT.rearrange("(p t) n -> p t n", t=PACK)
         c_rows = cT.rearrange("(p t) n -> p t n", t=PACK)
         w_rows = wT.rearrange("(p t) n -> p t n", t=PACK)
@@ -44,18 +44,14 @@ def tile_attend_pre_rotate_f_topk_kernel(tc, qT, kT, cT, wT, mg, offs, offs2, ou
         neg_margin = [sb.tile([P, 1], F32, name="neg_margin%d" % m) for m in range(q_tiles)]
         floor = sb.tile([P, 1], F32, name="floor")
 
-        nc.sync.dma_start(k_pl[0][:], k_rows[:, 0, :])
-        nc.sync.dma_start(ent_list[:], offs)
+        nc.sync.dma_start(c_pl[0][:], c_rows[:, 0, :])
         nc.sync.dma_start(rel_list[:], offs2)
-        for even in (0, 2):
-            odd = even + 1
-            if even:
-                nc.sync.dma_start(k_pl[even][:], k_rows[:, even, :])
-            nc.sync.dma_start(c_pl[even][:], c_rows[:, even, :])
-            nc.sync.dma_start(k_pl[odd][:], k_rows[:, odd, :])
-            nc.sync.dma_start(w_pl[odd][:], w_rows[:, odd, :])
-            nc.sync.dma_start(c_pl[odd][:], c_rows[:, odd, :])
-            nc.sync.dma_start(w_pl[even][:], w_rows[:, even, :])
+        nc.sync.dma_start(w_pl[0][:], w_rows[:, 0, :])
+        nc.sync.dma_start(c_pl[1][:], c_rows[:, 2, :])
+        nc.sync.dma_start(w_pl[1][:], w_rows[:, 2, :])
+        nc.sync.dma_start(ent_list[:], offs)
+        for t in range(PACK):
+            nc.sync.dma_start(k_pl[t][:], k_rows[:, t, :])
         nc.sync.dma_start(q_raw[:], qT[0].rearrange("(p t) n -> p t n", t=PACK))
         for m in range(q_tiles):
             nc.sync.dma_start(margin[m][:], mg[0, m * P:(m + 1) * P, :])
@@ -64,42 +60,40 @@ def tile_attend_pre_rotate_f_topk_kernel(tc, qT, kT, cT, wT, mg, offs, offs2, ou
         nc.scalar.activation(warm[:], floor[:], ACT.Sigmoid)
 
         u = sb.tile([P, SLOTS, PACK], BF16, name="u", tag="u", align_bytes=64)
-        pairs = sb.tile([P, 2, SLOTS, 2], BF16, name="pairs", align_bytes=64)
-        kg = [sb.tile([P, SLOTS], F32, name="kg%d" % t) for t in range(PACK)]
-        neg_kg = [sb.tile([P, SLOTS], F32, name="neg_kg%d" % h) for h in range(2)]
-        cos_part = [sb.tile([P, 2, SLOTS], F32, name="cos_part%d" % h) for h in range(2)]
-        sin_part = [sb.tile([P, 2, SLOTS], F32, name="sin_part%d" % h) for h in range(2)]
+        cg = [sb.tile([P, SLOTS], F32, name="cg%d" % h) for h in range(2)]
+        wg = [sb.tile([P, SLOTS], F32, name="wg%d" % h) for h in range(2)]
+        neg_wg = [sb.tile([P, SLOTS], F32, name="neg_wg%d" % h) for h in range(2)]
+        from_even = sb.tile([P, PACK, SLOTS], F32, name="from_even")
+        from_odd = sb.tile([P, PACK, SLOTS], F32, name="from_odd")
 
-        def products(h):
+        for h in range(2):
+            nc.vector.tensor_copy(cg[h][:], c_pl[h][:].indirect(rel_list[:]))
+            nc.vector.tensor_copy(wg[h][:], w_pl[h][:].indirect(rel_list[:]))
+            nc.scalar.activation(neg_wg[h][:], wg[h][:], ACT.Copy, scale=-1.0)
+
+        def product(dst, t_out, t_in, factor, lo=0, hi=SLOTS):
+            nc.vector.tensor_tensor(dst[:, t_out, lo:hi], k_pl[t_in][:].indirect(ent_list[:, lo // 16:hi // 16]),
+                                    factor[:, lo:hi], ALU.mult)
+
+        for h in range(2):
             even, odd = 2 * h, 2 * h + 1
-            nc.vector.tensor_copy(kg[even][:], k_pl[even][:].indirect(ent_list[:]))
-            nc.vector.tensor_tensor(cos_part[h][:, 0, :], c_pl[even][:].indirect(rel_list[:]), kg[even][:], ALU.mult)
-            nc.vector.tensor_copy(kg[odd][:], k_pl[odd][:].indirect(ent_list[:]))
-            nc.vector.tensor_tensor(sin_part[h][:, 1, :], w_pl[odd][:].indirect(rel_list[:]), kg[even][:], ALU.mult)
-            nc.scalar.activation(neg_kg[h][:], kg[odd][:], ACT.Copy, scale=-1.0)
-            nc.vector.tensor_tensor(cos_part[h][:, 1, :], c_pl[odd][:].indirect(rel_list[:]), kg[odd][:], ALU.mult)
+            product(from_even, even, even, cg[h])
+            product(from_even, odd, even, wg[h])
+            product(from_odd, even, odd, neg_wg[h])
+            if h == 0:
+                product(from_odd, odd, odd, cg[h])
+            else:
+                product(from_odd, odd, odd, cg[h], 0, SLOTS // 2)
+                product(from_odd, odd, odd, cg[h], SLOTS // 2, SLOTS)
 
-        def last_product(h, lo, hi):
-            nc.vector.tensor_tensor(sin_part[h][:, 0, lo:hi], w_pl[2 * h][:].indirect(rel_list[:, lo // 16:hi // 16]),
-                                    neg_kg[h][:, lo:hi], ALU.mult)
+        def turn_sum(j):
+            cols = slice(j * GROUP, (j + 1) * GROUP)
+            nc.vector.tensor_tensor(u[:, cols, :].rearrange("p (c i) t -> p c t i", i=2),
+                                    from_even[:, :, cols].rearrange("p t (c i) -> p c t i", i=2),
+                                    from_odd[:, :, cols].rearrange("p t (c i) -> p c t i", i=2), ALU.add)
 
-        def merge(lo, hi):
-            nc.vector.tensor_copy(u[:, lo:hi, :].rearrange("p (c i) (h e) -> p c h i e", i=4, h=2),
-                                  pairs[:, :, lo:hi, :].rearrange("p h (c i) e -> p c h i e", i=4))
-
-        def pair_sum(h, lo, hi):
-            nc.vector.tensor_tensor(pairs[:, h, lo:hi, :].rearrange("p (c i) e -> p c e i", i=4),
-                                    cos_part[h][:, :, lo:hi].rearrange("p e (c i) -> p c e i", i=4),
-                                    sin_part[h][:, :, lo:hi].rearrange("p e (c i) -> p c e i", i=4), ALU.add)
-
-        products(0)
-        last_product(0, 0, SLOTS)
-        products(1)
-        pair_sum(0, 0, SLOTS // 2)
-        pair_sum(0, SLOTS // 2, SLOTS)
-
-        q_bf1 = sb.tile([P, P * PACK], BF16, name="q_bf1", align_bytes=64)
-        q_bf = [pairs[:, 1, 0:256, :].rearrange("p n e -> p (n e)"), q_bf1[:]]
+        q_bf = [u[:, (groups - 2 + m) * GROUP:(groups - 1 + m) * GROUP, :].rearrange("p n t -> p (n t)")
+                for m in range(q_tiles)]
         q_codes = sb.tile([P, NQ], U32, name="q_codes", align_bytes=64)
         q_scales = sb.tile([P, NQ], U8, name="q_scales", align_bytes=64)
         u_codes = sb.tile([P, SLOTS], U32, name="u_codes", tag="codes", align_bytes=64)
@@ -116,49 +110,43 @@ def tile_attend_pre_rotate_f_topk_kernel(tc, qT, kT, cT, wT, mg, offs, offs2, ou
             nc.vector.quantize_mx(q_codes[:, cols].bitcast(FP8X4), q_scales[:, cols], q_bf[m])
 
         def quant_u(j):
-            lo, hi = GROUPS[j]
-            nc.vector.quantize_mx(u_codes[:, lo:hi].bitcast(FP8X4), u_scales[:, lo:hi],
-                                  u[:, lo:hi, :].rearrange("p n t -> p (n t)"))
+            cols = slice(j * GROUP, (j + 1) * GROUP)
+            nc.vector.quantize_mx(u_codes[:, cols].bitcast(FP8X4), u_scales[:, cols],
+                                  u[:, cols, :].rearrange("p n t -> p (n t)"))
 
         sig = sb.tile([P, q_tiles, SLOTS], F32, name="sig")
         acc = {}
 
         def score(j):
-            lo, hi = GROUPS[j]
+            slots = slice(j * GROUP, (j + 1) * GROUP)
             for m in range(q_tiles):
                 cols = slice(m * P, (m + 1) * P)
-                acc[j, m] = ps.tile([P, hi - lo], F32, name="acc%d_%d" % (j, m))
+                acc[j, m] = ps.tile([P, GROUP], F32, name="acc%d_%d" % (j, m))
                 nc.tensor.matmul_mx(acc[j, m][:], lhsT=q_codes[:, cols].bitcast(FP8X4), lhsT_scale=q_scales[:, cols],
-                                    rhs=u_codes[:, lo:hi].bitcast(FP8X4), rhs_scale=u_scales[:, lo:hi],
+                                    rhs=u_codes[:, slots].bitcast(FP8X4), rhs_scale=u_scales[:, slots],
                                     start=True, stop=True)
-                nc.scalar.activation(sig[:, m, lo:hi], acc[j, m][:], ACT.Sigmoid, bias=neg_margin[m][:])
+                nc.scalar.activation(sig[:, m, slots], acc[j, m][:], ACT.Sigmoid, bias=neg_margin[m][:])
 
-        for j in (0, 1):
-            last_product(1, *CHUNKS[j])
-        for j in (0, 1):
-            pair_sum(1, *CHUNKS[j])
-        last_product(1, *CHUNKS[2])
-        merge(*GROUPS[0])
-        last_product(1, *CHUNKS[3])
+        turn_sum(0)
+        turn_sum(1)
         quant_u(0)
         quant_q(0)
-        for j in (2, 3):
-            pair_sum(1, *CHUNKS[j])
         quant_q(1)
-        for j in (2, 3):
-            merge(*CHUNKS[j])
         quant_u(1)
+        turn_sum(2)
+        turn_sum(3)
         quant_u(2)
-        for j in range(len(GROUPS)):
+        quant_u(3)
+        for j in range(groups):
             score(j)
 
         v = sb.tile([P, q_tiles, SLOTS], F32, name="v", tag="u", align_bytes=64)
         lg = sb.tile([P, q_tiles, SLOTS], F32, name="lg", tag="codes", align_bytes=64)
         res = sb.tile([P, q_tiles, SLOTS], F32, name="res")
         for m in (1, 0):
-            for j in range(len(GROUPS)):
-                lo, hi = GROUPS[j]
-                nc.vector.tensor_scalar(v[:, m, lo:hi], acc[j, m][:], -1.0, margin[m][:], ALU.mult, ALU.add)
+            for j in range(groups):
+                slots = slice(j * GROUP, (j + 1) * GROUP)
+                nc.vector.tensor_scalar(v[:, m, slots], acc[j, m][:], -1.0, margin[m][:], ALU.mult, ALU.add)
         for m, lo, hi in PIECES:
             nc.scalar.activation(lg[:, m, lo:hi], sig[:, m, lo:hi], ACT.Ln, bias=floor[:])
             nc.vector.scalar_tensor_tensor(res[:, m, lo:hi], lg[:, m, lo:hi], -1.0, v[:, m, lo:hi], ALU.mult, ALU.max)

@@ -60,37 +60,33 @@ def tile_attend_pre_rotate_f_topk_kernel(tc, qT, kT, cT, wT, mg, offs, offs2, ou
         nc.scalar.activation(warm[:], floor[:], ACT.Sigmoid)
 
         u = sb.tile([P, SLOTS, PACK], BF16, name="u", tag="u", align_bytes=64)
-        cg = [sb.tile([P, SLOTS], F32, name="cg%d" % h) for h in range(2)]
-        wg = [sb.tile([P, SLOTS], F32, name="wg%d" % h) for h in range(2)]
-        neg_wg = [sb.tile([P, SLOTS], F32, name="neg_wg%d" % h) for h in range(2)]
-        from_even = sb.tile([P, PACK, SLOTS], F32, name="from_even")
-        from_odd = sb.tile([P, PACK, SLOTS], F32, name="from_odd")
+        half = SLOTS // 2
+        factors = [sb.tile([P, 3, SLOTS], F32, name="factors%d" % h) for h in range(2)]
+        kg = [[sb.tile([P, half], F32, name="kg%d_%d" % (t, s)) for s in range(2)] for t in range(PACK)]
+        from_even = [sb.tile([P, PACK, half], F32, name="from_even%d" % s) for s in range(2)]
+        from_odd = [sb.tile([P, PACK, half], F32, name="from_odd%d" % s) for s in range(2)]
 
         for h in range(2):
-            nc.vector.tensor_copy(cg[h][:], c_pl[h][:].indirect(rel_list[:]))
-            nc.vector.tensor_copy(wg[h][:], w_pl[h][:].indirect(rel_list[:]))
-            nc.scalar.activation(neg_wg[h][:], wg[h][:], ACT.Copy, scale=-1.0)
+            nc.vector.tensor_copy(factors[h][:, 1, :], c_pl[h][:].indirect(rel_list[:]))
+            nc.vector.tensor_copy(factors[h][:, 2, :], w_pl[h][:].indirect(rel_list[:]))
+            nc.scalar.activation(factors[h][:, 0, :], factors[h][:, 2, :], ACT.Copy, scale=-1.0)
 
-        def product(dst, t_out, t_in, factor, lo=0, hi=SLOTS):
-            nc.vector.tensor_tensor(dst[:, t_out, lo:hi], k_pl[t_in][:].indirect(ent_list[:, lo // 16:hi // 16]),
-                                    factor[:, lo:hi], ALU.mult)
-
-        for h in range(2):
-            even, odd = 2 * h, 2 * h + 1
-            product(from_even, even, even, cg[h])
-            product(from_even, odd, even, wg[h])
-            product(from_odd, even, odd, neg_wg[h])
-            if h == 0:
-                product(from_odd, odd, odd, cg[h])
-            else:
-                product(from_odd, odd, odd, cg[h], 0, SLOTS // 2)
-                product(from_odd, odd, odd, cg[h], SLOTS // 2, SLOTS)
+        for t in range(PACK):
+            h, odd = divmod(t, 2)
+            for s in range(2):
+                nc.vector.tensor_copy(kg[t][s][:], k_pl[t][:].indirect(ent_list[:, s * half // 16:(s + 1) * half // 16]))
+            for s in range(2):
+                dst = (from_odd if odd else from_even)[s]
+                nc.vector.tensor_tensor(dst[:, 2 * h:2 * h + 2, :],
+                                        factors[h][:, 1 - odd:3 - odd, s * half:(s + 1) * half],
+                                        kg[t][s][:].unsqueeze(1).to_broadcast([P, 2, half]), ALU.mult)
 
         def turn_sum(j):
             cols = slice(j * GROUP, (j + 1) * GROUP)
+            s, lo = divmod(j * GROUP, half)
             nc.vector.tensor_tensor(u[:, cols, :].rearrange("p (c i) t -> p c t i", i=2),
-                                    from_even[:, :, cols].rearrange("p t (c i) -> p c t i", i=2),
-                                    from_odd[:, :, cols].rearrange("p t (c i) -> p c t i", i=2), ALU.add)
+                                    from_even[s][:, :, lo:lo + GROUP].rearrange("p t (c i) -> p c t i", i=2),
+                                    from_odd[s][:, :, lo:lo + GROUP].rearrange("p t (c i) -> p c t i", i=2), ALU.add)
 
         q_bf = [u[:, (groups - 2 + m) * GROUP:(groups - 1 + m) * GROUP, :].rearrange("p n t -> p (n t)")
                 for m in range(q_tiles)]

@@ -1,6 +1,7 @@
 from contextlib import ExitStack
 
 import concourse.mybir as mybir
+from concourse.masks import make_identity
 
 F32 = mybir.dt.float32
 BF16 = mybir.dt.bfloat16
@@ -15,7 +16,7 @@ P = 128
 PACK = 4
 D, NQ, SLOTS = 512, 256, 512
 FLOPS = 2 * D * NQ * SLOTS
-GROUP = 128
+GROUPS = [(0, 256), (256, 384), (384, 512)]
 PIECES = [(1, 0, 128), (1, 128, 320), (1, 320, 512), (0, 0, 192), (0, 192, 384), (0, 384, 512)]
 LOG_FLOOR = 2.0 ** -60
 
@@ -25,7 +26,6 @@ def tile_attend_pre_rotate_f_topk_kernel(tc, qT, kT, cT, wT, mg, offs, offs2, ou
     n_ent = kT.shape[1]
     n_rel = cT.shape[1]
     q_tiles = NQ // P
-    groups = SLOTS // GROUP
 
     with ExitStack() as ctx:
         sb = ctx.enter_context(tc.tile_pool(name="sb", bufs=1))
@@ -39,7 +39,7 @@ def tile_attend_pre_rotate_f_topk_kernel(tc, qT, kT, cT, wT, mg, offs, offs2, ou
         k_rows = kT.rearrange("(p t) n -> p t n", t=PACK)
         c_rows = cT.rearrange("(p t) n -> p t n", t=PACK)
         w_rows = wT.rearrange("(p t) n -> p t n", t=PACK)
-        q_raw = sb.tile([P, PACK, NQ], F32, name="q_raw")
+        q_raw = [sb.tile([P, PACK, P], F32, name="q_raw%d" % m) for m in range(q_tiles)]
         margin = [sb.tile([P, 1], F32, name="margin%d" % m) for m in range(q_tiles)]
         neg_margin = [sb.tile([P, 1], F32, name="neg_margin%d" % m) for m in range(q_tiles)]
         floor = sb.tile([P, 1], F32, name="floor")
@@ -52,97 +52,128 @@ def tile_attend_pre_rotate_f_topk_kernel(tc, qT, kT, cT, wT, mg, offs, offs2, ou
         nc.sync.dma_start(ent_list[:], offs)
         for t in range(PACK):
             nc.sync.dma_start(k_pl[t][:], k_rows[:, t, :])
-        nc.sync.dma_start(q_raw[:], qT[0].rearrange("(p t) n -> p t n", t=PACK))
+        for m in range(q_tiles):
+            nc.sync.dma_start(q_raw[m][:], qT[0].rearrange("(p t) n -> p t n", t=PACK)[:, :, m * P:(m + 1) * P])
         for m in range(q_tiles):
             nc.sync.dma_start(margin[m][:], mg[0, m * P:(m + 1) * P, :])
         nc.gpsimd.memset(floor[:], LOG_FLOOR)
         warm = sb.tile([P, 1], F32, name="warm")
         nc.scalar.activation(warm[:], floor[:], ACT.Sigmoid)
 
-        u = sb.tile([P, SLOTS, PACK], BF16, name="u", tag="u", align_bytes=64)
+        ident = sb.tile([P, P], F32, name="ident")
+        make_identity(nc, ident[:])
+
+        u = sb.tile([P, SLOTS * PACK], BF16, name="u", tag="u", align_bytes=64)
+        u_pairs = u[:].rearrange("p (n h e) -> p n h e", h=2, e=2)
+        u_words = u[:].bitcast(F32).rearrange("p (n h) -> p n h", h=2)
         half = SLOTS // 2
+        blocks = half // P
         factors = [sb.tile([P, 3, SLOTS], F32, name="factors%d" % h) for h in range(2)]
         kg = [[sb.tile([P, half], F32, name="kg%d_%d" % (t, s)) for s in range(2)] for t in range(PACK)]
-        from_even = [sb.tile([P, PACK, half], F32, name="from_even%d" % s) for s in range(2)]
-        from_odd = [sb.tile([P, PACK, half], F32, name="from_odd%d" % s) for s in range(2)]
+        part = {}
 
         for h in range(2):
             nc.vector.tensor_copy(factors[h][:, 1, :], c_pl[h][:].indirect(rel_list[:]))
             nc.vector.tensor_copy(factors[h][:, 2, :], w_pl[h][:].indirect(rel_list[:]))
             nc.scalar.activation(factors[h][:, 0, :], factors[h][:, 2, :], ACT.Copy, scale=-1.0)
 
-        for t in range(PACK):
-            h, odd = divmod(t, 2)
+        def gather(t):
             for s in range(2):
                 nc.vector.tensor_copy(kg[t][s][:], k_pl[t][:].indirect(ent_list[:, s * half // 16:(s + 1) * half // 16]))
+
+        def product(t, lo, hi):
+            h, odd = divmod(t, 2)
+            s, first = divmod(lo, half)
+            if (t, s) not in part:
+                part[t, s] = sb.tile([P, 2, half], F32, name="part%d_%d" % (t, s), tag="part%d_%d" % (t, s),
+                                     align_bytes=64)
+            cols = slice(first, first + hi - lo)
+            nc.vector.tensor_tensor(part[t, s][:, :, cols], factors[h][:, 1 - odd:3 - odd, lo:hi],
+                                    kg[t][s][:, cols].unsqueeze(1).to_broadcast([P, 2, hi - lo]), ALU.mult)
+
+        turned = [ps.tile([P, blocks, 2, P], F32, name="turned%d" % s, tag="bank%d" % s) for s in range(2)]
+
+        def turn(t, s):
+            for b in range(blocks):
+                for e in range(2):
+                    nc.tensor.matmul(turned[s][:, b, e, :], part[t, s][:, e, b * P:(b + 1) * P], ident[:],
+                                     start=(t, b, e) == (0, 0, 0), stop=(t, b, e) == (1, blocks - 1, 1),
+                                     is_transpose=True)
+
+        def turn_back(s):
+            rounded = sb.tile([P, blocks * P * 2], BF16, name="rounded%d" % s)
+            nc.scalar.activation(rounded[:].rearrange("n (b p e) -> n b p e", b=blocks, e=2),
+                                 turned[s][:].rearrange("n b e p -> n b p e"), ACT.Copy)
+            back = ps.tile([P, half], F32, name="back%d" % s)
+            for b in range(blocks):
+                nc.tensor.transpose(back[:, b * P:(b + 1) * P], rounded[:].bitcast(F32)[:, b * P:(b + 1) * P], ident[:])
+            nc.scalar.copy(u_words[:, s * half:(s + 1) * half, 0], back[:])
+
+        for t in range(2):
+            gather(t)
             for s in range(2):
-                dst = (from_odd if odd else from_even)[s]
-                nc.vector.tensor_tensor(dst[:, 2 * h:2 * h + 2, :],
-                                        factors[h][:, 1 - odd:3 - odd, s * half:(s + 1) * half],
-                                        kg[t][s][:].unsqueeze(1).to_broadcast([P, 2, half]), ALU.mult)
+                product(t, s * half, (s + 1) * half)
+                turn(t, s)
+        for s in range(2):
+            turn_back(s)
+        gather(2)
+        product(2, 0, half)
+        product(2, half, SLOTS)
+        gather(3)
+        product(3, 0, half)
+        product(3, half, SLOTS)
 
-        def turn_sum(j):
-            cols = slice(j * GROUP, (j + 1) * GROUP)
-            s, lo = divmod(j * GROUP, half)
-            nc.vector.tensor_tensor(u[:, cols, :].rearrange("p (c i) t -> p c t i", i=2),
-                                    from_even[s][:, :, lo:lo + GROUP].rearrange("p t (c i) -> p c t i", i=2),
-                                    from_odd[s][:, :, lo:lo + GROUP].rearrange("p t (c i) -> p c t i", i=2), ALU.add)
+        def pair_sum(lo, hi):
+            s, first = divmod(lo, half)
+            cols = slice(first, first + hi - lo)
+            nc.vector.tensor_tensor(u_pairs[:, lo:hi, 1, :].rearrange("p (c i) e -> p c e i", i=2),
+                                    part[2, s][:, :, cols].rearrange("p e (c i) -> p c e i", i=2),
+                                    part[3, s][:, :, cols].rearrange("p e (c i) -> p c e i", i=2), ALU.add)
 
-        q_bf = [u[:, (groups - 2 + m) * GROUP:(groups - 1 + m) * GROUP, :].rearrange("p n t -> p (n t)")
-                for m in range(q_tiles)]
+        q_bf = sb.tile([P, NQ * PACK], BF16, name="q_bf", align_bytes=64)
         q_codes = sb.tile([P, NQ], U32, name="q_codes", align_bytes=64)
         q_scales = sb.tile([P, NQ], U8, name="q_scales", align_bytes=64)
         u_codes = sb.tile([P, SLOTS], U32, name="u_codes", tag="codes", align_bytes=64)
         u_scales = sb.tile([P, SLOTS], U8, name="u_scales", align_bytes=64)
         for m in range(q_tiles):
-            cols = slice(m * P, (m + 1) * P)
-            nc.scalar.activation(q_bf[m].rearrange("p (c i t) -> p c t i", i=4, t=PACK),
-                                 q_raw[:, :, cols].rearrange("p t (c i) -> p c t i", i=4), ACT.Copy)
+            nc.scalar.activation(q_bf[:, m * P * PACK:(m + 1) * P * PACK].rearrange("p (c i t) -> p c t i", i=4, t=PACK),
+                                 q_raw[m][:].rearrange("p t (c i) -> p c t i", i=4), ACT.Copy)
         for m in range(q_tiles):
             nc.scalar.activation(neg_margin[m][:], margin[m][:], ACT.Copy, scale=-1.0)
 
-        def quant_q(m):
-            cols = slice(m * P, (m + 1) * P)
-            nc.vector.quantize_mx(q_codes[:, cols].bitcast(FP8X4), q_scales[:, cols], q_bf[m])
-
-        def quant_u(j):
-            cols = slice(j * GROUP, (j + 1) * GROUP)
-            nc.vector.quantize_mx(u_codes[:, cols].bitcast(FP8X4), u_scales[:, cols],
-                                  u[:, cols, :].rearrange("p n t -> p (n t)"))
+        def quant_u(lo, hi):
+            nc.vector.quantize_mx(u_codes[:, lo:hi].bitcast(FP8X4), u_scales[:, lo:hi], u[:, lo * PACK:hi * PACK])
 
         sig = sb.tile([P, q_tiles, SLOTS], F32, name="sig")
         acc = {}
 
         def score(j):
-            slots = slice(j * GROUP, (j + 1) * GROUP)
+            lo, hi = GROUPS[j]
             for m in range(q_tiles):
                 cols = slice(m * P, (m + 1) * P)
-                acc[j, m] = ps.tile([P, GROUP], F32, name="acc%d_%d" % (j, m))
+                tag = "bank%d" % m if j == len(GROUPS) - 1 else "acc%d_%d" % (j, m)
+                acc[j, m] = ps.tile([P, hi - lo], F32, name="acc%d_%d" % (j, m), tag=tag)
                 nc.tensor.matmul_mx(acc[j, m][:], lhsT=q_codes[:, cols].bitcast(FP8X4), lhsT_scale=q_scales[:, cols],
-                                    rhs=u_codes[:, slots].bitcast(FP8X4), rhs_scale=u_scales[:, slots],
+                                    rhs=u_codes[:, lo:hi].bitcast(FP8X4), rhs_scale=u_scales[:, lo:hi],
                                     start=True, stop=True)
-                nc.scalar.activation(sig[:, m, slots], acc[j, m][:], ACT.Sigmoid, bias=neg_margin[m][:])
+                nc.scalar.activation(sig[:, m, lo:hi], acc[j, m][:], ACT.Sigmoid, bias=neg_margin[m][:])
 
-        turn_sum(0)
-        turn_sum(1)
-        quant_u(0)
-        quant_q(0)
-        quant_q(1)
-        quant_u(1)
-        turn_sum(2)
-        turn_sum(3)
-        quant_u(2)
-        quant_u(3)
-        for j in range(groups):
+        pair_sum(*GROUPS[0])
+        nc.vector.quantize_mx(q_codes[:].bitcast(FP8X4), q_scales[:], q_bf[:])
+        pair_sum(*GROUPS[1])
+        quant_u(*GROUPS[0])
+        pair_sum(*GROUPS[2])
+        quant_u(*GROUPS[1])
+        quant_u(*GROUPS[2])
+        for j in range(len(GROUPS)):
             score(j)
 
         v = sb.tile([P, q_tiles, SLOTS], F32, name="v", tag="u", align_bytes=64)
         lg = sb.tile([P, q_tiles, SLOTS], F32, name="lg", tag="codes", align_bytes=64)
         res = sb.tile([P, q_tiles, SLOTS], F32, name="res")
         for m in (1, 0):
-            for j in range(groups):
-                slots = slice(j * GROUP, (j + 1) * GROUP)
-                nc.vector.tensor_scalar(v[:, m, slots], acc[j, m][:], -1.0, margin[m][:], ALU.mult, ALU.add)
+            for j, (lo, hi) in enumerate(GROUPS):
+                nc.vector.tensor_scalar(v[:, m, lo:hi], acc[j, m][:], -1.0, margin[m][:], ALU.mult, ALU.add)
         for m, lo, hi in PIECES:
             nc.scalar.activation(lg[:, m, lo:hi], sig[:, m, lo:hi], ACT.Ln, bias=floor[:])
             nc.vector.scalar_tensor_tensor(res[:, m, lo:hi], lg[:, m, lo:hi], -1.0, v[:, m, lo:hi], ALU.mult, ALU.max)

@@ -69,7 +69,8 @@ def tile_attend_pre_rotate_f_topk_kernel(tc, qT, kT, cT, wT, mg, offs, offs2, ou
         half = SLOTS // 2
         blocks = half // P
         factors = [sb.tile([P, 3, SLOTS], F32, name="factors%d" % h) for h in range(2)]
-        kg = [[sb.tile([P, half], F32, name="kg%d_%d" % (t, s)) for s in range(2)] for t in range(PACK)]
+        kg = [[sb.tile([P, half], F32, name="kg%d_%d" % (t, s), tag="kg%d_%d" % (t, s), align_bytes=64)
+               for s in range(2)] for t in range(PACK)]
         part = {}
 
         for h in range(2):
@@ -81,14 +82,13 @@ def tile_attend_pre_rotate_f_topk_kernel(tc, qT, kT, cT, wT, mg, offs, offs2, ou
             for s in range(2):
                 nc.vector.tensor_copy(kg[t][s][:], k_pl[t][:].indirect(ent_list[:, s * half // 16:(s + 1) * half // 16]))
 
-        def product(t, lo, hi):
+        def product(t, lo, hi, engine=nc.vector, tag=None):
             h, odd = divmod(t, 2)
             s, first = divmod(lo, half)
-            if (t, s) not in part:
-                part[t, s] = sb.tile([P, 2, half], F32, name="part%d_%d" % (t, s), tag="part%d_%d" % (t, s),
-                                     align_bytes=64)
+            part[t, s] = sb.tile([P, 2, half], F32, name="part%d_%d" % (t, s), tag=tag or "part%d_%d" % (t, s),
+                                 align_bytes=64)
             cols = slice(first, first + hi - lo)
-            nc.vector.tensor_tensor(part[t, s][:, :, cols], factors[h][:, 1 - odd:3 - odd, lo:hi],
+            engine.tensor_tensor(part[t, s][:, :, cols], factors[h][:, 1 - odd:3 - odd, lo:hi],
                                     kg[t][s][:, cols].unsqueeze(1).to_broadcast([P, 2, hi - lo]), ALU.mult)
 
         turned = [ps.tile([P, blocks, 2, P], F32, name="turned%d" % s, tag="bank%d" % s) for s in range(2)]
@@ -111,14 +111,18 @@ def tile_attend_pre_rotate_f_topk_kernel(tc, qT, kT, cT, wT, mg, offs, offs2, ou
 
         for t in range(2):
             gather(t)
-            for s in range(2):
-                product(t, s * half, (s + 1) * half)
-                turn(t, s)
+            product(t, 0, half)
+            turn(t, 0)
+            if t == 0:
+                product(t, half, SLOTS, nc.gpsimd, "kg0_0")
+            else:
+                product(t, half, SLOTS)
+            turn(t, 1)
         for s in range(2):
             turn_back(s)
         gather(2)
         product(2, 0, half)
-        product(2, half, SLOTS)
+        product(2, half, SLOTS, nc.gpsimd, "kg2_0")
         gather(3)
         product(3, 0, half)
         product(3, half, SLOTS)

@@ -16,7 +16,7 @@ P = 128
 PACK = 4
 D, NQ, SLOTS = 512, 256, 512
 FLOPS = 2 * D * NQ * SLOTS
-GROUPS = [(0, 256), (256, 384), (384, 512)]
+GROUPS = [(0, 128), (128, 256), (256, 384), (384, 512)]
 PIECES = [(1, 0, 128), (1, 128, 320), (1, 320, 512), (0, 0, 192), (0, 192, 384), (0, 384, 512)]
 LOG_FLOOR = 2.0 ** -60
 
@@ -82,14 +82,33 @@ def tile_attend_pre_rotate_f_topk_kernel(tc, qT, kT, cT, wT, mg, offs, offs2, ou
             for s in range(2):
                 nc.vector.tensor_copy(kg[t][s][:], k_pl[t][:].indirect(ent_list[:, s * half // 16:(s + 1) * half // 16]))
 
-        def product(t, lo, hi, engine=nc.vector, tag=None):
+        def product(t, lo, hi, engine=nc.vector, tag=None, held=None):
             h, odd = divmod(t, 2)
             s, first = divmod(lo, half)
-            part[t, s] = sb.tile([P, 2, half], F32, name="part%d_%d" % (t, s), tag=tag or "part%d_%d" % (t, s),
-                                 align_bytes=64)
+            if (t, s) not in part:
+                part[t, s] = sb.tile([P, 2, half], F32, name="part%d_%d" % (t, s), tag=tag or "part%d_%d" % (t, s),
+                                     align_bytes=64)
             cols = slice(first, first + hi - lo)
-            engine.tensor_tensor(part[t, s][:, :, cols], factors[h][:, 1 - odd:3 - odd, lo:hi],
+            engine.tensor_tensor(part[t, s][:, :, cols],
+                                 factors[h][:, 1 - odd:3 - odd, lo:hi] if held is None else held[:],
                                     kg[t][s][:, cols].unsqueeze(1).to_broadcast([P, 2, hi - lo]), ALU.mult)
+
+        columns = [[(1, 2), (1, 3), (2, 2), (2, 3)], [(0, 2), (0, 3), (0, 0), (1, 0)]]
+        crossed = {}
+        for i, wanted in enumerate(columns):
+            across = ps.tile([P, len(wanted), P], F32, name="across%d" % i, tag="bank%d" % (2 + i))
+            landed = sb.tile([P, len(wanted), P], F32, name="landed%d" % i)
+            for x, (f, b) in enumerate(wanted):
+                nc.tensor.transpose(across[:, x, :], factors[1][:, f, b * P:(b + 1) * P], ident[:])
+                crossed[f, b] = landed[:, x, :]
+            nc.scalar.copy(landed[:], across[:])
+        held = {}
+        for i, (odd, lo, hi) in enumerate([(0, half, SLOTS), (1, half, SLOTS), (1, 0, P)]):
+            held[odd, lo] = ps.tile([P, 2, hi - lo], F32, name="held%d" % i, tag="bank%d" % (4 + i))
+            for e in range(2):
+                for b in range(lo // P, hi // P):
+                    nc.tensor.transpose(held[odd, lo][:, e, b * P - lo:(b + 1) * P - lo], crossed[1 - odd + e, b],
+                                        ident[:])
 
         turned = [ps.tile([P, blocks, 2, P], F32, name="turned%d" % s, tag="bank%d" % s) for s in range(2)]
 
@@ -104,7 +123,7 @@ def tile_attend_pre_rotate_f_topk_kernel(tc, qT, kT, cT, wT, mg, offs, offs2, ou
             rounded = sb.tile([P, blocks * P * 2], BF16, name="rounded%d" % s)
             nc.scalar.activation(rounded[:].rearrange("n (b p e) -> n b p e", b=blocks, e=2),
                                  turned[s][:].rearrange("n b e p -> n b p e"), ACT.Copy)
-            back = ps.tile([P, half], F32, name="back%d" % s)
+            back = ps.tile([P, half], F32, name="back%d" % s, tag="bank%d" % (2 + s))
             for b in range(blocks):
                 nc.tensor.transpose(back[:, b * P:(b + 1) * P], rounded[:].bitcast(F32)[:, b * P:(b + 1) * P], ident[:])
             nc.scalar.copy(u_words[:, s * half:(s + 1) * half, 0], back[:])
@@ -121,11 +140,12 @@ def tile_attend_pre_rotate_f_topk_kernel(tc, qT, kT, cT, wT, mg, offs, offs2, ou
         for s in range(2):
             turn_back(s)
         gather(2)
-        product(2, 0, half)
-        product(2, half, SLOTS, nc.gpsimd, "kg2_0")
+        product(2, 0, half, nc.gpsimd)
+        product(2, half, SLOTS, held=held[0, half])
         gather(3)
-        product(3, 0, half)
-        product(3, half, SLOTS)
+        product(3, P, half, nc.gpsimd)
+        product(3, 0, P, held=held[1, 0])
+        product(3, half, SLOTS, held=held[1, half])
 
         def pair_sum(lo, hi):
             s, first = divmod(lo, half)
@@ -155,7 +175,7 @@ def tile_attend_pre_rotate_f_topk_kernel(tc, qT, kT, cT, wT, mg, offs, offs2, ou
             lo, hi = GROUPS[j]
             for m in range(q_tiles):
                 cols = slice(m * P, (m + 1) * P)
-                tag = "bank%d" % m if j == len(GROUPS) - 1 else "acc%d_%d" % (j, m)
+                tag = "bank%d" % [[7, 4], [6, 5], [0, 1], [2, 3]][j][m]
                 acc[j, m] = ps.tile([P, hi - lo], F32, name="acc%d_%d" % (j, m), tag=tag)
                 nc.tensor.matmul_mx(acc[j, m][:], lhsT=q_codes[:, cols].bitcast(FP8X4), lhsT_scale=q_scales[:, cols],
                                     rhs=u_codes[:, lo:hi].bitcast(FP8X4), rhs_scale=u_scales[:, lo:hi],
@@ -163,12 +183,13 @@ def tile_attend_pre_rotate_f_topk_kernel(tc, qT, kT, cT, wT, mg, offs, offs2, ou
                 nc.scalar.activation(sig[:, m, lo:hi], acc[j, m][:], ACT.Sigmoid, bias=neg_margin[m][:])
 
         pair_sum(*GROUPS[0])
-        nc.vector.quantize_mx(q_codes[:].bitcast(FP8X4), q_scales[:], q_bf[:])
-        pair_sum(*GROUPS[1])
-        quant_u(*GROUPS[0])
-        pair_sum(*GROUPS[2])
-        quant_u(*GROUPS[1])
-        quant_u(*GROUPS[2])
+        for m in range(q_tiles):
+            nc.vector.quantize_mx(q_codes[:, m * P:(m + 1) * P].bitcast(FP8X4), q_scales[:, m * P:(m + 1) * P],
+                                  q_bf[:, m * P * PACK:(m + 1) * P * PACK])
+        for j in range(len(GROUPS)):
+            if j + 1 < len(GROUPS):
+                pair_sum(*GROUPS[j + 1])
+            quant_u(*GROUPS[j])
         for j in range(len(GROUPS)):
             score(j)
 

@@ -14,145 +14,167 @@ ACT = mybir.ActivationFunctionType
 
 P = 128
 PACK = 4
-D, NQ, SLOTS = 512, 256, 512
+PAIRS = PACK // 2
+D, NQ, SLOTS, ENTITIES, RELATIONS = 512, 256, 512, 2048, 1024
+HALF = SLOTS // 2
+BLOCKS = HALF // P
+PER_COLUMN = 16
 FLOPS = 2 * D * NQ * SLOTS
-GROUPS = [(0, 128), (128, 256), (256, 384), (384, 512)]
+BYTES = 4 * (D * ENTITIES + D * RELATIONS + D * NQ + NQ + NQ * SLOTS) + 2 * 2 * P * SLOTS // PER_COLUMN
+
+GROUPS = [(lo, lo + P) for lo in range(0, SLOTS, P)]
+NEG_SIN, COS, SIN = 0, 1, 2
+HELD = [(2, HALF, SLOTS), (3, HALF, SLOTS), (3, 0, P)]
+SUM_BANK, TRANSIT_BANK, HELD_BANK = 0, 2, 4
+SCORE_BANKS = [[7, 4], [6, 5], [0, 1], [2, 3]]
 PIECES = [(1, 0, 128), (1, 128, 320), (1, 320, 512), (0, 0, 192), (0, 192, 384), (0, 384, 512)]
-LOG_FLOOR = 2.0 ** -60
+TWICE_FLOOR = 2.0 ** -59
 
 
 def tile_attend_pre_rotate_f_topk_kernel(tc, qT, kT, cT, wT, mg, offs, offs2, out):
     nc = tc.nc
-    n_ent = kT.shape[1]
-    n_rel = cT.shape[1]
     q_tiles = NQ // P
 
     with ExitStack() as ctx:
         sb = ctx.enter_context(tc.tile_pool(name="sb", bufs=1))
         ps = ctx.enter_context(tc.psum_pool(name="ps", bufs=1))
 
-        ent_list = sb.tile([P, SLOTS // 16], U16, name="ent_list")
-        rel_list = sb.tile([P, SLOTS // 16], U16, name="rel_list")
-        k_pl = [sb.tile([P, n_ent], F32, name="k%d" % t) for t in range(PACK)]
-        c_pl = [sb.tile([P, n_rel], F32, name="c%d" % h) for h in range(2)]
-        w_pl = [sb.tile([P, n_rel], F32, name="w%d" % h) for h in range(2)]
+        ent_list = sb.tile([P, SLOTS // PER_COLUMN], U16, name="ent_list")
+        rel_list = sb.tile([P, SLOTS // PER_COLUMN], U16, name="rel_list")
+        k_plane = [sb.tile([P, ENTITIES], F32, name="k%d" % t) for t in range(PACK)]
+        c_plane = [sb.tile([P, RELATIONS], F32, name="c%d" % h) for h in range(PAIRS)]
+        w_plane = [sb.tile([P, RELATIONS], F32, name="w%d" % h) for h in range(PAIRS)]
         k_rows = kT.rearrange("(p t) n -> p t n", t=PACK)
         c_rows = cT.rearrange("(p t) n -> p t n", t=PACK)
         w_rows = wT.rearrange("(p t) n -> p t n", t=PACK)
+        q_rows = qT[0].rearrange("(p t) n -> p t n", t=PACK)
         q_raw = [sb.tile([P, PACK, P], F32, name="q_raw%d" % m) for m in range(q_tiles)]
         margin = [sb.tile([P, 1], F32, name="margin%d" % m) for m in range(q_tiles)]
         neg_margin = [sb.tile([P, 1], F32, name="neg_margin%d" % m) for m in range(q_tiles)]
         floor = sb.tile([P, 1], F32, name="floor")
 
-        nc.sync.dma_start(c_pl[0][:], c_rows[:, 0, :])
-        nc.sync.dma_start(rel_list[:], offs2)
-        nc.sync.dma_start(w_pl[0][:], w_rows[:, 0, :])
-        nc.sync.dma_start(c_pl[1][:], c_rows[:, 2, :])
-        nc.sync.dma_start(w_pl[1][:], w_rows[:, 2, :])
+        for h in range(PAIRS):
+            nc.sync.dma_start(c_plane[h][:], c_rows[:, 2 * h, :])
+            if h == 0:
+                nc.sync.dma_start(rel_list[:], offs2)
+            nc.sync.dma_start(w_plane[h][:], w_rows[:, 2 * h, :])
         nc.sync.dma_start(ent_list[:], offs)
         for t in range(PACK):
-            nc.sync.dma_start(k_pl[t][:], k_rows[:, t, :])
+            nc.sync.dma_start(k_plane[t][:], k_rows[:, t, :])
         for m in range(q_tiles):
-            nc.sync.dma_start(q_raw[m][:], qT[0].rearrange("(p t) n -> p t n", t=PACK)[:, :, m * P:(m + 1) * P])
+            nc.sync.dma_start(q_raw[m][:], q_rows[:, :, m * P:(m + 1) * P])
         for m in range(q_tiles):
             nc.sync.dma_start(margin[m][:], mg[0, m * P:(m + 1) * P, :])
-        nc.gpsimd.memset(floor[:], LOG_FLOOR)
-        warm = sb.tile([P, 1], F32, name="warm")
-        nc.scalar.activation(warm[:], floor[:], ACT.Sigmoid)
+
+        zero = sb.tile([P, 1], F32, name="zero")
+        nc.gpsimd.memset(zero[:], 0.0)
+        one_half = sb.tile([P, 1], F32, name="one_half")
+        nc.scalar.activation(one_half[:], zero[:], ACT.Sigmoid)
+        nc.scalar.activation(floor[:], one_half[:], ACT.Copy, scale=TWICE_FLOOR)
 
         ident = sb.tile([P, P], F32, name="ident")
         make_identity(nc, ident[:])
 
         u = sb.tile([P, SLOTS * PACK], BF16, name="u", tag="u", align_bytes=64)
-        u_pairs = u[:].rearrange("p (n h e) -> p n h e", h=2, e=2)
-        u_words = u[:].bitcast(F32).rearrange("p (n h) -> p n h", h=2)
-        half = SLOTS // 2
-        blocks = half // P
-        factors = [sb.tile([P, 3, SLOTS], F32, name="factors%d" % h) for h in range(2)]
-        kg = [[sb.tile([P, half], F32, name="kg%d_%d" % (t, s), tag="kg%d_%d" % (t, s), align_bytes=64)
-               for s in range(2)] for t in range(PACK)]
-        part = {}
+        u_pairs = u[:].rearrange("p (n h e) -> p n h e", h=PAIRS, e=2)
+        u_words = u[:].bitcast(F32).rearrange("p (n h) -> p n h", h=PAIRS)
+        factors = [sb.tile([P, 3, SLOTS], F32, name="factors%d" % h) for h in range(PAIRS)]
+        picked = [[sb.tile([P, HALF], F32, name="picked%d_%d" % (t, s), tag="picked%d_%d" % (t, s), align_bytes=64)
+                   for s in range(2)] for t in range(PACK)]
 
-        for h in range(2):
-            nc.vector.tensor_copy(factors[h][:, 1, :], c_pl[h][:].indirect(rel_list[:]))
-            nc.vector.tensor_copy(factors[h][:, 2, :], w_pl[h][:].indirect(rel_list[:]))
-            nc.scalar.activation(factors[h][:, 0, :], factors[h][:, 2, :], ACT.Copy, scale=-1.0)
+        for h in range(PAIRS):
+            nc.vector.tensor_copy(factors[h][:, COS, :], c_plane[h][:].indirect(rel_list[:]))
+            nc.vector.tensor_copy(factors[h][:, SIN, :], w_plane[h][:].indirect(rel_list[:]))
+            nc.scalar.activation(factors[h][:, NEG_SIN, :], factors[h][:, SIN, :], ACT.Copy, scale=-1.0)
+
+        def first_factor(t):
+            return NEG_SIN if t % 2 else COS
 
         def gather(t):
             for s in range(2):
-                nc.vector.tensor_copy(kg[t][s][:], k_pl[t][:].indirect(ent_list[:, s * half // 16:(s + 1) * half // 16]))
+                entries = ent_list[:, s * HALF // PER_COLUMN:(s + 1) * HALF // PER_COLUMN]
+                nc.vector.tensor_copy(picked[t][s][:], k_plane[t][:].indirect(entries))
 
-        def product(t, lo, hi, engine=nc.vector, tag=None, held=None):
-            h, odd = divmod(t, 2)
-            s, first = divmod(lo, half)
-            if (t, s) not in part:
-                part[t, s] = sb.tile([P, 2, half], F32, name="part%d_%d" % (t, s), tag=tag or "part%d_%d" % (t, s),
+        term = {}
+
+        def product(engine, t, lo, hi, source=None, tag=None):
+            s, first = divmod(lo, HALF)
+            if (t, s) not in term:
+                term[t, s] = sb.tile([P, 2, HALF], F32, name="term%d_%d" % (t, s), tag=tag or "term%d_%d" % (t, s),
                                      align_bytes=64)
+            if source is None:
+                source = factors[t // 2][:, first_factor(t):first_factor(t) + 2, lo:hi]
             cols = slice(first, first + hi - lo)
-            engine.tensor_tensor(part[t, s][:, :, cols],
-                                 factors[h][:, 1 - odd:3 - odd, lo:hi] if held is None else held[:],
-                                    kg[t][s][:, cols].unsqueeze(1).to_broadcast([P, 2, hi - lo]), ALU.mult)
+            engine.tensor_tensor(term[t, s][:, :, cols], source,
+                                 picked[t][s][:, cols].unsqueeze(1).to_broadcast([P, 2, hi - lo]), ALU.mult)
 
-        columns = [[(1, 2), (1, 3), (2, 2), (2, 3)], [(0, 2), (0, 3), (0, 0), (1, 0)]]
-        crossed = {}
-        for i, wanted in enumerate(columns):
-            across = ps.tile([P, len(wanted), P], F32, name="across%d" % i, tag="bank%d" % (2 + i))
-            landed = sb.tile([P, len(wanted), P], F32, name="landed%d" % i)
-            for x, (f, b) in enumerate(wanted):
-                nc.tensor.transpose(across[:, x, :], factors[1][:, f, b * P:(b + 1) * P], ident[:])
-                crossed[f, b] = landed[:, x, :]
-            nc.scalar.copy(landed[:], across[:])
-        held = {}
-        for i, (odd, lo, hi) in enumerate([(0, half, SLOTS), (1, half, SLOTS), (1, 0, P)]):
-            held[odd, lo] = ps.tile([P, 2, hi - lo], F32, name="held%d" % i, tag="bank%d" % (4 + i))
+        needed = []
+        for t, lo, hi in HELD:
             for e in range(2):
                 for b in range(lo // P, hi // P):
-                    nc.tensor.transpose(held[odd, lo][:, e, b * P - lo:(b + 1) * P - lo], crossed[1 - odd + e, b],
-                                        ident[:])
+                    if (first_factor(t) + e, b) not in needed:
+                        needed.append((first_factor(t) + e, b))
+        flipped = {}
+        for i in range(len(needed) // 4):
+            across = ps.tile([P, 4, P], F32, name="across%d" % i, tag="bank%d" % (TRANSIT_BANK + i))
+            landed = sb.tile([P, 4, P], F32, name="landed%d" % i)
+            for x, (row, b) in enumerate(needed[4 * i:4 * i + 4]):
+                nc.tensor.transpose(across[:, x, :], factors[1][:, row, b * P:(b + 1) * P], ident[:])
+                flipped[row, b] = landed[:, x, :]
+            nc.scalar.copy(landed[:], across[:])
+        held = {}
+        for i, (t, lo, hi) in enumerate(HELD):
+            held[t, lo] = ps.tile([P, 2, hi - lo], F32, name="held%d" % i, tag="bank%d" % (HELD_BANK + i))
+            for e in range(2):
+                for b in range(lo // P, hi // P):
+                    nc.tensor.transpose(held[t, lo][:, e, b * P - lo:(b + 1) * P - lo],
+                                        flipped[first_factor(t) + e, b], ident[:])
 
-        turned = [ps.tile([P, blocks, 2, P], F32, name="turned%d" % s, tag="bank%d" % s) for s in range(2)]
+        summed = [ps.tile([P, BLOCKS, 2, P], F32, name="summed%d" % s, tag="bank%d" % (SUM_BANK + s))
+                  for s in range(2)]
 
-        def turn(t, s):
-            for b in range(blocks):
+        def add_transposed(t, s):
+            for b in range(BLOCKS):
                 for e in range(2):
-                    nc.tensor.matmul(turned[s][:, b, e, :], part[t, s][:, e, b * P:(b + 1) * P], ident[:],
-                                     start=(t, b, e) == (0, 0, 0), stop=(t, b, e) == (1, blocks - 1, 1),
+                    nc.tensor.matmul(summed[s][:, b, e, :], term[t, s][:, e, b * P:(b + 1) * P], ident[:],
+                                     start=(t, b, e) == (0, 0, 0), stop=(t, b, e) == (1, BLOCKS - 1, 1),
                                      is_transpose=True)
 
-        def turn_back(s):
-            rounded = sb.tile([P, blocks * P * 2], BF16, name="rounded%d" % s)
-            nc.scalar.activation(rounded[:].rearrange("n (b p e) -> n b p e", b=blocks, e=2),
-                                 turned[s][:].rearrange("n b e p -> n b p e"), ACT.Copy)
-            back = ps.tile([P, half], F32, name="back%d" % s, tag="bank%d" % (2 + s))
-            for b in range(blocks):
-                nc.tensor.transpose(back[:, b * P:(b + 1) * P], rounded[:].bitcast(F32)[:, b * P:(b + 1) * P], ident[:])
-            nc.scalar.copy(u_words[:, s * half:(s + 1) * half, 0], back[:])
+        def lay_first_pair(s):
+            rounded = sb.tile([P, BLOCKS * P * 2], BF16, name="rounded%d" % s)
+            nc.scalar.activation(rounded[:].rearrange("n (b p e) -> n b p e", b=BLOCKS, e=2),
+                                 summed[s][:].rearrange("n b e p -> n b p e"), ACT.Copy)
+            back = ps.tile([P, HALF], F32, name="back%d" % s, tag="bank%d" % (TRANSIT_BANK + s))
+            for b in range(BLOCKS):
+                nc.tensor.transpose(back[:, b * P:(b + 1) * P], rounded[:].bitcast(F32)[:, b * P:(b + 1) * P],
+                                    ident[:])
+            nc.scalar.copy(u_words[:, s * HALF:(s + 1) * HALF, 0], back[:])
 
-        for t in range(2):
-            gather(t)
-            product(t, 0, half)
-            turn(t, 0)
-            if t == 0:
-                product(t, half, SLOTS, nc.gpsimd, "kg0_0")
-            else:
-                product(t, half, SLOTS)
-            turn(t, 1)
+        gather(0)
+        product(nc.vector, 0, 0, HALF)
+        add_transposed(0, 0)
+        product(nc.gpsimd, 0, HALF, SLOTS, tag="picked0_0")
+        add_transposed(0, 1)
+        gather(1)
         for s in range(2):
-            turn_back(s)
+            product(nc.vector, 1, s * HALF, (s + 1) * HALF)
+            add_transposed(1, s)
+        for s in range(2):
+            lay_first_pair(s)
         gather(2)
-        product(2, 0, half, nc.gpsimd)
-        product(2, half, SLOTS, held=held[0, half])
+        product(nc.gpsimd, 2, 0, HALF)
+        product(nc.vector, 2, HALF, SLOTS, held[2, HALF][:])
         gather(3)
-        product(3, P, half, nc.gpsimd)
-        product(3, 0, P, held=held[1, 0])
-        product(3, half, SLOTS, held=held[1, half])
+        product(nc.gpsimd, 3, P, HALF)
+        product(nc.vector, 3, 0, P, held[3, 0][:])
+        product(nc.vector, 3, HALF, SLOTS, held[3, HALF][:])
 
-        def pair_sum(lo, hi):
-            s, first = divmod(lo, half)
+        def sum_second_pair(lo, hi):
+            s, first = divmod(lo, HALF)
             cols = slice(first, first + hi - lo)
             nc.vector.tensor_tensor(u_pairs[:, lo:hi, 1, :].rearrange("p (c i) e -> p c e i", i=2),
-                                    part[2, s][:, :, cols].rearrange("p e (c i) -> p c e i", i=2),
-                                    part[3, s][:, :, cols].rearrange("p e (c i) -> p c e i", i=2), ALU.add)
+                                    term[2, s][:, :, cols].rearrange("p e (c i) -> p c e i", i=2),
+                                    term[3, s][:, :, cols].rearrange("p e (c i) -> p c e i", i=2), ALU.add)
 
         q_bf = sb.tile([P, NQ * PACK], BF16, name="q_bf", align_bytes=64)
         q_codes = sb.tile([P, NQ], U32, name="q_codes", align_bytes=64)
@@ -160,46 +182,40 @@ def tile_attend_pre_rotate_f_topk_kernel(tc, qT, kT, cT, wT, mg, offs, offs2, ou
         u_codes = sb.tile([P, SLOTS], U32, name="u_codes", tag="codes", align_bytes=64)
         u_scales = sb.tile([P, SLOTS], U8, name="u_scales", align_bytes=64)
         for m in range(q_tiles):
-            nc.scalar.activation(q_bf[:, m * P * PACK:(m + 1) * P * PACK].rearrange("p (c i t) -> p c t i", i=4, t=PACK),
-                                 q_raw[m][:].rearrange("p t (c i) -> p c t i", i=4), ACT.Copy)
+            nc.scalar.activation(
+                q_bf[:, m * P * PACK:(m + 1) * P * PACK].rearrange("p (c i t) -> p c t i", i=4, t=PACK),
+                q_raw[m][:].rearrange("p t (c i) -> p c t i", i=4), ACT.Copy)
         for m in range(q_tiles):
             nc.scalar.activation(neg_margin[m][:], margin[m][:], ACT.Copy, scale=-1.0)
 
-        def quant_u(lo, hi):
-            nc.vector.quantize_mx(u_codes[:, lo:hi].bitcast(FP8X4), u_scales[:, lo:hi], u[:, lo * PACK:hi * PACK])
-
-        sig = sb.tile([P, q_tiles, SLOTS], F32, name="sig")
-        acc = {}
-
-        def score(j):
-            lo, hi = GROUPS[j]
-            for m in range(q_tiles):
-                cols = slice(m * P, (m + 1) * P)
-                tag = "bank%d" % [[7, 4], [6, 5], [0, 1], [2, 3]][j][m]
-                acc[j, m] = ps.tile([P, hi - lo], F32, name="acc%d_%d" % (j, m), tag=tag)
-                nc.tensor.matmul_mx(acc[j, m][:], lhsT=q_codes[:, cols].bitcast(FP8X4), lhsT_scale=q_scales[:, cols],
-                                    rhs=u_codes[:, lo:hi].bitcast(FP8X4), rhs_scale=u_scales[:, lo:hi],
-                                    start=True, stop=True)
-                nc.scalar.activation(sig[:, m, lo:hi], acc[j, m][:], ACT.Sigmoid, bias=neg_margin[m][:])
-
-        pair_sum(*GROUPS[0])
+        sum_second_pair(*GROUPS[0])
         for m in range(q_tiles):
             nc.vector.quantize_mx(q_codes[:, m * P:(m + 1) * P].bitcast(FP8X4), q_scales[:, m * P:(m + 1) * P],
                                   q_bf[:, m * P * PACK:(m + 1) * P * PACK])
-        for j in range(len(GROUPS)):
+        for j, (lo, hi) in enumerate(GROUPS):
             if j + 1 < len(GROUPS):
-                pair_sum(*GROUPS[j + 1])
-            quant_u(*GROUPS[j])
-        for j in range(len(GROUPS)):
-            score(j)
+                sum_second_pair(*GROUPS[j + 1])
+            nc.vector.quantize_mx(u_codes[:, lo:hi].bitcast(FP8X4), u_scales[:, lo:hi], u[:, lo * PACK:hi * PACK])
+
+        sig = sb.tile([P, q_tiles, SLOTS], F32, name="sig")
+        score = {}
+        for j, (lo, hi) in enumerate(GROUPS):
+            for m in range(q_tiles):
+                rows = slice(m * P, (m + 1) * P)
+                score[j, m] = ps.tile([P, hi - lo], F32, name="score%d_%d" % (j, m), tag="bank%d" % SCORE_BANKS[j][m])
+                nc.tensor.matmul_mx(score[j, m][:], lhsT=q_codes[:, rows].bitcast(FP8X4), lhsT_scale=q_scales[:, rows],
+                                    rhs=u_codes[:, lo:hi].bitcast(FP8X4), rhs_scale=u_scales[:, lo:hi],
+                                    start=True, stop=True)
+                nc.scalar.activation(sig[:, m, lo:hi], score[j, m][:], ACT.Sigmoid, bias=neg_margin[m][:])
 
         v = sb.tile([P, q_tiles, SLOTS], F32, name="v", tag="u", align_bytes=64)
-        lg = sb.tile([P, q_tiles, SLOTS], F32, name="lg", tag="codes", align_bytes=64)
-        res = sb.tile([P, q_tiles, SLOTS], F32, name="res")
-        for m in (1, 0):
+        log_sig = sb.tile([P, q_tiles, SLOTS], F32, name="log_sig", tag="codes", align_bytes=64)
+        result = sb.tile([P, q_tiles, SLOTS], F32, name="result")
+        for m in reversed(range(q_tiles)):
             for j, (lo, hi) in enumerate(GROUPS):
-                nc.vector.tensor_scalar(v[:, m, lo:hi], acc[j, m][:], -1.0, margin[m][:], ALU.mult, ALU.add)
+                nc.vector.tensor_scalar(v[:, m, lo:hi], score[j, m][:], -1.0, margin[m][:], ALU.mult, ALU.add)
         for m, lo, hi in PIECES:
-            nc.scalar.activation(lg[:, m, lo:hi], sig[:, m, lo:hi], ACT.Ln, bias=floor[:])
-            nc.vector.scalar_tensor_tensor(res[:, m, lo:hi], lg[:, m, lo:hi], -1.0, v[:, m, lo:hi], ALU.mult, ALU.max)
-            nc.sync.dma_start(out[0, m * P:(m + 1) * P, lo:hi], res[:, m, lo:hi])
+            nc.scalar.activation(log_sig[:, m, lo:hi], sig[:, m, lo:hi], ACT.Ln, bias=floor[:])
+            nc.vector.scalar_tensor_tensor(result[:, m, lo:hi], log_sig[:, m, lo:hi], -1.0, v[:, m, lo:hi],
+                                           ALU.mult, ALU.max)
+            nc.sync.dma_start(out[0, m * P:(m + 1) * P, lo:hi], result[:, m, lo:hi])

@@ -41,14 +41,14 @@ def tile_attend_pre_rotate_f_topk_kernel(tc, qT, kT, cT, wT, mg, offs, offs2, ou
 
         ent_list = sb.tile([P, SLOTS // PER_COLUMN], U16, name="ent_list")
         rel_list = sb.tile([P, SLOTS // PER_COLUMN], U16, name="rel_list")
-        k_plane = [sb.tile([P, ENTITIES], F32, name="k%d" % t) for t in range(PACK)]
-        c_plane = [sb.tile([P, RELATIONS], F32, name="c%d" % h) for h in range(PAIRS)]
-        w_plane = [sb.tile([P, RELATIONS], F32, name="w%d" % h) for h in range(PAIRS)]
+        k_plane = [sb.tile([P, ENTITIES], F32, name="k%d" % t, align_bytes=256) for t in range(PACK)]
+        c_plane = [sb.tile([P, RELATIONS], F32, name="c%d" % h, align_bytes=256) for h in range(PAIRS)]
+        w_plane = [sb.tile([P, RELATIONS], F32, name="w%d" % h, align_bytes=256) for h in range(PAIRS)]
         k_rows = kT.rearrange("(p t) n -> p t n", t=PACK)
         c_rows = cT.rearrange("(p t) n -> p t n", t=PACK)
         w_rows = wT.rearrange("(p t) n -> p t n", t=PACK)
         q_rows = qT[0].rearrange("(p t) n -> p t n", t=PACK)
-        q_raw = [sb.tile([P, PACK, P], F32, name="q_raw%d" % m) for m in range(q_tiles)]
+        q_raw = [sb.tile([P, PACK, P], F32, name="q_raw%d" % m, align_bytes=256) for m in range(q_tiles)]
         margin = [sb.tile([P, 1], F32, name="margin%d" % m) for m in range(q_tiles)]
         neg_margin = [sb.tile([P, 1], F32, name="neg_margin%d" % m) for m in range(q_tiles)]
         floor = sb.tile([P, 1], F32, name="floor")
@@ -75,11 +75,11 @@ def tile_attend_pre_rotate_f_topk_kernel(tc, qT, kT, cT, wT, mg, offs, offs2, ou
         ident = sb.tile([P, P], F32, name="ident")
         make_identity(nc, ident[:])
 
-        u = sb.tile([P, SLOTS * PACK], BF16, name="u", tag="u", align_bytes=64)
+        u = sb.tile([P, SLOTS * PACK], BF16, name="u", tag="u", align_bytes=256)
         u_pairs = u[:].rearrange("p (n h e) -> p n h e", h=PAIRS, e=2)
         u_words = u[:].bitcast(F32).rearrange("p (n h) -> p n h", h=PAIRS)
-        factors = [sb.tile([P, 3, SLOTS], F32, name="factors%d" % h) for h in range(PAIRS)]
-        picked = [[sb.tile([P, HALF], F32, name="picked%d_%d" % (t, s), tag="picked%d_%d" % (t, s), align_bytes=64)
+        factors = [sb.tile([P, 3, SLOTS], F32, name="factors%d" % h, align_bytes=256) for h in range(PAIRS)]
+        picked = [[sb.tile([P, HALF], F32, name="picked%d_%d" % (t, s), tag="picked%d_%d" % (t, s), align_bytes=256)
                    for s in range(2)] for t in range(PACK)]
 
         for h in range(PAIRS):
@@ -101,7 +101,7 @@ def tile_attend_pre_rotate_f_topk_kernel(tc, qT, kT, cT, wT, mg, offs, offs2, ou
             s, first = divmod(lo, HALF)
             if (t, s) not in term:
                 term[t, s] = sb.tile([P, 2, HALF], F32, name="term%d_%d" % (t, s), tag=tag or "term%d_%d" % (t, s),
-                                     align_bytes=64)
+                                     align_bytes=256)
             if source is None:
                 source = factors[t // 2][:, first_factor(t):first_factor(t) + 2, lo:hi]
             cols = slice(first, first + hi - lo)
@@ -176,11 +176,11 @@ def tile_attend_pre_rotate_f_topk_kernel(tc, qT, kT, cT, wT, mg, offs, offs2, ou
                                     term[2, s][:, :, cols].rearrange("p e (c i) -> p c e i", i=2),
                                     term[3, s][:, :, cols].rearrange("p e (c i) -> p c e i", i=2), ALU.add)
 
-        q_bf = sb.tile([P, NQ * PACK], BF16, name="q_bf", align_bytes=64)
-        q_codes = sb.tile([P, NQ], U32, name="q_codes", align_bytes=64)
-        q_scales = sb.tile([P, NQ], U8, name="q_scales", align_bytes=64)
-        u_codes = sb.tile([P, SLOTS], U32, name="u_codes", tag="codes", align_bytes=64)
-        u_scales = sb.tile([P, SLOTS], U8, name="u_scales", align_bytes=64)
+        q_bf = sb.tile([P, NQ * PACK], BF16, name="q_bf", align_bytes=256)
+        q_codes = sb.tile([P, NQ], U32, name="q_codes", align_bytes=256)
+        q_scales = sb.tile([P, NQ], U8, name="q_scales", align_bytes=256)
+        u_codes = sb.tile([P, SLOTS], U32, name="u_codes", tag="codes", align_bytes=256)
+        u_scales = sb.tile([P, SLOTS], U8, name="u_scales", align_bytes=256)
         for m in range(q_tiles):
             nc.scalar.activation(
                 q_bf[:, m * P * PACK:(m + 1) * P * PACK].rearrange("p (c i t) -> p c t i", i=4, t=PACK),
@@ -197,7 +197,7 @@ def tile_attend_pre_rotate_f_topk_kernel(tc, qT, kT, cT, wT, mg, offs, offs2, ou
                 sum_second_pair(*GROUPS[j + 1])
             nc.vector.quantize_mx(u_codes[:, lo:hi].bitcast(FP8X4), u_scales[:, lo:hi], u[:, lo * PACK:hi * PACK])
 
-        sig = sb.tile([P, q_tiles, SLOTS], F32, name="sig")
+        sig = sb.tile([P, q_tiles, SLOTS], F32, name="sig", align_bytes=256)
         score = {}
         for j, (lo, hi) in enumerate(GROUPS):
             for m in range(q_tiles):
@@ -208,9 +208,9 @@ def tile_attend_pre_rotate_f_topk_kernel(tc, qT, kT, cT, wT, mg, offs, offs2, ou
                                     start=True, stop=True)
                 nc.scalar.activation(sig[:, m, lo:hi], score[j, m][:], ACT.Sigmoid, bias=neg_margin[m][:])
 
-        v = sb.tile([P, q_tiles, SLOTS], F32, name="v", tag="u", align_bytes=64)
-        log_sig = sb.tile([P, q_tiles, SLOTS], F32, name="log_sig", tag="codes", align_bytes=64)
-        result = sb.tile([P, q_tiles, SLOTS], F32, name="result")
+        v = sb.tile([P, q_tiles, SLOTS], F32, name="v", tag="u", align_bytes=256)
+        log_sig = sb.tile([P, q_tiles, SLOTS], F32, name="log_sig", tag="codes", align_bytes=256)
+        result = sb.tile([P, q_tiles, SLOTS], F32, name="result", align_bytes=256)
         for m in reversed(range(q_tiles)):
             for j, (lo, hi) in enumerate(GROUPS):
                 nc.vector.tensor_scalar(v[:, m, lo:hi], score[j, m][:], -1.0, margin[m][:], ALU.mult, ALU.add)

@@ -24,8 +24,10 @@ BYTES = 4 * (D * ENTITIES + D * RELATIONS + D * NQ + NQ + NQ * SLOTS) + 2 * 2 * 
 
 GROUPS = [(lo, lo + P) for lo in range(0, SLOTS, P)]
 NEG_SIN, COS, SIN = 0, 1, 2
-HELD = [(2, HALF, SLOTS), (3, HALF, SLOTS), (3, 0, P)]
-SUM_BANK, TRANSIT_BANK, HELD_BANK = 0, 2, 4
+HELD = [(1, 0, HALF), (2, HALF, SLOTS), (3, HALF, SLOTS), (3, 0, P)]
+HELD_BANKS = [7, 4, 5, 6]
+ACROSS_BANKS = [0, 2, 3]
+SUM_BANK, TRANSIT_BANK = 0, 2
 SCORE_BANKS = [[7, 4], [6, 5], [0, 1], [2, 3]]
 PIECES = [(1, 0, 128), (1, 128, 320), (1, 320, 512), (0, 0, 192), (0, 192, 384), (0, 384, 512)]
 TWICE_FLOOR = 2.0 ** -59
@@ -90,8 +92,8 @@ def tile_attend_pre_rotate_f_topk_kernel(tc, qT, kT, cT, wT, mg, offs, offs2, ou
         def first_factor(t):
             return NEG_SIN if t % 2 else COS
 
-        def gather(t):
-            for s in range(2):
+        def gather(t, halves=(0, 1)):
+            for s in halves:
                 entries = ent_list[:, s * HALF // PER_COLUMN:(s + 1) * HALF // PER_COLUMN]
                 nc.vector.tensor_copy(picked[t][s][:], k_plane[t][:].indirect(entries))
 
@@ -112,23 +114,28 @@ def tile_attend_pre_rotate_f_topk_kernel(tc, qT, kT, cT, wT, mg, offs, offs2, ou
         for t, lo, hi in HELD:
             for e in range(2):
                 for b in range(lo // P, hi // P):
-                    if (first_factor(t) + e, b) not in needed:
-                        needed.append((first_factor(t) + e, b))
+                    if (t // 2, first_factor(t) + e, b) not in needed:
+                        needed.append((t // 2, first_factor(t) + e, b))
         flipped = {}
-        for i in range(len(needed) // 4):
-            across = ps.tile([P, 4, P], F32, name="across%d" % i, tag="bank%d" % (TRANSIT_BANK + i))
-            landed = sb.tile([P, 4, P], F32, name="landed%d" % i)
-            for x, (row, b) in enumerate(needed[4 * i:4 * i + 4]):
-                nc.tensor.transpose(across[:, x, :], factors[1][:, row, b * P:(b + 1) * P], ident[:])
-                flipped[row, b] = landed[:, x, :]
-            nc.scalar.copy(landed[:], across[:])
         held = {}
-        for i, (t, lo, hi) in enumerate(HELD):
-            held[t, lo] = ps.tile([P, 2, hi - lo], F32, name="held%d" % i, tag="bank%d" % (HELD_BANK + i))
-            for e in range(2):
-                for b in range(lo // P, hi // P):
-                    nc.tensor.transpose(held[t, lo][:, e, b * P - lo:(b + 1) * P - lo],
-                                        flipped[first_factor(t) + e, b], ident[:])
+        for h in range(PAIRS):
+            for i in range(len(needed) // 4):
+                if needed[4 * i][0] != h:
+                    continue
+                across = ps.tile([P, 4, P], F32, name="across%d" % i, tag="bank%d" % ACROSS_BANKS[i])
+                landed = sb.tile([P, 4, P], F32, name="landed%d" % i)
+                for x, (pair, row, b) in enumerate(needed[4 * i:4 * i + 4]):
+                    nc.tensor.transpose(across[:, x, :], factors[pair][:, row, b * P:(b + 1) * P], ident[:])
+                    flipped[pair, row, b] = landed[:, x, :]
+                nc.scalar.copy(landed[:], across[:])
+            for i, (t, lo, hi) in enumerate(HELD):
+                if t // 2 != h:
+                    continue
+                held[t, lo] = ps.tile([P, 2, hi - lo], F32, name="held%d" % i, tag="bank%d" % HELD_BANKS[i])
+                for e in range(2):
+                    for b in range(lo // P, hi // P):
+                        nc.tensor.transpose(held[t, lo][:, e, b * P - lo:(b + 1) * P - lo],
+                                            flipped[h, first_factor(t) + e, b], ident[:])
 
         summed = [ps.tile([P, BLOCKS, 2, P], F32, name="summed%d" % s, tag="bank%d" % (SUM_BANK + s))
                   for s in range(2)]
@@ -148,7 +155,7 @@ def tile_attend_pre_rotate_f_topk_kernel(tc, qT, kT, cT, wT, mg, offs, offs2, ou
             for b in range(BLOCKS):
                 nc.tensor.transpose(back[:, b * P:(b + 1) * P], rounded[:].bitcast(F32)[:, b * P:(b + 1) * P],
                                     ident[:])
-            nc.scalar.copy(u_words[:, s * HALF:(s + 1) * HALF, 0], back[:])
+            nc.scalar.copy(u_words[:, s * HALF:(s + 1) * HALF, :], back[:].unsqueeze(2).to_broadcast([P, HALF, PAIRS]))
 
         gather(0)
         product(nc.vector, 0, 0, HALF)
@@ -156,14 +163,15 @@ def tile_attend_pre_rotate_f_topk_kernel(tc, qT, kT, cT, wT, mg, offs, offs2, ou
         product(nc.gpsimd, 0, HALF, SLOTS, tag="picked0_0")
         add_transposed(0, 1)
         gather(1)
-        for s in range(2):
-            product(nc.vector, 1, s * HALF, (s + 1) * HALF)
-            add_transposed(1, s)
+        product(nc.vector, 1, 0, HALF, held[1, 0][:])
+        add_transposed(1, 0)
+        product(nc.gpsimd, 1, HALF, SLOTS)
+        add_transposed(1, 1)
         for s in range(2):
             lay_first_pair(s)
-        gather(2)
-        product(nc.gpsimd, 2, 0, HALF)
+        gather(2, halves=(1, 0))
         product(nc.vector, 2, HALF, SLOTS, held[2, HALF][:])
+        product(nc.gpsimd, 2, 0, HALF)
         gather(3)
         product(nc.gpsimd, 3, P, HALF)
         product(nc.vector, 3, 0, P, held[3, 0][:])

@@ -22,11 +22,11 @@ PER_COLUMN = 16
 FLOPS = 2 * D * NQ * SLOTS
 BYTES = 4 * (D * ENTITIES + D * RELATIONS + D * NQ + NQ + NQ * SLOTS) + 2 * 2 * P * SLOTS // PER_COLUMN
 
-GROUPS = [(lo, lo + P) for lo in range(0, SLOTS, P)]
+GROUPS = [(0, P), (2 * P, 3 * P), (P, 2 * P), (3 * P, 4 * P)]
 NEG_SIN, COS, SIN = 0, 1, 2
-HELD = [(1, 0, HALF), (2, HALF, SLOTS), (3, HALF, SLOTS), (3, 0, P)]
-HELD_BANKS = [7, 4, 5, 6]
-ACROSS_BANKS = [0, 2, 3]
+HELD = [(2, HALF, SLOTS), (3, HALF, SLOTS), (3, 0, P)]
+HELD_BANKS = [4, 5, 6]
+ACROSS_BANKS = [2, 3]
 SUM_BANK, TRANSIT_BANK = 0, 2
 SCORE_BANKS = [[7, 4], [6, 5], [0, 1], [2, 3]]
 PIECES = [(1, 0, 128), (1, 128, 320), (1, 320, 512), (0, 0, 192), (0, 192, 384), (0, 384, 512)]
@@ -80,6 +80,7 @@ def tile_attend_pre_rotate_f_topk_kernel(tc, qT, kT, cT, wT, mg, offs, offs2, ou
         u = sb.tile([P, SLOTS * PACK], BF16, name="u", tag="u", align_bytes=256)
         u_pairs = u[:].rearrange("p (n h e) -> p n h e", h=PAIRS, e=2)
         u_words = u[:].bitcast(F32).rearrange("p (n h) -> p n h", h=PAIRS)
+        apart = sb.tile([P, PAIRS * HALF * 2], BF16, name="apart", align_bytes=256)
         factors = [sb.tile([P, 3, SLOTS], F32, name="factors%d" % h, align_bytes=256) for h in range(PAIRS)]
         picked = [[sb.tile([P, HALF], F32, name="picked%d_%d" % (t, s), tag="picked%d_%d" % (t, s), align_bytes=256)
                    for s in range(2)] for t in range(PACK)]
@@ -155,19 +156,21 @@ def tile_attend_pre_rotate_f_topk_kernel(tc, qT, kT, cT, wT, mg, offs, offs2, ou
             for b in range(BLOCKS):
                 nc.tensor.transpose(back[:, b * P:(b + 1) * P], rounded[:].bitcast(F32)[:, b * P:(b + 1) * P],
                                     ident[:])
-            nc.scalar.copy(u_words[:, s * HALF:(s + 1) * HALF, :], back[:].unsqueeze(2).to_broadcast([P, HALF, PAIRS]))
+            if s == 0:
+                nc.scalar.copy(apart[:].bitcast(F32)[:, 0:HALF], back[:])
+            else:
+                nc.scalar.copy(u_words[:, HALF:SLOTS, :], back[:].unsqueeze(2).to_broadcast([P, HALF, PAIRS]))
 
         gather(0)
         product(nc.vector, 0, 0, HALF)
         add_transposed(0, 0)
         product(nc.gpsimd, 0, HALF, SLOTS, tag="picked0_0")
         add_transposed(0, 1)
-        gather(1)
-        product(nc.vector, 1, 0, HALF, held[1, 0][:])
-        add_transposed(1, 0)
-        product(nc.gpsimd, 1, HALF, SLOTS)
-        add_transposed(1, 1)
-        for s in range(2):
+        gather(1, halves=(1, 0))
+        for s in (1, 0):
+            product(nc.vector, 1, s * HALF, (s + 1) * HALF)
+            add_transposed(1, s)
+        for s in (1, 0):
             lay_first_pair(s)
         gather(2, halves=(1, 0))
         product(nc.vector, 2, HALF, SLOTS, held[2, HALF][:])
@@ -180,9 +183,16 @@ def tile_attend_pre_rotate_f_topk_kernel(tc, qT, kT, cT, wT, mg, offs, offs2, ou
         def sum_second_pair(lo, hi):
             s, first = divmod(lo, HALF)
             cols = slice(first, first + hi - lo)
-            nc.vector.tensor_tensor(u_pairs[:, lo:hi, 1, :].rearrange("p (c i) e -> p c e i", i=2),
-                                    term[2, s][:, :, cols].rearrange("p e (c i) -> p c e i", i=2),
+            if s == 0:
+                target = apart[:, 2 * (HALF + lo):2 * (HALF + hi)].rearrange("p (c i e) -> p c e i", i=2, e=2)
+            else:
+                target = u_pairs[:, lo:hi, 1, :].rearrange("p (c i) e -> p c e i", i=2)
+            nc.vector.tensor_tensor(target, term[2, s][:, :, cols].rearrange("p e (c i) -> p c e i", i=2),
                                     term[3, s][:, :, cols].rearrange("p e (c i) -> p c e i", i=2), ALU.add)
+
+        def weave(lo, hi):
+            nc.scalar.copy(u_words[:, lo:hi, :],
+                           apart[:].bitcast(F32).rearrange("p (h n) -> p n h", h=PAIRS)[:, lo:hi, :])
 
         q_bf = sb.tile([P, NQ * PACK], BF16, name="q_bf", align_bytes=256)
         q_codes = sb.tile([P, NQ], U32, name="q_codes", align_bytes=256)
@@ -193,17 +203,24 @@ def tile_attend_pre_rotate_f_topk_kernel(tc, qT, kT, cT, wT, mg, offs, offs2, ou
             nc.scalar.activation(
                 q_bf[:, m * P * PACK:(m + 1) * P * PACK].rearrange("p (c i t) -> p c t i", i=4, t=PACK),
                 q_raw[m][:].rearrange("p t (c i) -> p c t i", i=4), ACT.Copy)
+
+        def quantize_u(lo, hi):
+            nc.vector.quantize_mx(u_codes[:, lo:hi].bitcast(FP8X4), u_scales[:, lo:hi], u[:, lo * PACK:hi * PACK])
+
+        for j in (0, 2):
+            sum_second_pair(*GROUPS[j])
+            weave(*GROUPS[j])
         for m in range(q_tiles):
             nc.scalar.activation(neg_margin[m][:], margin[m][:], ACT.Copy, scale=-1.0)
-
-        sum_second_pair(*GROUPS[0])
+        sum_second_pair(*GROUPS[1])
         for m in range(q_tiles):
             nc.vector.quantize_mx(q_codes[:, m * P:(m + 1) * P].bitcast(FP8X4), q_scales[:, m * P:(m + 1) * P],
                                   q_bf[:, m * P * PACK:(m + 1) * P * PACK])
-        for j, (lo, hi) in enumerate(GROUPS):
-            if j + 1 < len(GROUPS):
-                sum_second_pair(*GROUPS[j + 1])
-            nc.vector.quantize_mx(u_codes[:, lo:hi].bitcast(FP8X4), u_scales[:, lo:hi], u[:, lo * PACK:hi * PACK])
+        quantize_u(*GROUPS[0])
+        quantize_u(*GROUPS[1])
+        sum_second_pair(*GROUPS[3])
+        quantize_u(*GROUPS[2])
+        quantize_u(*GROUPS[3])
 
         sig = sb.tile([P, q_tiles, SLOTS], F32, name="sig", align_bytes=256)
         score = {}

@@ -55,9 +55,9 @@ def tile_attend_pre_rotate_f_topk_kernel(tc, qT, kT, cT, wT, mg, offs, offs2, ou
         neg_margin = [sb.tile([P, 1], F32, name="neg_margin%d" % m) for m in range(q_tiles)]
         floor = sb.tile([P, 1], F32, name="floor")
 
-        for h in range(PAIRS):
+        for h in reversed(range(PAIRS)):
             nc.sync.dma_start(c_plane[h][:], c_rows[:, 2 * h, :])
-            if h == 0:
+            if h == PAIRS - 1:
                 nc.sync.dma_start(rel_list[:], offs2)
             nc.sync.dma_start(w_plane[h][:], w_rows[:, 2 * h, :])
         nc.sync.dma_start(ent_list[:], offs)
@@ -85,7 +85,7 @@ def tile_attend_pre_rotate_f_topk_kernel(tc, qT, kT, cT, wT, mg, offs, offs2, ou
         picked = [[sb.tile([P, HALF], F32, name="picked%d_%d" % (t, s), tag="picked%d_%d" % (t, s), align_bytes=256)
                    for s in range(2)] for t in range(PACK)]
 
-        for h in range(PAIRS):
+        for h in reversed(range(PAIRS)):
             nc.vector.tensor_copy(factors[h][:, COS, :], c_plane[h][:].indirect(rel_list[:]))
             nc.vector.tensor_copy(factors[h][:, SIN, :], w_plane[h][:].indirect(rel_list[:]))
             nc.scalar.activation(factors[h][:, NEG_SIN, :], factors[h][:, SIN, :], ACT.Copy, scale=-1.0)

@@ -24,9 +24,9 @@ BYTES = 4 * (D * ENTITIES + D * RELATIONS + D * NQ + NQ + NQ * SLOTS) + 2 * 2 * 
 
 GROUPS = [(0, P), (2 * P, 3 * P), (P, 2 * P), (3 * P, 4 * P)]
 NEG_SIN, COS, SIN = 0, 1, 2
-HELD = [(2, HALF, SLOTS), (3, HALF, SLOTS), (3, 0, P)]
-HELD_BANKS = [4, 5, 6]
-ACROSS_BANKS = [2, 3]
+HELD = [(2, HALF, SLOTS), (3, HALF, SLOTS), (3, 0, P), (1, 0, HALF)]
+HELD_BANKS = [4, 5, 6, 1]
+ACROSS_BANKS = [2, 3, 7]
 SUM_BANK, TRANSIT_BANK = 0, 2
 SCORE_BANKS = [[7, 4], [6, 5], [0, 1], [2, 3]]
 PIECES = [(1, 0, 128), (1, 128, 320), (1, 320, 512), (0, 0, 192), (0, 192, 384), (0, 384, 512)]
@@ -138,40 +138,46 @@ def tile_attend_pre_rotate_f_topk_kernel(tc, qT, kT, cT, wT, mg, offs, offs2, ou
                         nc.tensor.transpose(held[t, lo][:, e, b * P - lo:(b + 1) * P - lo],
                                             flipped[h, first_factor(t) + e, b], ident[:])
 
-        summed = [ps.tile([P, BLOCKS, 2, P], F32, name="summed%d" % s, tag="bank%d" % (SUM_BANK + s))
-                  for s in range(2)]
+        summed = ps.tile([P, BLOCKS, 2, P], F32, name="summed", tag="bank%d" % SUM_BANK)
 
-        def add_transposed(t, s):
+        def add_transposed(t):
             for b in range(BLOCKS):
                 for e in range(2):
-                    nc.tensor.matmul(summed[s][:, b, e, :], term[t, s][:, e, b * P:(b + 1) * P], ident[:],
+                    nc.tensor.matmul(summed[:, b, e, :], term[t, 0][:, e, b * P:(b + 1) * P], ident[:],
                                      start=(t, b, e) == (0, 0, 0), stop=(t, b, e) == (1, BLOCKS - 1, 1),
                                      is_transpose=True)
 
-        def lay_first_pair(s):
-            rounded = sb.tile([P, BLOCKS * P * 2], BF16, name="rounded%d" % s)
+        def lay_first_pair():
+            rounded = sb.tile([P, BLOCKS * P * 2], BF16, name="rounded")
             nc.scalar.activation(rounded[:].rearrange("n (b p e) -> n b p e", b=BLOCKS, e=2),
-                                 summed[s][:].rearrange("n b e p -> n b p e"), ACT.Copy)
-            back = ps.tile([P, HALF], F32, name="back%d" % s, tag="bank%d" % (TRANSIT_BANK + s))
+                                 summed[:].rearrange("n b e p -> n b p e"), ACT.Copy)
+            back = ps.tile([P, HALF], F32, name="back", tag="bank%d" % TRANSIT_BANK)
             for b in range(BLOCKS):
                 nc.tensor.transpose(back[:, b * P:(b + 1) * P], rounded[:].bitcast(F32)[:, b * P:(b + 1) * P],
                                     ident[:])
-            if s == 0:
-                nc.scalar.copy(apart[:].bitcast(F32)[:, 0:HALF], back[:])
-            else:
-                nc.scalar.copy(u_words[:, HALF:SLOTS, :], back[:].unsqueeze(2).to_broadcast([P, HALF, PAIRS]))
+            nc.scalar.copy(apart[:].bitcast(F32)[:, 0:HALF], back[:])
+
+        woven = [sb.tile([P, HALF, 2], F32, name="woven%d" % t, align_bytes=256) for t in range(2)]
+        for t in range(2):
+            nc.scalar.copy(woven[t][:], factors[0][:, first_factor(t):first_factor(t) + 2, HALF:SLOTS]
+                           .rearrange("p e n -> p n e"))
+        woven_term = {}
+
+        def woven_product(engine, t, tag):
+            woven_term[t] = sb.tile([P, HALF, 2], F32, name="woven_term%d" % t, tag=tag, align_bytes=256)
+            engine.tensor_tensor(woven_term[t][:], woven[t][:],
+                                 picked[t][1][:].unsqueeze(2).to_broadcast([P, HALF, 2]), ALU.mult)
 
         gather(0)
         product(nc.vector, 0, 0, HALF)
-        add_transposed(0, 0)
-        product(nc.gpsimd, 0, HALF, SLOTS, tag="picked0_0")
-        add_transposed(0, 1)
+        add_transposed(0)
+        woven_product(nc.gpsimd, 0, "picked0_0")
         gather(1, halves=(1, 0))
-        for s in (1, 0):
-            product(nc.vector, 1, s * HALF, (s + 1) * HALF)
-            add_transposed(1, s)
-        for s in (1, 0):
-            lay_first_pair(s)
+        woven_product(nc.vector, 1, "woven_term1")
+        nc.gpsimd.tensor_tensor(u_pairs[:, HALF:SLOTS, 0, :], woven_term[0][:], woven_term[1][:], ALU.add)
+        product(nc.vector, 1, 0, HALF, held[1, 0][:])
+        add_transposed(1)
+        lay_first_pair()
         gather(2, halves=(1, 0))
         product(nc.vector, 2, HALF, SLOTS, held[2, HALF][:])
         product(nc.gpsimd, 2, 0, HALF)

@@ -100,11 +100,10 @@ def tile_attend_pre_rotate_f_topk_kernel(tc, qT, kT, cT, wT, mg, offs, offs2, ou
 
         term = {}
 
-        def product(engine, t, lo, hi, source=None, tag=None):
+        def product(engine, t, lo, hi, source=None):
             s, first = divmod(lo, HALF)
             if (t, s) not in term:
-                term[t, s] = sb.tile([P, 2, HALF], F32, name="term%d_%d" % (t, s), tag=tag or "term%d_%d" % (t, s),
-                                     align_bytes=256)
+                term[t, s] = sb.tile([P, 2, HALF], F32, name="term%d_%d" % (t, s), align_bytes=256)
             if source is None:
                 source = factors[t // 2][:, first_factor(t):first_factor(t) + 2, lo:hi]
             cols = slice(first, first + hi - lo)
@@ -213,9 +212,9 @@ def tile_attend_pre_rotate_f_topk_kernel(tc, qT, kT, cT, wT, mg, offs, offs2, ou
         def quantize_u(lo, hi):
             nc.vector.quantize_mx(u_codes[:, lo:hi].bitcast(FP8X4), u_scales[:, lo:hi], u[:, lo * PACK:hi * PACK])
 
-        for j in (0, 2):
-            sum_second_pair(*GROUPS[j])
-            weave(*GROUPS[j])
+        for lo, hi in GROUPS[0::2]:
+            sum_second_pair(lo, hi)
+            weave(lo, hi)
         for m in range(q_tiles):
             nc.scalar.activation(neg_margin[m][:], margin[m][:], ACT.Copy, scale=-1.0)
         sum_second_pair(*GROUPS[1])

@@ -17,18 +17,13 @@ PACK = 4
 PAIRS = PACK // 2
 D, NQ, SLOTS, ENTITIES, RELATIONS = 512, 256, 512, 2048, 1024
 HALF = SLOTS // 2
-BLOCKS = HALF // P
+GROUPS = SLOTS // P
 PER_COLUMN = 16
 FLOPS = 2 * D * NQ * SLOTS
 BYTES = 4 * (D * ENTITIES + D * RELATIONS + D * NQ + NQ + NQ * SLOTS) + 2 * 2 * P * SLOTS // PER_COLUMN
 
-GROUPS = [(0, P), (2 * P, 3 * P), (P, 2 * P), (3 * P, 4 * P)]
 NEG_SIN, COS, SIN = 0, 1, 2
-HELD = [(2, HALF, SLOTS), (3, HALF, SLOTS), (3, 0, P), (1, 0, HALF)]
-HELD_BANKS = [4, 5, 6, 1]
-ACROSS_BANKS = [2, 3, 7]
-SUM_BANK, TRANSIT_BANK = 0, 2
-SCORE_BANKS = [[7, 4], [6, 5], [0, 1], [2, 3]]
+WOVEN = (1, 2)
 PIECES = [(1, 0, 128), (1, 128, 320), (1, 320, 512), (0, 0, 192), (0, 192, 384), (0, 384, 512)]
 TWICE_FLOOR = 2.0 ** -59
 
@@ -49,22 +44,22 @@ def tile_attend_pre_rotate_f_topk_kernel(tc, qT, kT, cT, wT, mg, offs, offs2, ou
         k_rows = kT.rearrange("(p t) n -> p t n", t=PACK)
         c_rows = cT.rearrange("(p t) n -> p t n", t=PACK)
         w_rows = wT.rearrange("(p t) n -> p t n", t=PACK)
-        q_rows = qT[0].rearrange("(p t) n -> p t n", t=PACK)
-        q_raw = [sb.tile([P, PACK, P], F32, name="q_raw%d" % m, align_bytes=256) for m in range(q_tiles)]
+        q_raw = sb.tile([P, PACK, NQ], F32, name="q_raw", tag="q_raw", align_bytes=256)
         margin = [sb.tile([P, 1], F32, name="margin%d" % m) for m in range(q_tiles)]
         neg_margin = [sb.tile([P, 1], F32, name="neg_margin%d" % m) for m in range(q_tiles)]
         floor = sb.tile([P, 1], F32, name="floor")
 
-        for h in reversed(range(PAIRS)):
-            nc.sync.dma_start(c_plane[h][:], c_rows[:, 2 * h, :])
-            if h == PAIRS - 1:
-                nc.sync.dma_start(rel_list[:], offs2)
-            nc.sync.dma_start(w_plane[h][:], w_rows[:, 2 * h, :])
+        nc.sync.dma_start(w_plane[1][:], w_rows[:, 2, :])
+        nc.sync.dma_start(rel_list[:], offs2)
+        nc.sync.dma_start(c_plane[0][:], c_rows[:, 0, :])
+        nc.sync.dma_start(w_plane[0][:], w_rows[:, 0, :])
         nc.sync.dma_start(ent_list[:], offs)
-        for t in range(PACK):
-            nc.sync.dma_start(k_plane[t][:], k_rows[:, t, :])
-        for m in range(q_tiles):
-            nc.sync.dma_start(q_raw[m][:], q_rows[:, :, m * P:(m + 1) * P])
+        nc.sync.dma_start(k_plane[0][:], k_rows[:, 0, :])
+        nc.sync.dma_start(k_plane[1][:], k_rows[:, 1, :])
+        nc.sync.dma_start(c_plane[1][:], c_rows[:, 2, :])
+        nc.sync.dma_start(k_plane[2][:], k_rows[:, 2, :])
+        nc.sync.dma_start(k_plane[3][:], k_rows[:, 3, :])
+        nc.sync.dma_start(q_raw[:], qT[0].rearrange("(p t) n -> p t n", t=PACK))
         for m in range(q_tiles):
             nc.sync.dma_start(margin[m][:], mg[0, m * P:(m + 1) * P, :])
 
@@ -77,173 +72,144 @@ def tile_attend_pre_rotate_f_topk_kernel(tc, qT, kT, cT, wT, mg, offs, offs2, ou
         ident = sb.tile([P, P], F32, name="ident")
         make_identity(nc, ident[:])
 
-        u = sb.tile([P, SLOTS * PACK], BF16, name="u", tag="u", align_bytes=256)
-        u_pairs = u[:].rearrange("p (n h e) -> p n h e", h=PAIRS, e=2)
-        u_words = u[:].bitcast(F32).rearrange("p (n h) -> p n h", h=PAIRS)
-        apart = sb.tile([P, PAIRS * HALF * 2], BF16, name="apart", align_bytes=256)
+        u = {j: sb.tile([P, P * PACK], BF16, name="u%d" % j, tag="u%d" % j, align_bytes=256)[:]
+             for j in range(GROUPS) if j not in WOVEN}
+        apart = {j: sb.tile([P, PAIRS, P * 2], BF16, name="apart%d" % j, align_bytes=256) for j in WOVEN}
         factors = [sb.tile([P, 3, SLOTS], F32, name="factors%d" % h, align_bytes=256) for h in range(PAIRS)]
-        picked = [[sb.tile([P, HALF], F32, name="picked%d_%d" % (t, s), tag="picked%d_%d" % (t, s), align_bytes=256)
-                   for s in range(2)] for t in range(PACK)]
 
-        for h in reversed(range(PAIRS)):
-            nc.vector.tensor_copy(factors[h][:, COS, :], c_plane[h][:].indirect(rel_list[:]))
-            nc.vector.tensor_copy(factors[h][:, SIN, :], w_plane[h][:].indirect(rel_list[:]))
-            nc.scalar.activation(factors[h][:, NEG_SIN, :], factors[h][:, SIN, :], ACT.Copy, scale=-1.0)
+        def vector_gather(target, window, entries):
+            nc.vector.tensor_copy(target, window.indirect(entries))
+
+        def scalar_gather(target, window, entries):
+            nc.scalar.activation(target, window.indirect(entries), ACT.Copy)
+
+        def entries(lo, hi):
+            return ent_list[:, lo // PER_COLUMN:hi // PER_COLUMN]
 
         def first_factor(t):
             return NEG_SIN if t % 2 else COS
 
-        def gather(t, halves=(0, 1)):
-            for s in halves:
-                entries = ent_list[:, s * HALF // PER_COLUMN:(s + 1) * HALF // PER_COLUMN]
-                nc.vector.tensor_copy(picked[t][s][:], k_plane[t][:].indirect(entries))
-
-        term = {}
-
-        def product(engine, t, lo, hi, source=None):
-            s, first = divmod(lo, HALF)
-            if (t, s) not in term:
-                term[t, s] = sb.tile([P, 2, HALF], F32, name="term%d_%d" % (t, s), align_bytes=256)
+        def product(engine, t, lo, hi, picked, source=None):
+            term = sb.tile([P, 2, hi - lo], F32, name="term%d_%d" % (t, lo), align_bytes=256)
             if source is None:
                 source = factors[t // 2][:, first_factor(t):first_factor(t) + 2, lo:hi]
-            cols = slice(first, first + hi - lo)
-            engine.tensor_tensor(term[t, s][:, :, cols], source,
-                                 picked[t][s][:, cols].unsqueeze(1).to_broadcast([P, 2, hi - lo]), ALU.mult)
+            engine.tensor_tensor(term[:], source, picked.unsqueeze(1).to_broadcast([P, 2, hi - lo]), ALU.mult)
+            return term
 
-        needed = []
-        for t, lo, hi in HELD:
-            for e in range(2):
-                for b in range(lo // P, hi // P):
-                    if (t // 2, first_factor(t) + e, b) not in needed:
-                        needed.append((t // 2, first_factor(t) + e, b))
-        flipped = {}
-        held = {}
-        for h in range(PAIRS):
-            for i in range(len(needed) // 4):
-                if needed[4 * i][0] != h:
-                    continue
-                across = ps.tile([P, 4, P], F32, name="across%d" % i, tag="bank%d" % ACROSS_BANKS[i])
-                landed = sb.tile([P, 4, P], F32, name="landed%d" % i)
-                for x, (pair, row, b) in enumerate(needed[4 * i:4 * i + 4]):
-                    nc.tensor.transpose(across[:, x, :], factors[pair][:, row, b * P:(b + 1) * P], ident[:])
-                    flipped[pair, row, b] = landed[:, x, :]
-                nc.scalar.copy(landed[:], across[:])
-            for i, (t, lo, hi) in enumerate(HELD):
-                if t // 2 != h:
-                    continue
-                held[t, lo] = ps.tile([P, 2, hi - lo], F32, name="held%d" % i, tag="bank%d" % HELD_BANKS[i])
-                for e in range(2):
-                    for b in range(lo // P, hi // P):
-                        nc.tensor.transpose(held[t, lo][:, e, b * P - lo:(b + 1) * P - lo],
-                                            flipped[h, first_factor(t) + e, b], ident[:])
-
-        summed = ps.tile([P, BLOCKS, 2, P], F32, name="summed", tag="bank%d" % SUM_BANK)
-
-        def add_transposed(t):
-            for b in range(BLOCKS):
-                for e in range(2):
-                    nc.tensor.matmul(summed[:, b, e, :], term[t, 0][:, e, b * P:(b + 1) * P], ident[:],
-                                     start=(t, b, e) == (0, 0, 0), stop=(t, b, e) == (1, BLOCKS - 1, 1),
-                                     is_transpose=True)
-
-        def lay_first_pair():
-            rounded = sb.tile([P, BLOCKS * P * 2], BF16, name="rounded")
-            nc.scalar.activation(rounded[:].rearrange("n (b p e) -> n b p e", b=BLOCKS, e=2),
-                                 summed[:].rearrange("n b e p -> n b p e"), ACT.Copy)
-            back = ps.tile([P, HALF], F32, name="back", tag="bank%d" % TRANSIT_BANK)
-            for b in range(BLOCKS):
-                nc.tensor.transpose(back[:, b * P:(b + 1) * P], rounded[:].bitcast(F32)[:, b * P:(b + 1) * P],
-                                    ident[:])
-            nc.scalar.copy(apart[:].bitcast(F32)[:, 0:HALF], back[:])
-
-        woven = [sb.tile([P, HALF, 2], F32, name="woven%d" % t, align_bytes=256) for t in range(2)]
-        for t in range(2):
-            nc.scalar.copy(woven[t][:], factors[0][:, first_factor(t):first_factor(t) + 2, HALF:SLOTS]
-                           .rearrange("p e n -> p n e"))
-        woven_term = {}
-
-        def woven_product(engine, t, tag):
-            woven_term[t] = sb.tile([P, HALF, 2], F32, name="woven_term%d" % t, tag=tag, align_bytes=256)
-            engine.tensor_tensor(woven_term[t][:], woven[t][:],
-                                 picked[t][1][:].unsqueeze(2).to_broadcast([P, HALF, 2]), ALU.mult)
-
-        gather(0)
-        product(nc.vector, 0, 0, HALF)
-        add_transposed(0)
-        woven_product(nc.gpsimd, 0, "picked0_0")
-        gather(1, halves=(1, 0))
-        woven_product(nc.vector, 1, "woven_term1")
-        nc.gpsimd.tensor_tensor(u_pairs[:, HALF:SLOTS, 0, :], woven_term[0][:], woven_term[1][:], ALU.add)
-        product(nc.vector, 1, 0, HALF, held[1, 0][:])
-        add_transposed(1)
-        lay_first_pair()
-        gather(2, halves=(1, 0))
-        product(nc.vector, 2, HALF, SLOTS, held[2, HALF][:])
-        product(nc.gpsimd, 2, 0, HALF)
-        gather(3)
-        product(nc.gpsimd, 3, P, HALF)
-        product(nc.vector, 3, 0, P, held[3, 0][:])
-        product(nc.vector, 3, HALF, SLOTS, held[3, HALF][:])
-
-        def sum_second_pair(lo, hi):
-            s, first = divmod(lo, HALF)
-            cols = slice(first, first + hi - lo)
-            if s == 0:
-                target = apart[:, 2 * (HALF + lo):2 * (HALF + hi)].rearrange("p (c i e) -> p c e i", i=2, e=2)
+        def pair_sum(h, j, first, second):
+            if j in WOVEN:
+                target = apart[j][:, h, :].rearrange("p (c i e) -> p c e i", i=2, e=2)
             else:
-                target = u_pairs[:, lo:hi, 1, :].rearrange("p (c i) e -> p c e i", i=2)
-            nc.vector.tensor_tensor(target, term[2, s][:, :, cols].rearrange("p e (c i) -> p c e i", i=2),
-                                    term[3, s][:, :, cols].rearrange("p e (c i) -> p c e i", i=2), ALU.add)
+                target = u[j].rearrange("p (c i h e) -> p h c e i", i=2, h=PAIRS, e=2)[:, h]
+            nc.vector.tensor_tensor(target, first.rearrange("p e (c i) -> p c e i", i=2),
+                                    second.rearrange("p e (c i) -> p c e i", i=2), ALU.add)
 
-        def weave(lo, hi):
-            nc.scalar.copy(u_words[:, lo:hi, :],
-                           apart[:].bitcast(F32).rearrange("p (h n) -> p n h", h=PAIRS)[:, lo:hi, :])
+        held = {j: ps.tile([P, 2, P], F32, name="held%d" % j, tag="bank%d" % j) for j in range(1, GROUPS)}
 
-        q_bf = sb.tile([P, NQ * PACK], BF16, name="q_bf", align_bytes=256)
+        def hold(e, row):
+            across = ps.tile([P, GROUPS - 1, P], F32, name="across%d" % e, tag="bank%d" % (4 + e))
+            landed = sb.tile([P, GROUPS - 1, P], F32, name="landed%d" % e)
+            for j in range(1, GROUPS):
+                nc.tensor.transpose(across[:, j - 1, :], factors[1][:, row, j * P:(j + 1) * P], ident[:])
+            nc.scalar.copy(landed[:], across[:])
+            for j in range(1, GROUPS):
+                nc.tensor.transpose(held[j][:, e, :], landed[:, j - 1, :], ident[:])
+
+        vector_gather(factors[1][:, SIN, :], w_plane[1][:], rel_list[:])
+        nc.scalar.activation(factors[1][:, NEG_SIN, :], factors[1][:, SIN, :], ACT.Copy, scale=-1.0)
+        hold(0, NEG_SIN)
+        vector_gather(factors[0][:, COS, :], c_plane[0][:], rel_list[:])
+        vector_gather(factors[0][:, SIN, :], w_plane[0][:], rel_list[:])
+        nc.scalar.activation(factors[0][:, NEG_SIN, :], factors[0][:, SIN, :], ACT.Copy, scale=-1.0)
+
+        def shared_gather(t):
+            halves = [sb.tile([P, HALF], F32, name="picked%d_%d" % (t, s), align_bytes=256) for s in range(2)]
+            scalar_gather(halves[0][:], k_plane[t][:], entries(0, HALF))
+            vector_gather(halves[1][:], k_plane[t][:], entries(HALF, SLOTS))
+            return [product(nc.vector, t, s * HALF, (s + 1) * HALF, halves[s][:]) for s in range(2)]
+
+        def group_of(terms, j):
+            s, first = divmod(j * P, HALF)
+            return terms[s][:, :, first:first + P]
+
+        terms0 = shared_gather(0)
+        terms1 = shared_gather(1)
+        scalar_gather(factors[1][:, COS, :], c_plane[1][:], rel_list[:])
+        hold(1, COS)
+        for j in range(GROUPS):
+            pair_sum(0, j, group_of(terms0, j), group_of(terms1, j))
+        terms2 = shared_gather(2)
+
+        picked = [sb.tile([P, P], F32, name="picked3_%d" % j, align_bytes=256) for j in range(GROUPS)]
+        vector_gather(picked[0][:], k_plane[3][:], entries(0, P))
+        for j in range(1, GROUPS):
+            scalar_gather(picked[j][:], k_plane[3][:], entries(j * P, (j + 1) * P))
+        terms3 = [product(nc.gpsimd, 3, 0, P, picked[0][:])]
+        for j in range(1, GROUPS):
+            terms3.append(product(nc.vector, 3, j * P, (j + 1) * P, picked[j][:], held[j][:]))
+
+        q_bf = [sb.tile([P, P * PACK], BF16, name="q_bf%d" % m, align_bytes=256) for m in range(q_tiles)]
         q_codes = sb.tile([P, NQ], U32, name="q_codes", align_bytes=256)
         q_scales = sb.tile([P, NQ], U8, name="q_scales", align_bytes=256)
         u_codes = sb.tile([P, SLOTS], U32, name="u_codes", tag="codes", align_bytes=256)
         u_scales = sb.tile([P, SLOTS], U8, name="u_scales", align_bytes=256)
         for m in range(q_tiles):
-            nc.scalar.activation(
-                q_bf[:, m * P * PACK:(m + 1) * P * PACK].rearrange("p (c i t) -> p c t i", i=4, t=PACK),
-                q_raw[m][:].rearrange("p t (c i) -> p c t i", i=4), ACT.Copy)
+            nc.scalar.activation(q_bf[m][:].rearrange("p (c i t) -> p c t i", i=4, t=PACK),
+                                 q_raw[:, :, m * P:(m + 1) * P].rearrange("p t (c i) -> p c t i", i=4), ACT.Copy)
 
-        def quantize_u(lo, hi):
-            nc.vector.quantize_mx(u_codes[:, lo:hi].bitcast(FP8X4), u_scales[:, lo:hi], u[:, lo * PACK:hi * PACK])
+        u_woven = sb.tile([P, len(WOVEN), P * PACK], BF16, name="u_woven", tag="q_raw", align_bytes=256)
+        for i, j in enumerate(WOVEN):
+            u[j] = u_woven[:, i, :]
 
-        for lo, hi in GROUPS[0::2]:
-            sum_second_pair(lo, hi)
-            weave(lo, hi)
+        def weave(j):
+            nc.scalar.copy(u[j].bitcast(F32).rearrange("p (n h) -> p n h", h=PAIRS),
+                           apart[j][:].rearrange("p h x -> p (h x)").bitcast(F32).rearrange("p (h n) -> p n h", h=PAIRS))
+
+        def quantize_u(j):
+            cols = slice(j * P, (j + 1) * P)
+            nc.vector.quantize_mx(u_codes[:, cols].bitcast(FP8X4), u_scales[:, cols], u[j])
+
+        def last_sum(j):
+            pair_sum(1, j, group_of(terms2, j), terms3[j][:])
+
+        def quantize_q(m):
+            nc.vector.quantize_mx(q_codes[:, m * P:(m + 1) * P].bitcast(FP8X4), q_scales[:, m * P:(m + 1) * P],
+                                  q_bf[m][:])
+
+        last_sum(1)
+        weave(1)
+        last_sum(0)
+        quantize_q(0)
+        quantize_u(0)
+        last_sum(2)
+        weave(2)
         for m in range(q_tiles):
             nc.scalar.activation(neg_margin[m][:], margin[m][:], ACT.Copy, scale=-1.0)
-        sum_second_pair(*GROUPS[1])
-        for m in range(q_tiles):
-            nc.vector.quantize_mx(q_codes[:, m * P:(m + 1) * P].bitcast(FP8X4), q_scales[:, m * P:(m + 1) * P],
-                                  q_bf[:, m * P * PACK:(m + 1) * P * PACK])
-        quantize_u(*GROUPS[0])
-        quantize_u(*GROUPS[1])
-        sum_second_pair(*GROUPS[3])
-        quantize_u(*GROUPS[2])
-        quantize_u(*GROUPS[3])
+        quantize_q(1)
+        quantize_u(1)
+        last_sum(3)
+        quantize_u(2)
+        quantize_u(3)
 
         sig = sb.tile([P, q_tiles, SLOTS], F32, name="sig", align_bytes=256)
         score = {}
-        for j, (lo, hi) in enumerate(GROUPS):
+        for j in range(GROUPS):
+            cols = slice(j * P, (j + 1) * P)
             for m in range(q_tiles):
                 rows = slice(m * P, (m + 1) * P)
-                score[j, m] = ps.tile([P, hi - lo], F32, name="score%d_%d" % (j, m), tag="bank%d" % SCORE_BANKS[j][m])
+                score[j, m] = ps.tile([P, P], F32, name="score%d_%d" % (j, m), tag="bank%d" % (2 * j + m))
                 nc.tensor.matmul_mx(score[j, m][:], lhsT=q_codes[:, rows].bitcast(FP8X4), lhsT_scale=q_scales[:, rows],
-                                    rhs=u_codes[:, lo:hi].bitcast(FP8X4), rhs_scale=u_scales[:, lo:hi],
+                                    rhs=u_codes[:, cols].bitcast(FP8X4), rhs_scale=u_scales[:, cols],
                                     start=True, stop=True)
-                nc.scalar.activation(sig[:, m, lo:hi], score[j, m][:], ACT.Sigmoid, bias=neg_margin[m][:])
+                nc.scalar.activation(sig[:, m, cols], score[j, m][:], ACT.Sigmoid, bias=neg_margin[m][:])
 
-        v = sb.tile([P, q_tiles, SLOTS], F32, name="v", tag="u", align_bytes=256)
+        v = sb.tile([P, q_tiles, SLOTS], F32, name="v", tag="u3", align_bytes=256)
         log_sig = sb.tile([P, q_tiles, SLOTS], F32, name="log_sig", tag="codes", align_bytes=256)
         result = sb.tile([P, q_tiles, SLOTS], F32, name="result", align_bytes=256)
         for m in reversed(range(q_tiles)):
-            for j, (lo, hi) in enumerate(GROUPS):
-                nc.vector.tensor_scalar(v[:, m, lo:hi], score[j, m][:], -1.0, margin[m][:], ALU.mult, ALU.add)
+            for j in range(GROUPS):
+                nc.vector.tensor_scalar(v[:, m, j * P:(j + 1) * P], score[j, m][:], -1.0, margin[m][:],
+                                        ALU.mult, ALU.add)
         for m, lo, hi in PIECES:
             nc.scalar.activation(log_sig[:, m, lo:hi], sig[:, m, lo:hi], ACT.Ln, bias=floor[:])
             nc.vector.scalar_tensor_tensor(result[:, m, lo:hi], log_sig[:, m, lo:hi], -1.0, v[:, m, lo:hi],

@@ -44,24 +44,27 @@ def tile_attend_pre_rotate_f_topk_kernel(tc, qT, kT, cT, wT, mg, offs, offs2, ou
         k_rows = kT.rearrange("(p t) n -> p t n", t=PACK)
         c_rows = cT.rearrange("(p t) n -> p t n", t=PACK)
         w_rows = wT.rearrange("(p t) n -> p t n", t=PACK)
-        q_raw = sb.tile([P, PACK, NQ], F32, name="q_raw", tag="q_raw", align_bytes=256)
-        margin = [sb.tile([P, 1], F32, name="margin%d" % m) for m in range(q_tiles)]
-        neg_margin = [sb.tile([P, 1], F32, name="neg_margin%d" % m) for m in range(q_tiles)]
+        q_raw = [sb.tile([P, PACK, P], F32, name="q_raw%d" % m, tag="q_raw%d" % m, align_bytes=256)
+                 for m in range(q_tiles)]
+        margin_row = sb.tile([P, NQ], F32, name="margin_row")
+        margin = sb.tile([P, q_tiles], F32, name="margin")
+        neg_margin = sb.tile([P, q_tiles], F32, name="neg_margin")
         floor = sb.tile([P, 1], F32, name="floor")
 
+        nc.gpsimd.memset(margin_row[:], 0.0)
         nc.sync.dma_start(w_plane[1][:], w_rows[:, 2, :])
         nc.sync.dma_start(rel_list[:], offs2)
         nc.sync.dma_start(c_plane[0][:], c_rows[:, 0, :])
         nc.sync.dma_start(w_plane[0][:], w_rows[:, 0, :])
         nc.sync.dma_start(ent_list[:], offs)
+        nc.sync.dma_start(margin_row[0:1, :], mg[0].rearrange("q o -> o q"))
         nc.sync.dma_start(k_plane[0][:], k_rows[:, 0, :])
         nc.sync.dma_start(k_plane[1][:], k_rows[:, 1, :])
         nc.sync.dma_start(c_plane[1][:], c_rows[:, 2, :])
         nc.sync.dma_start(k_plane[2][:], k_rows[:, 2, :])
         nc.sync.dma_start(k_plane[3][:], k_rows[:, 3, :])
-        nc.sync.dma_start(q_raw[:], qT[0].rearrange("(p t) n -> p t n", t=PACK))
         for m in range(q_tiles):
-            nc.sync.dma_start(margin[m][:], mg[0, m * P:(m + 1) * P, :])
+            nc.sync.dma_start(q_raw[m][:], qT[0].rearrange("(p t) n -> p t n", t=PACK)[:, :, m * P:(m + 1) * P])
 
         zero = sb.tile([P, 1], F32, name="zero")
         nc.gpsimd.memset(zero[:], 0.0)
@@ -71,6 +74,12 @@ def tile_attend_pre_rotate_f_topk_kernel(tc, qT, kT, cT, wT, mg, offs, offs2, ou
 
         ident = sb.tile([P, P], F32, name="ident")
         make_identity(nc, ident[:])
+
+        margin_turned = ps.tile([P, q_tiles, P], F32, name="margin_turned", tag="bank0")
+        for m in range(q_tiles):
+            nc.tensor.transpose(margin_turned[:, m, :], margin_row[:, m * P:(m + 1) * P], ident[:])
+        nc.scalar.copy(margin[:], margin_turned[:, :, 0])
+        nc.scalar.activation(neg_margin[:], margin_turned[:, :, 0], ACT.Copy, scale=-1.0)
 
         u = {j: sb.tile([P, P * PACK], BF16, name="u%d" % j, tag="u%d" % j, align_bytes=256)[:]
              for j in range(GROUPS) if j not in WOVEN}
@@ -111,7 +120,10 @@ def tile_attend_pre_rotate_f_topk_kernel(tc, qT, kT, cT, wT, mg, offs, offs2, ou
             landed = sb.tile([P, GROUPS - 1, P], F32, name="landed%d" % e)
             for j in range(1, GROUPS):
                 nc.tensor.transpose(across[:, j - 1, :], factors[1][:, row, j * P:(j + 1) * P], ident[:])
-            nc.scalar.copy(landed[:], across[:])
+            if row == COS:
+                nc.vector.tensor_copy(landed[:], across[:])
+            else:
+                nc.scalar.copy(landed[:], across[:])
             for j in range(1, GROUPS):
                 nc.tensor.transpose(held[j][:, e, :], landed[:, j - 1, :], ident[:])
 
@@ -135,18 +147,22 @@ def tile_attend_pre_rotate_f_topk_kernel(tc, qT, kT, cT, wT, mg, offs, offs2, ou
         terms0 = shared_gather(0)
         terms1 = shared_gather(1)
         scalar_gather(factors[1][:, COS, :], c_plane[1][:], rel_list[:])
-        hold(1, COS)
         for j in range(GROUPS):
             pair_sum(0, j, group_of(terms0, j), group_of(terms1, j))
-        terms2 = shared_gather(2)
+        hold(1, COS)
+        halves = [sb.tile([P, HALF], F32, name="picked2_%d" % s, align_bytes=256) for s in range(2)]
+        scalar_gather(halves[0][:], k_plane[2][:], entries(0, HALF))
+        scalar_gather(halves[1][:, :P], k_plane[2][:], entries(HALF, HALF + P))
+        vector_gather(halves[1][:, P:], k_plane[2][:], entries(HALF + P, SLOTS))
+        terms2 = [product(nc.vector, 2, s * HALF, (s + 1) * HALF, halves[s][:]) for s in range(2)]
 
         picked = [sb.tile([P, P], F32, name="picked3_%d" % j, align_bytes=256) for j in range(GROUPS)]
-        vector_gather(picked[0][:], k_plane[3][:], entries(0, P))
+        for j in range(GROUPS):
+            gather = scalar_gather if j else vector_gather
+            gather(picked[j][:], k_plane[3][:], entries(j * P, (j + 1) * P))
+        terms3 = {0: product(nc.gpsimd, 3, 0, P, picked[0][:])}
         for j in range(1, GROUPS):
-            scalar_gather(picked[j][:], k_plane[3][:], entries(j * P, (j + 1) * P))
-        terms3 = [product(nc.gpsimd, 3, 0, P, picked[0][:])]
-        for j in range(1, GROUPS):
-            terms3.append(product(nc.vector, 3, j * P, (j + 1) * P, picked[j][:], held[j][:]))
+            terms3[j] = product(nc.vector, 3, j * P, (j + 1) * P, picked[j][:], held[j][:])
 
         q_bf = [sb.tile([P, P * PACK], BF16, name="q_bf%d" % m, align_bytes=256) for m in range(q_tiles)]
         q_codes = sb.tile([P, NQ], U32, name="q_codes", align_bytes=256)
@@ -155,9 +171,9 @@ def tile_attend_pre_rotate_f_topk_kernel(tc, qT, kT, cT, wT, mg, offs, offs2, ou
         u_scales = sb.tile([P, SLOTS], U8, name="u_scales", align_bytes=256)
         for m in range(q_tiles):
             nc.scalar.activation(q_bf[m][:].rearrange("p (c i t) -> p c t i", i=4, t=PACK),
-                                 q_raw[:, :, m * P:(m + 1) * P].rearrange("p t (c i) -> p c t i", i=4), ACT.Copy)
+                                 q_raw[m][:].rearrange("p t (c i) -> p c t i", i=4), ACT.Copy)
 
-        u_woven = sb.tile([P, len(WOVEN), P * PACK], BF16, name="u_woven", tag="q_raw", align_bytes=256)
+        u_woven = sb.tile([P, len(WOVEN), P * PACK], BF16, name="u_woven", tag="q_raw1", align_bytes=256)
         for i, j in enumerate(WOVEN):
             u[j] = u_woven[:, i, :]
 
@@ -183,8 +199,6 @@ def tile_attend_pre_rotate_f_topk_kernel(tc, qT, kT, cT, wT, mg, offs, offs2, ou
         quantize_u(0)
         last_sum(2)
         weave(2)
-        for m in range(q_tiles):
-            nc.scalar.activation(neg_margin[m][:], margin[m][:], ACT.Copy, scale=-1.0)
         quantize_q(1)
         quantize_u(1)
         last_sum(3)
@@ -201,14 +215,14 @@ def tile_attend_pre_rotate_f_topk_kernel(tc, qT, kT, cT, wT, mg, offs, offs2, ou
                 nc.tensor.matmul_mx(score[j, m][:], lhsT=q_codes[:, rows].bitcast(FP8X4), lhsT_scale=q_scales[:, rows],
                                     rhs=u_codes[:, cols].bitcast(FP8X4), rhs_scale=u_scales[:, cols],
                                     start=True, stop=True)
-                nc.scalar.activation(sig[:, m, cols], score[j, m][:], ACT.Sigmoid, bias=neg_margin[m][:])
+                nc.scalar.activation(sig[:, m, cols], score[j, m][:], ACT.Sigmoid, bias=neg_margin[:, m:m + 1])
 
         v = sb.tile([P, q_tiles, SLOTS], F32, name="v", tag="u3", align_bytes=256)
         log_sig = sb.tile([P, q_tiles, SLOTS], F32, name="log_sig", tag="codes", align_bytes=256)
         result = sb.tile([P, q_tiles, SLOTS], F32, name="result", align_bytes=256)
         for m in reversed(range(q_tiles)):
             for j in range(GROUPS):
-                nc.vector.tensor_scalar(v[:, m, j * P:(j + 1) * P], score[j, m][:], -1.0, margin[m][:],
+                nc.vector.tensor_scalar(v[:, m, j * P:(j + 1) * P], score[j, m][:], -1.0, margin[:, m:m + 1],
                                         ALU.mult, ALU.add)
         for m, lo, hi in PIECES:
             nc.scalar.activation(log_sig[:, m, lo:hi], sig[:, m, lo:hi], ACT.Ln, bias=floor[:])

@@ -23,7 +23,7 @@ FLOPS = 2 * D * NQ * SLOTS
 BYTES = 4 * (D * ENTITIES + D * RELATIONS + D * NQ + NQ + NQ * SLOTS) + 2 * 2 * P * SLOTS // PER_COLUMN
 
 NEG_SIN, COS, SIN = 0, 1, 2
-WOVEN = (1, 2)
+FINISH = (0, 2, 3, 1)
 PIECES = [(1, 0, 128), (1, 128, 320), (1, 320, 512), (0, 0, 192), (0, 192, 384), (0, 384, 512)]
 TWICE_FLOOR = 2.0 ** -59
 
@@ -81,9 +81,7 @@ def tile_attend_pre_rotate_f_topk_kernel(tc, qT, kT, cT, wT, mg, offs, offs2, ou
         nc.scalar.copy(margin[:], margin_turned[:, :, 0])
         nc.scalar.activation(neg_margin[:], margin_turned[:, :, 0], ACT.Copy, scale=-1.0)
 
-        u = {j: sb.tile([P, P * PACK], BF16, name="u%d" % j, tag="u%d" % j, align_bytes=256)[:]
-             for j in range(GROUPS) if j not in WOVEN}
-        apart = {j: sb.tile([P, PAIRS, P * 2], BF16, name="apart%d" % j, align_bytes=256) for j in WOVEN}
+        apart = sb.tile([P, PAIRS, HALF * 2], BF16, name="apart", align_bytes=256)
         factors = [sb.tile([P, 3, SLOTS], F32, name="factors%d" % h, align_bytes=256) for h in range(PAIRS)]
 
         def vector_gather(target, window, entries):
@@ -99,19 +97,19 @@ def tile_attend_pre_rotate_f_topk_kernel(tc, qT, kT, cT, wT, mg, offs, offs2, ou
             return NEG_SIN if t % 2 else COS
 
         def product(engine, t, lo, hi, picked, source=None):
-            term = sb.tile([P, 2, hi - lo], F32, name="term%d_%d" % (t, lo), align_bytes=256)
+            term = sb.tile([P, 2, hi - lo], F32, name="term%d_%d" % (t, lo), tag="term%d_%d" % (t, lo), align_bytes=256)
             if source is None:
                 source = factors[t // 2][:, first_factor(t):first_factor(t) + 2, lo:hi]
             engine.tensor_tensor(term[:], source, picked.unsqueeze(1).to_broadcast([P, 2, hi - lo]), ALU.mult)
             return term
 
-        def pair_sum(h, j, first, second):
-            if j in WOVEN:
-                target = apart[j][:, h, :].rearrange("p (c i e) -> p c e i", i=2, e=2)
+        def pair_sum(engine, h, lo, hi, first, second):
+            if lo >= HALF:
+                target = apart[:, h, 2 * (lo - HALF):2 * (hi - HALF)].rearrange("p (c i e) -> p c e i", i=2, e=2)
             else:
-                target = u[j].rearrange("p (c i h e) -> p h c e i", i=2, h=PAIRS, e=2)[:, h]
-            nc.vector.tensor_tensor(target, first.rearrange("p e (c i) -> p c e i", i=2),
-                                    second.rearrange("p e (c i) -> p c e i", i=2), ALU.add)
+                target = u_direct[:, lo * PACK:hi * PACK].rearrange("p (c i h e) -> p h c e i", i=2, h=PAIRS, e=2)[:, h]
+            engine.tensor_tensor(target, first.rearrange("p e (c i) -> p c e i", i=2),
+                                 second.rearrange("p e (c i) -> p c e i", i=2), ALU.add)
 
         held = {j: ps.tile([P, 2, P], F32, name="held%d" % j, tag="bank%d" % j) for j in range(1, GROUPS)}
 
@@ -120,10 +118,7 @@ def tile_attend_pre_rotate_f_topk_kernel(tc, qT, kT, cT, wT, mg, offs, offs2, ou
             landed = sb.tile([P, GROUPS - 1, P], F32, name="landed%d" % e)
             for j in range(1, GROUPS):
                 nc.tensor.transpose(across[:, j - 1, :], factors[1][:, row, j * P:(j + 1) * P], ident[:])
-            if row == COS:
-                nc.vector.tensor_copy(landed[:], across[:])
-            else:
-                nc.scalar.copy(landed[:], across[:])
+            nc.scalar.copy(landed[:], across[:])
             for j in range(1, GROUPS):
                 nc.tensor.transpose(held[j][:, e, :], landed[:, j - 1, :], ident[:])
 
@@ -138,7 +133,8 @@ def tile_attend_pre_rotate_f_topk_kernel(tc, qT, kT, cT, wT, mg, offs, offs2, ou
             halves = [sb.tile([P, HALF], F32, name="picked%d_%d" % (t, s), align_bytes=256) for s in range(2)]
             scalar_gather(halves[0][:], k_plane[t][:], entries(0, HALF))
             vector_gather(halves[1][:], k_plane[t][:], entries(HALF, SLOTS))
-            return [product(nc.vector, t, s * HALF, (s + 1) * HALF, halves[s][:]) for s in range(2)]
+            order = (1, 0) if t == 2 else (0, 1)
+            return {s: product(nc.vector, t, s * HALF, (s + 1) * HALF, halves[s][:]) for s in order}
 
         def group_of(terms, j):
             s, first = divmod(j * P, HALF)
@@ -146,22 +142,20 @@ def tile_attend_pre_rotate_f_topk_kernel(tc, qT, kT, cT, wT, mg, offs, offs2, ou
 
         terms0 = shared_gather(0)
         terms1 = shared_gather(1)
-        scalar_gather(factors[1][:, COS, :], c_plane[1][:], rel_list[:])
-        for j in range(GROUPS):
-            pair_sum(0, j, group_of(terms0, j), group_of(terms1, j))
+        scalar_gather(factors[1][:, COS, P:], c_plane[1][:], rel_list[:, P // PER_COLUMN:])
+        pair_sum(nc.vector, 0, HALF, SLOTS, terms0[1][:], terms1[1][:])
+        u_direct = sb.tile([P, HALF * PACK], BF16, name="u_direct", tag="term1_%d" % HALF, align_bytes=256)
+        pair_sum(nc.gpsimd, 0, 0, HALF, terms0[0][:], terms1[0][:])
+        vector_gather(factors[1][:, COS, :P], c_plane[1][:], rel_list[:, :P // PER_COLUMN])
         hold(1, COS)
-        halves = [sb.tile([P, HALF], F32, name="picked2_%d" % s, align_bytes=256) for s in range(2)]
-        scalar_gather(halves[0][:], k_plane[2][:], entries(0, HALF))
-        scalar_gather(halves[1][:, :P], k_plane[2][:], entries(HALF, HALF + P))
-        vector_gather(halves[1][:, P:], k_plane[2][:], entries(HALF + P, SLOTS))
-        terms2 = [product(nc.vector, 2, s * HALF, (s + 1) * HALF, halves[s][:]) for s in range(2)]
+        terms2 = shared_gather(2)
 
         picked = [sb.tile([P, P], F32, name="picked3_%d" % j, align_bytes=256) for j in range(GROUPS)]
         for j in range(GROUPS):
-            gather = scalar_gather if j else vector_gather
+            gather = vector_gather if j < 2 else scalar_gather
             gather(picked[j][:], k_plane[3][:], entries(j * P, (j + 1) * P))
         terms3 = {0: product(nc.gpsimd, 3, 0, P, picked[0][:])}
-        for j in range(1, GROUPS):
+        for j in (2, 1, 3):
             terms3[j] = product(nc.vector, 3, j * P, (j + 1) * P, picked[j][:], held[j][:])
 
         q_bf = [sb.tile([P, P * PACK], BF16, name="q_bf%d" % m, align_bytes=256) for m in range(q_tiles)]
@@ -173,55 +167,55 @@ def tile_attend_pre_rotate_f_topk_kernel(tc, qT, kT, cT, wT, mg, offs, offs2, ou
             nc.scalar.activation(q_bf[m][:].rearrange("p (c i t) -> p c t i", i=4, t=PACK),
                                  q_raw[m][:].rearrange("p t (c i) -> p c t i", i=4), ACT.Copy)
 
-        u_woven = sb.tile([P, len(WOVEN), P * PACK], BF16, name="u_woven", tag="q_raw1", align_bytes=256)
-        for i, j in enumerate(WOVEN):
-            u[j] = u_woven[:, i, :]
+        u_woven = sb.tile([P, HALF * PACK], BF16, name="u_woven", tag="q_raw1", align_bytes=256)
+        u = [half[:, i * P * PACK:(i + 1) * P * PACK] for half in (u_direct, u_woven) for i in range(2)]
 
         def weave(j):
+            words = apart[:].rearrange("p h x -> p (h x)").bitcast(F32).rearrange("p (h n) -> p n h", h=PAIRS)
             nc.scalar.copy(u[j].bitcast(F32).rearrange("p (n h) -> p n h", h=PAIRS),
-                           apart[j][:].rearrange("p h x -> p (h x)").bitcast(F32).rearrange("p (h n) -> p n h", h=PAIRS))
+                           words[:, j * P - HALF:(j + 1) * P - HALF, :])
 
         def quantize_u(j):
             cols = slice(j * P, (j + 1) * P)
             nc.vector.quantize_mx(u_codes[:, cols].bitcast(FP8X4), u_scales[:, cols], u[j])
 
         def last_sum(j):
-            pair_sum(1, j, group_of(terms2, j), terms3[j][:])
+            pair_sum(nc.vector, 1, j * P, (j + 1) * P, group_of(terms2, j), terms3[j][:])
 
         def quantize_q(m):
             nc.vector.quantize_mx(q_codes[:, m * P:(m + 1) * P].bitcast(FP8X4), q_scales[:, m * P:(m + 1) * P],
                                   q_bf[m][:])
 
-        last_sum(1)
-        weave(1)
+        last_sum(2)
+        weave(2)
         last_sum(0)
         quantize_q(0)
         quantize_u(0)
-        last_sum(2)
-        weave(2)
-        quantize_q(1)
-        quantize_u(1)
         last_sum(3)
+        weave(3)
+        quantize_q(1)
         quantize_u(2)
+        last_sum(1)
         quantize_u(3)
+        quantize_u(1)
 
         sig = sb.tile([P, q_tiles, SLOTS], F32, name="sig", align_bytes=256)
         score = {}
-        for j in range(GROUPS):
+        for i, j in enumerate(FINISH):
             cols = slice(j * P, (j + 1) * P)
             for m in range(q_tiles):
                 rows = slice(m * P, (m + 1) * P)
-                score[j, m] = ps.tile([P, P], F32, name="score%d_%d" % (j, m), tag="bank%d" % (2 * j + m))
+                score[j, m] = ps.tile([P, P], F32, name="score%d_%d" % (j, m), tag="bank%d" % (2 * i + m))
                 nc.tensor.matmul_mx(score[j, m][:], lhsT=q_codes[:, rows].bitcast(FP8X4), lhsT_scale=q_scales[:, rows],
                                     rhs=u_codes[:, cols].bitcast(FP8X4), rhs_scale=u_scales[:, cols],
                                     start=True, stop=True)
                 nc.scalar.activation(sig[:, m, cols], score[j, m][:], ACT.Sigmoid, bias=neg_margin[:, m:m + 1])
 
-        v = sb.tile([P, q_tiles, SLOTS], F32, name="v", tag="u3", align_bytes=256)
+        v = sb.tile([P, q_tiles, SLOTS], F32, name="v", tag="term1_%d" % HALF, align_bytes=256)
         log_sig = sb.tile([P, q_tiles, SLOTS], F32, name="log_sig", tag="codes", align_bytes=256)
         result = sb.tile([P, q_tiles, SLOTS], F32, name="result", align_bytes=256)
         for m in reversed(range(q_tiles)):
-            for j in range(GROUPS):
+            for j in FINISH:
                 nc.vector.tensor_scalar(v[:, m, j * P:(j + 1) * P], score[j, m][:], -1.0, margin[:, m:m + 1],
                                         ALU.mult, ALU.add)
         for m, lo, hi in PIECES:

@@ -107,7 +107,7 @@ def tile_attend_pre_rotate_f_topk_kernel(tc, qT, kT, cT, wT, mg, offs, offs2, ou
             if lo >= HALF:
                 target = apart[:, h, 2 * (lo - HALF):2 * (hi - HALF)].rearrange("p (c i e) -> p c e i", i=2, e=2)
             else:
-                target = u_direct[:, lo * PACK:hi * PACK].rearrange("p (c i h e) -> p h c e i", i=2, h=PAIRS, e=2)[:, h]
+                target = u_direct[lo // P][:].rearrange("p (c i h e) -> p h c e i", i=2, h=PAIRS, e=2)[:, h]
             engine.tensor_tensor(target, first.rearrange("p e (c i) -> p c e i", i=2),
                                  second.rearrange("p e (c i) -> p c e i", i=2), ALU.add)
 
@@ -126,7 +126,7 @@ def tile_attend_pre_rotate_f_topk_kernel(tc, qT, kT, cT, wT, mg, offs, offs2, ou
         nc.scalar.activation(factors[1][:, NEG_SIN, :], factors[1][:, SIN, :], ACT.Copy, scale=-1.0)
         hold(0, NEG_SIN)
         vector_gather(factors[0][:, COS, :], c_plane[0][:], rel_list[:])
-        vector_gather(factors[0][:, SIN, :], w_plane[0][:], rel_list[:])
+        scalar_gather(factors[0][:, SIN, :], w_plane[0][:], rel_list[:])
         nc.scalar.activation(factors[0][:, NEG_SIN, :], factors[0][:, SIN, :], ACT.Copy, scale=-1.0)
 
         def shared_gather(t):
@@ -143,19 +143,21 @@ def tile_attend_pre_rotate_f_topk_kernel(tc, qT, kT, cT, wT, mg, offs, offs2, ou
         terms0 = shared_gather(0)
         terms1 = shared_gather(1)
         scalar_gather(factors[1][:, COS, P:], c_plane[1][:], rel_list[:, P // PER_COLUMN:])
+        u_direct = {1: sb.tile([P, P * PACK], BF16, name="u1", tag="u1", align_bytes=256)}
+        pair_sum(nc.vector, 0, P, HALF, terms0[0][:, :, P:], terms1[0][:, :, P:])
         pair_sum(nc.vector, 0, HALF, SLOTS, terms0[1][:], terms1[1][:])
-        u_direct = sb.tile([P, HALF * PACK], BF16, name="u_direct", tag="term1_%d" % HALF, align_bytes=256)
-        pair_sum(nc.gpsimd, 0, 0, HALF, terms0[0][:], terms1[0][:])
+        u_direct[0] = sb.tile([P, P * PACK], BF16, name="u0", tag="term1_%d" % HALF, align_bytes=256)
+        pair_sum(nc.gpsimd, 0, 0, P, terms0[0][:, :, :P], terms1[0][:, :, :P])
         vector_gather(factors[1][:, COS, :P], c_plane[1][:], rel_list[:, :P // PER_COLUMN])
         hold(1, COS)
         terms2 = shared_gather(2)
 
         picked = [sb.tile([P, P], F32, name="picked3_%d" % j, align_bytes=256) for j in range(GROUPS)]
-        for j in range(GROUPS):
-            gather = vector_gather if j < 2 else scalar_gather
+        for j in (0, 2, 3, 1):
+            gather = scalar_gather if j else vector_gather
             gather(picked[j][:], k_plane[3][:], entries(j * P, (j + 1) * P))
         terms3 = {0: product(nc.gpsimd, 3, 0, P, picked[0][:])}
-        for j in (2, 1, 3):
+        for j in (2, 3, 1):
             terms3[j] = product(nc.vector, 3, j * P, (j + 1) * P, picked[j][:], held[j][:])
 
         q_bf = [sb.tile([P, P * PACK], BF16, name="q_bf%d" % m, align_bytes=256) for m in range(q_tiles)]
@@ -168,7 +170,7 @@ def tile_attend_pre_rotate_f_topk_kernel(tc, qT, kT, cT, wT, mg, offs, offs2, ou
                                  q_raw[m][:].rearrange("p t (c i) -> p c t i", i=4), ACT.Copy)
 
         u_woven = sb.tile([P, HALF * PACK], BF16, name="u_woven", tag="q_raw1", align_bytes=256)
-        u = [half[:, i * P * PACK:(i + 1) * P * PACK] for half in (u_direct, u_woven) for i in range(2)]
+        u = [u_direct[0][:], u_direct[1][:], u_woven[:, :P * PACK], u_woven[:, P * PACK:]]
 
         def weave(j):
             words = apart[:].rearrange("p h x -> p (h x)").bitcast(F32).rearrange("p (h n) -> p n h", h=PAIRS)
@@ -211,7 +213,7 @@ def tile_attend_pre_rotate_f_topk_kernel(tc, qT, kT, cT, wT, mg, offs, offs2, ou
                                     start=True, stop=True)
                 nc.scalar.activation(sig[:, m, cols], score[j, m][:], ACT.Sigmoid, bias=neg_margin[:, m:m + 1])
 
-        v = sb.tile([P, q_tiles, SLOTS], F32, name="v", tag="term1_%d" % HALF, align_bytes=256)
+        v = sb.tile([P, q_tiles, SLOTS], F32, name="v", tag="u1", align_bytes=256)
         log_sig = sb.tile([P, q_tiles, SLOTS], F32, name="log_sig", tag="codes", align_bytes=256)
         result = sb.tile([P, q_tiles, SLOTS], F32, name="result", align_bytes=256)
         for m in reversed(range(q_tiles)):

@@ -52,12 +52,12 @@ def tile_attend_pre_rotate_f_topk_kernel(tc, qT, kT, cT, wT, mg, offs, offs2, ou
         floor = sb.tile([P, 1], F32, name="floor")
 
         nc.gpsimd.memset(margin_row[:], 0.0)
+        nc.scalar.dma_start(margin_row[0:1, :], mg[0].rearrange("q o -> o q"))
         nc.sync.dma_start(w_plane[1][:], w_rows[:, 2, :])
         nc.sync.dma_start(rel_list[:], offs2)
         nc.sync.dma_start(c_plane[0][:], c_rows[:, 0, :])
         nc.sync.dma_start(w_plane[0][:], w_rows[:, 0, :])
         nc.sync.dma_start(ent_list[:], offs)
-        nc.sync.dma_start(margin_row[0:1, :], mg[0].rearrange("q o -> o q"))
         nc.sync.dma_start(k_plane[0][:], k_rows[:, 0, :])
         nc.sync.dma_start(k_plane[1][:], k_rows[:, 1, :])
         nc.sync.dma_start(c_plane[1][:], c_rows[:, 2, :])
@@ -133,8 +133,7 @@ def tile_attend_pre_rotate_f_topk_kernel(tc, qT, kT, cT, wT, mg, offs, offs2, ou
             halves = [sb.tile([P, HALF], F32, name="picked%d_%d" % (t, s), align_bytes=256) for s in range(2)]
             scalar_gather(halves[0][:], k_plane[t][:], entries(0, HALF))
             vector_gather(halves[1][:], k_plane[t][:], entries(HALF, SLOTS))
-            order = (1, 0) if t == 2 else (0, 1)
-            return {s: product(nc.vector, t, s * HALF, (s + 1) * HALF, halves[s][:]) for s in order}
+            return {s: product(nc.vector, t, s * HALF, (s + 1) * HALF, halves[s][:]) for s in (1, 0)}
 
         def group_of(terms, j):
             s, first = divmod(j * P, HALF)
@@ -143,21 +142,25 @@ def tile_attend_pre_rotate_f_topk_kernel(tc, qT, kT, cT, wT, mg, offs, offs2, ou
         terms0 = shared_gather(0)
         terms1 = shared_gather(1)
         scalar_gather(factors[1][:, COS, P:], c_plane[1][:], rel_list[:, P // PER_COLUMN:])
+        scalar_gather(factors[1][:, COS, :P], c_plane[1][:], rel_list[:, :P // PER_COLUMN])
         u_direct = {1: sb.tile([P, P * PACK], BF16, name="u1", tag="u1", align_bytes=256)}
         pair_sum(nc.vector, 0, P, HALF, terms0[0][:, :, P:], terms1[0][:, :, P:])
         pair_sum(nc.vector, 0, HALF, SLOTS, terms0[1][:], terms1[1][:])
         u_direct[0] = sb.tile([P, P * PACK], BF16, name="u0", tag="term1_%d" % HALF, align_bytes=256)
         pair_sum(nc.gpsimd, 0, 0, P, terms0[0][:, :, :P], terms1[0][:, :, :P])
-        vector_gather(factors[1][:, COS, :P], c_plane[1][:], rel_list[:, :P // PER_COLUMN])
         hold(1, COS)
-        terms2 = shared_gather(2)
+        halves = [sb.tile([P, HALF], F32, name="picked2_%d" % s, align_bytes=256) for s in range(2)]
+        vector_gather(halves[1][:], k_plane[2][:], entries(HALF, SLOTS))
+        vector_gather(halves[0][:, P:], k_plane[2][:], entries(P, HALF))
+        scalar_gather(halves[0][:, :P], k_plane[2][:], entries(0, P))
+        terms2 = {s: product(nc.vector, 2, s * HALF, (s + 1) * HALF, halves[s][:]) for s in (1, 0)}
 
         picked = [sb.tile([P, P], F32, name="picked3_%d" % j, align_bytes=256) for j in range(GROUPS)]
-        for j in (0, 2, 3, 1):
-            gather = scalar_gather if j else vector_gather
+        for j in range(GROUPS):
+            gather = vector_gather if j < 2 else scalar_gather
             gather(picked[j][:], k_plane[3][:], entries(j * P, (j + 1) * P))
         terms3 = {0: product(nc.gpsimd, 3, 0, P, picked[0][:])}
-        for j in (2, 3, 1):
+        for j in (2, 1, 3):
             terms3[j] = product(nc.vector, 3, j * P, (j + 1) * P, picked[j][:], held[j][:])
 
         q_bf = [sb.tile([P, P * PACK], BF16, name="q_bf%d" % m, align_bytes=256) for m in range(q_tiles)]

@@ -24,6 +24,8 @@ BYTES = 4 * (D * ENTITIES + D * RELATIONS + D * NQ + NQ + NQ * SLOTS) + 2 * 2 * 
 
 NEG_SIN, COS, SIN = 0, 1, 2
 FINISH = (0, 2, 3, 1)
+WOVEN = (2, 3)
+SCORE_BANKS = [(0, 4), (5, 6), (7, 2), (3, 1)]
 PIECES = [(1, 0, 128), (1, 128, 320), (1, 320, 512), (0, 0, 192), (0, 192, 384), (0, 384, 512)]
 TWICE_FLOOR = 2.0 ** -59
 
@@ -34,6 +36,7 @@ def tile_attend_pre_rotate_f_topk_kernel(tc, qT, kT, cT, wT, mg, offs, offs2, ou
 
     with ExitStack() as ctx:
         sb = ctx.enter_context(tc.tile_pool(name="sb", bufs=1))
+        late = ctx.enter_context(tc.tile_pool(name="late", bufs=1))
         ps = ctx.enter_context(tc.psum_pool(name="ps", bufs=1))
 
         ent_list = sb.tile([P, SLOTS // PER_COLUMN], U16, name="ent_list")
@@ -44,8 +47,8 @@ def tile_attend_pre_rotate_f_topk_kernel(tc, qT, kT, cT, wT, mg, offs, offs2, ou
         k_rows = kT.rearrange("(p t) n -> p t n", t=PACK)
         c_rows = cT.rearrange("(p t) n -> p t n", t=PACK)
         w_rows = wT.rearrange("(p t) n -> p t n", t=PACK)
-        q_raw = [sb.tile([P, PACK, P], F32, name="q_raw%d" % m, tag="q_raw%d" % m, align_bytes=256)
-                 for m in range(q_tiles)]
+        q_raw = [sb.tile([P, PACK, P], F32, name="q_raw0", align_bytes=256),
+                 late.tile([P, PACK, P], F32, name="q_raw1", align_bytes=256, offset=0)]
         margin_row = sb.tile([P, NQ], F32, name="margin_row")
         margin = sb.tile([P, q_tiles], F32, name="margin")
         neg_margin = sb.tile([P, q_tiles], F32, name="neg_margin")
@@ -103,11 +106,13 @@ def tile_attend_pre_rotate_f_topk_kernel(tc, qT, kT, cT, wT, mg, offs, offs2, ou
             engine.tensor_tensor(term[:], source, picked.unsqueeze(1).to_broadcast([P, 2, hi - lo]), ALU.mult)
             return term
 
-        def pair_sum(engine, h, lo, hi, first, second):
-            if lo >= HALF:
-                target = apart[:, h, 2 * (lo - HALF):2 * (hi - HALF)].rearrange("p (c i e) -> p c e i", i=2, e=2)
-            else:
-                target = u_direct[lo // P][:].rearrange("p (c i h e) -> p h c e i", i=2, h=PAIRS, e=2)[:, h]
+        def whole_lines(h, words):
+            return words[:, h, :].rearrange("p (c i e) -> p c e i", i=2, e=2)
+
+        def in_place(h, slots):
+            return slots.rearrange("p (c i h e) -> p h c e i", i=2, h=PAIRS, e=2)[:, h]
+
+        def pair_sum(engine, target, first, second):
             engine.tensor_tensor(target, first.rearrange("p e (c i) -> p c e i", i=2),
                                  second.rearrange("p e (c i) -> p c e i", i=2), ALU.add)
 
@@ -143,11 +148,12 @@ def tile_attend_pre_rotate_f_topk_kernel(tc, qT, kT, cT, wT, mg, offs, offs2, ou
         terms1 = shared_gather(1)
         scalar_gather(factors[1][:, COS, P:], c_plane[1][:], rel_list[:, P // PER_COLUMN:])
         scalar_gather(factors[1][:, COS, :P], c_plane[1][:], rel_list[:, :P // PER_COLUMN])
-        u_direct = {1: sb.tile([P, P * PACK], BF16, name="u1", tag="u1", align_bytes=256)}
-        pair_sum(nc.vector, 0, P, HALF, terms0[0][:, :, P:], terms1[0][:, :, P:])
-        pair_sum(nc.vector, 0, HALF, SLOTS, terms0[1][:], terms1[1][:])
-        u_direct[0] = sb.tile([P, P * PACK], BF16, name="u0", tag="term1_%d" % HALF, align_bytes=256)
-        pair_sum(nc.gpsimd, 0, 0, P, terms0[0][:, :, :P], terms1[0][:, :, :P])
+        u_last = sb.tile([P, P * PACK], BF16, name="u_last", tag="u_last", align_bytes=256)
+        pair_sum(nc.vector, in_place(0, u_last[:]), terms0[0][:, :, P:], terms1[0][:, :, P:])
+        pair_sum(nc.vector, whole_lines(0, apart), terms0[1][:], terms1[1][:])
+        u_first = sb.tile([P, P * PACK], BF16, name="u_first", tag="term1_%d" % HALF, align_bytes=256)
+        pair_sum(nc.gpsimd, in_place(0, u_first[:]), terms0[0][:, :, :P], terms1[0][:, :, :P])
+        words = {2: apart[:, :, :2 * P], 3: apart[:, :, 2 * P:]}
         hold(1, COS)
         halves = [sb.tile([P, HALF], F32, name="picked2_%d" % s, align_bytes=256) for s in range(2)]
         vector_gather(halves[1][:], k_plane[2][:], entries(HALF, SLOTS))
@@ -155,12 +161,12 @@ def tile_attend_pre_rotate_f_topk_kernel(tc, qT, kT, cT, wT, mg, offs, offs2, ou
         scalar_gather(halves[0][:, :P], k_plane[2][:], entries(0, P))
         terms2 = {s: product(nc.vector, 2, s * HALF, (s + 1) * HALF, halves[s][:]) for s in (1, 0)}
 
-        picked = [sb.tile([P, P], F32, name="picked3_%d" % j, align_bytes=256) for j in range(GROUPS)]
-        for j in range(GROUPS):
-            gather = vector_gather if j < 2 else scalar_gather
+        picked = {j: sb.tile([P, P], F32, name="picked3_%d" % j, align_bytes=256) for j in range(GROUPS)}
+        for j in (0, 3, 2, 1):
+            gather = vector_gather if j in (0, 3) else scalar_gather
             gather(picked[j][:], k_plane[3][:], entries(j * P, (j + 1) * P))
         terms3 = {0: product(nc.gpsimd, 3, 0, P, picked[0][:])}
-        for j in (2, 1, 3):
+        for j in (2, 3):
             terms3[j] = product(nc.vector, 3, j * P, (j + 1) * P, picked[j][:], held[j][:])
 
         q_bf = [sb.tile([P, P * PACK], BF16, name="q_bf%d" % m, align_bytes=256) for m in range(q_tiles)]
@@ -172,20 +178,23 @@ def tile_attend_pre_rotate_f_topk_kernel(tc, qT, kT, cT, wT, mg, offs, offs2, ou
             nc.scalar.activation(q_bf[m][:].rearrange("p (c i t) -> p c t i", i=4, t=PACK),
                                  q_raw[m][:].rearrange("p t (c i) -> p c t i", i=4), ACT.Copy)
 
-        u_woven = sb.tile([P, HALF * PACK], BF16, name="u_woven", tag="q_raw1", align_bytes=256)
-        u = [u_direct[0][:], u_direct[1][:], u_woven[:, :P * PACK], u_woven[:, P * PACK:]]
+        last_term = late.tile([P, 2, P], F32, name="last_term", align_bytes=256, offset=0)
+        u_woven = late.tile([P, len(WOVEN), P * PACK], BF16, name="u_woven", align_bytes=256, offset=8 * P)
+        u = {j: u_woven[:, i, :] for i, j in enumerate(WOVEN)}
+        u[0] = u_first[:]
+        u[1] = u_last[:]
 
         def weave(j):
-            words = apart[:].rearrange("p h x -> p (h x)").bitcast(F32).rearrange("p (h n) -> p n h", h=PAIRS)
             nc.scalar.copy(u[j].bitcast(F32).rearrange("p (n h) -> p n h", h=PAIRS),
-                           words[:, j * P - HALF:(j + 1) * P - HALF, :])
+                           words[j].bitcast(F32).rearrange("p h n -> p n h"))
 
         def quantize_u(j):
             cols = slice(j * P, (j + 1) * P)
             nc.vector.quantize_mx(u_codes[:, cols].bitcast(FP8X4), u_scales[:, cols], u[j])
 
         def last_sum(j):
-            pair_sum(nc.vector, 1, j * P, (j + 1) * P, group_of(terms2, j), terms3[j][:])
+            target = whole_lines(1, words[j]) if j in WOVEN else in_place(1, u[j])
+            pair_sum(nc.vector, target, group_of(terms2, j), terms3[j][:])
 
         def quantize_q(m):
             nc.vector.quantize_mx(q_codes[:, m * P:(m + 1) * P].bitcast(FP8X4), q_scales[:, m * P:(m + 1) * P],
@@ -199,6 +208,8 @@ def tile_attend_pre_rotate_f_topk_kernel(tc, qT, kT, cT, wT, mg, offs, offs2, ou
         last_sum(3)
         weave(3)
         quantize_q(1)
+        nc.vector.tensor_tensor(last_term[:], held[1][:], picked[1][:].unsqueeze(1).to_broadcast([P, 2, P]), ALU.mult)
+        terms3[1] = last_term
         quantize_u(2)
         last_sum(1)
         quantize_u(3)
@@ -210,13 +221,13 @@ def tile_attend_pre_rotate_f_topk_kernel(tc, qT, kT, cT, wT, mg, offs, offs2, ou
             cols = slice(j * P, (j + 1) * P)
             for m in range(q_tiles):
                 rows = slice(m * P, (m + 1) * P)
-                score[j, m] = ps.tile([P, P], F32, name="score%d_%d" % (j, m), tag="bank%d" % (2 * i + m))
+                score[j, m] = ps.tile([P, P], F32, name="score%d_%d" % (j, m), tag="bank%d" % SCORE_BANKS[i][m])
                 nc.tensor.matmul_mx(score[j, m][:], lhsT=q_codes[:, rows].bitcast(FP8X4), lhsT_scale=q_scales[:, rows],
                                     rhs=u_codes[:, cols].bitcast(FP8X4), rhs_scale=u_scales[:, cols],
                                     start=True, stop=True)
                 nc.scalar.activation(sig[:, m, cols], score[j, m][:], ACT.Sigmoid, bias=neg_margin[:, m:m + 1])
 
-        v = sb.tile([P, q_tiles, SLOTS], F32, name="v", tag="u1", align_bytes=256)
+        v = sb.tile([P, q_tiles, SLOTS], F32, name="v", tag="u_last", align_bytes=256)
         log_sig = sb.tile([P, q_tiles, SLOTS], F32, name="log_sig", tag="codes", align_bytes=256)
         result = sb.tile([P, q_tiles, SLOTS], F32, name="result", align_bytes=256)
         for m in reversed(range(q_tiles)):

@@ -22,7 +22,7 @@ PER_COLUMN = 16
 FLOPS = 2 * D * NQ * SLOTS
 BYTES = 4 * (D * ENTITIES + D * RELATIONS + D * NQ + NQ + NQ * SLOTS) + 2 * 2 * P * SLOTS // PER_COLUMN
 
-NEG_SIN, COS, SIN = 0, 1, 2
+COS, SIN, NEG_COS = 0, 1, 2
 FINISH = (0, 2, 3, 1)
 WOVEN = (2, 3)
 SCORE_BANKS = [(0, 4), (5, 6), (7, 2), (3, 1)]
@@ -42,30 +42,23 @@ def tile_attend_pre_rotate_f_topk_kernel(tc, qT, kT, cT, wT, mg, offs, offs2, ou
         ent_list = sb.tile([P, SLOTS // PER_COLUMN], U16, name="ent_list")
         rel_list = sb.tile([P, SLOTS // PER_COLUMN], U16, name="rel_list")
         k_plane = [sb.tile([P, ENTITIES], F32, name="k%d" % t, align_bytes=256) for t in range(PACK)]
-        c_plane = [sb.tile([P, RELATIONS], F32, name="c%d" % h, align_bytes=256) for h in range(PAIRS)]
-        w_plane = [sb.tile([P, RELATIONS], F32, name="w%d" % h, align_bytes=256) for h in range(PAIRS)]
+        c_table = sb.tile([P, PAIRS, RELATIONS], F32, name="c_table", align_bytes=256)
+        w_table = sb.tile([P, PAIRS, RELATIONS], F32, name="w_table", align_bytes=256)
         k_rows = kT.rearrange("(p t) n -> p t n", t=PACK)
-        c_rows = cT.rearrange("(p t) n -> p t n", t=PACK)
-        w_rows = wT.rearrange("(p t) n -> p t n", t=PACK)
         q_raw = [sb.tile([P, PACK, P], F32, name="q_raw0", align_bytes=256),
                  late.tile([P, PACK, P], F32, name="q_raw1", align_bytes=256, offset=0)]
         margin_row = sb.tile([P, NQ], F32, name="margin_row")
-        margin = sb.tile([P, q_tiles], F32, name="margin")
         neg_margin = sb.tile([P, q_tiles], F32, name="neg_margin")
         floor = sb.tile([P, 1], F32, name="floor")
 
         nc.gpsimd.memset(margin_row[:], 0.0)
         nc.scalar.dma_start(margin_row[0:1, :], mg[0].rearrange("q o -> o q"))
-        nc.sync.dma_start(w_plane[1][:], w_rows[:, 2, :])
+        nc.sync.dma_start(w_table[:], wT.rearrange("(p t) n -> p t n", t=PACK)[:, 1:3, :])
         nc.sync.dma_start(rel_list[:], offs2)
-        nc.sync.dma_start(c_plane[0][:], c_rows[:, 0, :])
-        nc.sync.dma_start(w_plane[0][:], w_rows[:, 0, :])
+        nc.sync.dma_start(c_table[:], cT.rearrange("(p t) n -> p t n", t=PACK)[:, 1:3, :])
         nc.sync.dma_start(ent_list[:], offs)
-        nc.sync.dma_start(k_plane[0][:], k_rows[:, 0, :])
-        nc.sync.dma_start(k_plane[1][:], k_rows[:, 1, :])
-        nc.sync.dma_start(c_plane[1][:], c_rows[:, 2, :])
-        nc.sync.dma_start(k_plane[2][:], k_rows[:, 2, :])
-        nc.sync.dma_start(k_plane[3][:], k_rows[:, 3, :])
+        for t in range(PACK):
+            nc.sync.dma_start(k_plane[t][:], k_rows[:, t, :])
         for m in range(q_tiles):
             nc.sync.dma_start(q_raw[m][:], qT[0].rearrange("(p t) n -> p t n", t=PACK)[:, :, m * P:(m + 1) * P])
 
@@ -78,32 +71,19 @@ def tile_attend_pre_rotate_f_topk_kernel(tc, qT, kT, cT, wT, mg, offs, offs2, ou
         ident = sb.tile([P, P], F32, name="ident")
         make_identity(nc, ident[:])
 
-        margin_turned = ps.tile([P, q_tiles, P], F32, name="margin_turned", tag="bank0")
-        for m in range(q_tiles):
-            nc.tensor.transpose(margin_turned[:, m, :], margin_row[:, m * P:(m + 1) * P], ident[:])
-        nc.scalar.copy(margin[:], margin_turned[:, :, 0])
-        nc.scalar.activation(neg_margin[:], margin_turned[:, :, 0], ACT.Copy, scale=-1.0)
-
-        apart = sb.tile([P, PAIRS, HALF * 2], BF16, name="apart", align_bytes=256)
-        factors = [sb.tile([P, 3, SLOTS], F32, name="factors%d" % h, align_bytes=256) for h in range(PAIRS)]
-
         def vector_gather(target, window, entries):
             nc.vector.tensor_copy(target, window.indirect(entries))
 
         def scalar_gather(target, window, entries):
             nc.scalar.activation(target, window.indirect(entries), ACT.Copy)
 
-        def entries(lo, hi):
-            return ent_list[:, lo // PER_COLUMN:hi // PER_COLUMN]
+        def entries(offsets, lo, hi):
+            return offsets[:, lo // PER_COLUMN:hi // PER_COLUMN]
 
-        def first_factor(t):
-            return NEG_SIN if t % 2 else COS
-
-        def product(engine, t, lo, hi, picked, source=None):
-            term = sb.tile([P, 2, hi - lo], F32, name="term%d_%d" % (t, lo), tag="term%d_%d" % (t, lo), align_bytes=256)
-            if source is None:
-                source = factors[t // 2][:, first_factor(t):first_factor(t) + 2, lo:hi]
-            engine.tensor_tensor(term[:], source, picked.unsqueeze(1).to_broadcast([P, 2, hi - lo]), ALU.mult)
+        def product(engine, name, rows, picked):
+            width = picked.shape[1]
+            term = sb.tile([P, 2, width], F32, name=name, tag=name, align_bytes=256)
+            engine.tensor_tensor(term[:], rows, picked.unsqueeze(1).to_broadcast([P, 2, width]), ALU.mult)
             return term
 
         def whole_lines(h, words):
@@ -114,60 +94,94 @@ def tile_attend_pre_rotate_f_topk_kernel(tc, qT, kT, cT, wT, mg, offs, offs2, ou
 
         def pair_sum(engine, target, first, second):
             engine.tensor_tensor(target, first.rearrange("p e (c i) -> p c e i", i=2),
-                                 second.rearrange("p e (c i) -> p c e i", i=2), ALU.add)
+                                 second.rearrange("p e (c i) -> p c e i", i=2), ALU.subtract)
 
-        held = {j: ps.tile([P, 2, P], F32, name="held%d" % j, tag="bank%d" % j) for j in range(1, GROUPS)}
-
-        def hold(e, row):
-            across = ps.tile([P, GROUPS - 1, P], F32, name="across%d" % e, tag="bank%d" % (4 + e))
-            landed = sb.tile([P, GROUPS - 1, P], F32, name="landed%d" % e)
+        def turn(name, row, bank):
+            across = ps.tile([P, GROUPS - 1, P], F32, name="across_" + name, tag="bank%d" % bank)
             for j in range(1, GROUPS):
-                nc.tensor.transpose(across[:, j - 1, :], factors[1][:, row, j * P:(j + 1) * P], ident[:])
-            nc.scalar.copy(landed[:], across[:])
-            for j in range(1, GROUPS):
-                nc.tensor.transpose(held[j][:, e, :], landed[:, j - 1, :], ident[:])
+                nc.tensor.transpose(across[:, j - 1, :], row[:, j * P:(j + 1) * P], ident[:])
+            return across
 
-        vector_gather(factors[1][:, SIN, :], w_plane[1][:], rel_list[:])
-        nc.scalar.activation(factors[1][:, NEG_SIN, :], factors[1][:, SIN, :], ACT.Copy, scale=-1.0)
-        hold(0, NEG_SIN)
-        vector_gather(factors[0][:, COS, :], c_plane[0][:], rel_list[:])
-        scalar_gather(factors[0][:, SIN, :], w_plane[0][:], rel_list[:])
-        nc.scalar.activation(factors[0][:, NEG_SIN, :], factors[0][:, SIN, :], ACT.Copy, scale=-1.0)
+        def hold(name, across, sign, places, on_vector=False):
+            landed = sb.tile([P, GROUPS - 1, P], F32, name="landed_" + name)
+            if on_vector:
+                nc.vector.tensor_scalar(landed[:], across[:], sign, None, ALU.mult)
+            else:
+                nc.scalar.activation(landed[:], across[:], ACT.Copy, scale=sign)
+            for j, place in places:
+                nc.tensor.transpose(place, landed[:, j - 1, :], ident[:])
+
+        def upper(tile, e):
+            return [(j, tile[:, e, (j - 2) * P:(j - 1) * P]) for j in (2, 3)]
+
+        factors = [sb.tile([P, 3, SLOTS], F32, name="factors%d" % h, align_bytes=256) for h in range(PAIRS)]
+        odd0_1 = ps.tile([P, 2, P], F32, name="odd0_1", tag="bank6")
+        odd0_23 = ps.tile([P, 2, HALF], F32, name="odd0_23", tag="bank7")
+        held1 = ps.tile([P, 3, P], F32, name="held1", tag="bank1")
+        held_cw = ps.tile([P, 2, HALF], F32, name="held_cw", tag="bank3")
+        held_wc = ps.tile([P, 2, HALF], F32, name="held_wc", tag="bank2")
+
+        vector_gather(factors[0][:, SIN, :], w_table[:, 0, :], rel_list[:])
+        scalar_gather(factors[1][:, SIN, :], w_table[:, 1, :], rel_list[:])
+        w_across = [turn("w%d" % h, factors[h][:, SIN, :], 4 + h) for h in range(PAIRS)]
+        hold("w0", w_across[0], 1.0, [(1, odd0_1[:, 0, :])] + upper(odd0_23, 0), on_vector=True)
+        hold("w1", w_across[1], 1.0, [(1, held1[:, SIN, :])] + upper(held_cw, 1) + upper(held_wc, 0))
+        vector_gather(factors[0][:, COS, :], c_table[:, 0, :], rel_list[:])
+        scalar_gather(factors[1][:, COS, :], c_table[:, 1, :], rel_list[:])
+        for h in range(PAIRS):
+            nc.gpsimd.tensor_scalar(factors[h][:, NEG_COS, :P], factors[h][:, COS, :P], -1.0, 0.0, ALU.mult, ALU.add)
+        c0_across = turn("c0", factors[0][:, COS, :], 0)
+        c_across = turn("c1", factors[1][:, COS, :], 4)
+        hold("neg_c0", c0_across, -1.0, [(1, odd0_1[:, 1, :])] + upper(odd0_23, 1), on_vector=True)
 
         def shared_gather(t):
             halves = [sb.tile([P, HALF], F32, name="picked%d_%d" % (t, s), align_bytes=256) for s in range(2)]
-            scalar_gather(halves[0][:], k_plane[t][:], entries(0, HALF))
-            vector_gather(halves[1][:], k_plane[t][:], entries(HALF, SLOTS))
-            return {s: product(nc.vector, t, s * HALF, (s + 1) * HALF, halves[s][:]) for s in (1, 0)}
+            vector_gather(halves[0][:], k_plane[t][:], entries(ent_list, 0, HALF))
+            scalar_gather(halves[1][:], k_plane[t][:], entries(ent_list, HALF, SLOTS))
+            return halves
 
-        def group_of(terms, j):
-            s, first = divmod(j * P, HALF)
-            return terms[s][:, :, first:first + P]
+        halves = shared_gather(0)
+        term0 = [product(nc.vector, "term0_%d" % s, factors[0][:, 0:2, s * HALF:(s + 1) * HALF], halves[s][:])
+                 for s in (1, 0)][::-1]
 
-        terms0 = shared_gather(0)
-        terms1 = shared_gather(1)
-        scalar_gather(factors[1][:, COS, P:], c_plane[1][:], rel_list[:, P // PER_COLUMN:])
-        scalar_gather(factors[1][:, COS, :P], c_plane[1][:], rel_list[:, :P // PER_COLUMN])
+        hold("c1", c_across, 1.0, [(1, held1[:, COS, :])] + upper(held_cw, 0))
+        hold("neg_c1", c_across, -1.0, [(1, held1[:, NEG_COS, :])] + upper(held_wc, 1))
+        margin_turned = ps.tile([P, q_tiles, P], F32, name="margin_turned", tag="bank5")
+        for m in range(q_tiles):
+            nc.tensor.transpose(margin_turned[:, m, :], margin_row[:, m * P:(m + 1) * P], ident[:])
+        nc.scalar.activation(neg_margin[:], margin_turned[:, :, 0], ACT.Copy, scale=-1.0)
+
+        halves = shared_gather(1)
+        term1_0 = product(nc.gpsimd, "term1_0", factors[0][:, 1:3, :P], halves[0][:, :P])
+        term1_23 = product(nc.vector, "term1_23", odd0_23[:], halves[1][:])
+        term1_1 = product(nc.vector, "term1_1", odd0_1[:], halves[0][:, P:])
+
+        apart = sb.tile([P, PAIRS, HALF * 2], BF16, name="apart", align_bytes=256)
         u_last = sb.tile([P, P * PACK], BF16, name="u_last", tag="u_last", align_bytes=256)
-        pair_sum(nc.vector, in_place(0, u_last[:]), terms0[0][:, :, P:], terms1[0][:, :, P:])
-        pair_sum(nc.vector, whole_lines(0, apart), terms0[1][:], terms1[1][:])
-        u_first = sb.tile([P, P * PACK], BF16, name="u_first", tag="term1_%d" % HALF, align_bytes=256)
-        pair_sum(nc.gpsimd, in_place(0, u_first[:]), terms0[0][:, :, :P], terms1[0][:, :, :P])
+        pair_sum(nc.vector, whole_lines(0, apart), term0[1][:], term1_23[:])
+        pair_sum(nc.vector, in_place(0, u_last[:]), term0[0][:, :, P:], term1_1[:])
+        u_first = sb.tile([P, P * PACK], BF16, name="u_first", tag="term1_1", align_bytes=256)
+        pair_sum(nc.gpsimd, in_place(0, u_first[:]), term0[0][:, :, :P], term1_0[:])
         words = {2: apart[:, :, :2 * P], 3: apart[:, :, 2 * P:]}
-        hold(1, COS)
-        halves = [sb.tile([P, HALF], F32, name="picked2_%d" % s, align_bytes=256) for s in range(2)]
-        vector_gather(halves[1][:], k_plane[2][:], entries(HALF, SLOTS))
-        vector_gather(halves[0][:, P:], k_plane[2][:], entries(P, HALF))
-        scalar_gather(halves[0][:, :P], k_plane[2][:], entries(0, P))
-        terms2 = {s: product(nc.vector, 2, s * HALF, (s + 1) * HALF, halves[s][:]) for s in (1, 0)}
+
+        parts = {lo: sb.tile([P, hi - lo], F32, name="picked2_%d" % lo, align_bytes=256)
+                 for lo, hi in ((0, P), (P, HALF), (HALF, SLOTS))}
+        vector_gather(parts[0][:], k_plane[2][:], entries(ent_list, 0, P))
+        scalar_gather(parts[HALF][:], k_plane[2][:], entries(ent_list, HALF, SLOTS))
+        scalar_gather(parts[P][:], k_plane[2][:], entries(ent_list, P, HALF))
+        term2_23 = product(nc.vector, "term2_23", held_cw[:], parts[HALF][:])
+        terms2 = {0: product(nc.gpsimd, "term2_0", factors[1][:, 0:2, :P], parts[0][:])[:],
+                  1: product(nc.vector, "term2_1", held1[:, 0:2, :], parts[P][:])[:]}
+        for j in (2, 3):
+            terms2[j] = term2_23[:, :, (j - 2) * P:(j - 1) * P]
 
         picked = {j: sb.tile([P, P], F32, name="picked3_%d" % j, align_bytes=256) for j in range(GROUPS)}
         for j in (0, 3, 2, 1):
             gather = vector_gather if j in (0, 3) else scalar_gather
-            gather(picked[j][:], k_plane[3][:], entries(j * P, (j + 1) * P))
-        terms3 = {0: product(nc.gpsimd, 3, 0, P, picked[0][:])}
+            gather(picked[j][:], k_plane[3][:], entries(ent_list, j * P, (j + 1) * P))
+        terms3 = {0: product(nc.gpsimd, "term3_0", factors[1][:, 1:3, :P], picked[0][:])}
         for j in (2, 3):
-            terms3[j] = product(nc.vector, 3, j * P, (j + 1) * P, picked[j][:], held[j][:])
+            terms3[j] = product(nc.vector, "term3_%d" % j, held_wc[:, :, (j - 2) * P:(j - 1) * P], picked[j][:])
 
         q_bf = [sb.tile([P, P * PACK], BF16, name="q_bf%d" % m, align_bytes=256) for m in range(q_tiles)]
         q_codes = sb.tile([P, NQ], U32, name="q_codes", align_bytes=256)
@@ -194,7 +208,7 @@ def tile_attend_pre_rotate_f_topk_kernel(tc, qT, kT, cT, wT, mg, offs, offs2, ou
 
         def last_sum(j):
             target = whole_lines(1, words[j]) if j in WOVEN else in_place(1, u[j])
-            pair_sum(nc.vector, target, group_of(terms2, j), terms3[j][:])
+            pair_sum(nc.vector, target, terms2[j], terms3[j][:])
 
         def quantize_q(m):
             nc.vector.quantize_mx(q_codes[:, m * P:(m + 1) * P].bitcast(FP8X4), q_scales[:, m * P:(m + 1) * P],
@@ -208,7 +222,8 @@ def tile_attend_pre_rotate_f_topk_kernel(tc, qT, kT, cT, wT, mg, offs, offs2, ou
         last_sum(3)
         weave(3)
         quantize_q(1)
-        nc.vector.tensor_tensor(last_term[:], held[1][:], picked[1][:].unsqueeze(1).to_broadcast([P, 2, P]), ALU.mult)
+        nc.vector.tensor_tensor(last_term[:], held1[:, 1:3, :], picked[1][:].unsqueeze(1).to_broadcast([P, 2, P]),
+                                ALU.mult)
         terms3[1] = last_term
         quantize_u(2)
         last_sum(1)
@@ -232,8 +247,8 @@ def tile_attend_pre_rotate_f_topk_kernel(tc, qT, kT, cT, wT, mg, offs, offs2, ou
         result = sb.tile([P, q_tiles, SLOTS], F32, name="result", align_bytes=256)
         for m in reversed(range(q_tiles)):
             for j in FINISH:
-                nc.vector.tensor_scalar(v[:, m, j * P:(j + 1) * P], score[j, m][:], -1.0, margin[:, m:m + 1],
-                                        ALU.mult, ALU.add)
+                nc.vector.tensor_scalar(v[:, m, j * P:(j + 1) * P], score[j, m][:], neg_margin[:, m:m + 1], -1.0,
+                                        ALU.add, ALU.mult)
         for m, lo, hi in PIECES:
             nc.scalar.activation(log_sig[:, m, lo:hi], sig[:, m, lo:hi], ACT.Ln, bias=floor[:])
             nc.vector.scalar_tensor_tensor(result[:, m, lo:hi], log_sig[:, m, lo:hi], -1.0, v[:, m, lo:hi],

@@ -166,9 +166,9 @@ def tile_attend_pre_rotate_f_topk_kernel(tc, qT, kT, cT, wT, mg, offs, offs2, ou
 
         parts = {lo: sb.tile([P, hi - lo], F32, name="picked2_%d" % lo, align_bytes=256)
                  for lo, hi in ((0, P), (P, HALF), (HALF, SLOTS))}
-        vector_gather(parts[0][:], k_plane[2][:], entries(ent_list, 0, P))
         scalar_gather(parts[HALF][:], k_plane[2][:], entries(ent_list, HALF, SLOTS))
         scalar_gather(parts[P][:], k_plane[2][:], entries(ent_list, P, HALF))
+        scalar_gather(parts[0][:], k_plane[2][:], entries(ent_list, 0, P))
         term2_23 = product(nc.vector, "term2_23", held_cw[:], parts[HALF][:])
         terms2 = {0: product(nc.gpsimd, "term2_0", factors[1][:, 0:2, :P], parts[0][:])[:],
                   1: product(nc.vector, "term2_1", held1[:, 0:2, :], parts[P][:])[:]}

@@ -45,8 +45,7 @@ def tile_attend_pre_rotate_f_topk_kernel(tc, qT, kT, cT, wT, mg, offs, offs2, ou
         c_table = sb.tile([P, PAIRS, RELATIONS], F32, name="c_table", align_bytes=256)
         w_table = sb.tile([P, PAIRS, RELATIONS], F32, name="w_table", align_bytes=256)
         k_rows = kT.rearrange("(p t) n -> p t n", t=PACK)
-        q_raw = [sb.tile([P, PACK, P], F32, name="q_raw0", align_bytes=256),
-                 late.tile([P, PACK, P], F32, name="q_raw1", align_bytes=256, offset=0)]
+        q_raw = late.tile([P, PACK, NQ], F32, name="q_raw", align_bytes=256, offset=0)
         margin_row = sb.tile([P, NQ], F32, name="margin_row")
         neg_margin = sb.tile([P, q_tiles], F32, name="neg_margin")
         floor = sb.tile([P, 1], F32, name="floor")
@@ -59,8 +58,7 @@ def tile_attend_pre_rotate_f_topk_kernel(tc, qT, kT, cT, wT, mg, offs, offs2, ou
         nc.sync.dma_start(ent_list[:], offs)
         for t in range(PACK):
             nc.sync.dma_start(k_plane[t][:], k_rows[:, t, :])
-        for m in range(q_tiles):
-            nc.sync.dma_start(q_raw[m][:], qT[0].rearrange("(p t) n -> p t n", t=PACK)[:, :, m * P:(m + 1) * P])
+        nc.sync.dma_start(q_raw[:], qT[0].rearrange("(p t) n -> p t n", t=PACK))
 
         zero = sb.tile([P, 1], F32, name="zero")
         nc.gpsimd.memset(zero[:], 0.0)
@@ -156,7 +154,7 @@ def tile_attend_pre_rotate_f_topk_kernel(tc, qT, kT, cT, wT, mg, offs, offs2, ou
         term1_23 = product(nc.vector, "term1_23", odd0_23[:], halves[1][:])
         term1_1 = product(nc.vector, "term1_1", odd0_1[:], halves[0][:, P:])
 
-        apart = sb.tile([P, PAIRS, HALF * 2], BF16, name="apart", align_bytes=256)
+        apart = sb.tile([P, PAIRS, HALF * 2], BF16, name="apart", tag="apart", align_bytes=256)
         u_last = sb.tile([P, P * PACK], BF16, name="u_last", tag="u_last", align_bytes=256)
         pair_sum(nc.vector, whole_lines(0, apart), term0[1][:], term1_23[:])
         pair_sum(nc.vector, in_place(0, u_last[:]), term0[0][:, :, P:], term1_1[:])
@@ -176,8 +174,8 @@ def tile_attend_pre_rotate_f_topk_kernel(tc, qT, kT, cT, wT, mg, offs, offs2, ou
             terms2[j] = term2_23[:, :, (j - 2) * P:(j - 1) * P]
 
         picked = {j: sb.tile([P, P], F32, name="picked3_%d" % j, align_bytes=256) for j in range(GROUPS)}
-        for j in (0, 3, 2, 1):
-            gather = vector_gather if j in (0, 3) else scalar_gather
+        for j in (0, 2, 3, 1):
+            gather = vector_gather if j == 0 else scalar_gather
             gather(picked[j][:], k_plane[3][:], entries(ent_list, j * P, (j + 1) * P))
         terms3 = {0: product(nc.gpsimd, "term3_0", factors[1][:, 1:3, :P], picked[0][:])}
         for j in (2, 3):
@@ -190,7 +188,7 @@ def tile_attend_pre_rotate_f_topk_kernel(tc, qT, kT, cT, wT, mg, offs, offs2, ou
         u_scales = sb.tile([P, SLOTS], U8, name="u_scales", align_bytes=256)
         for m in range(q_tiles):
             nc.scalar.activation(q_bf[m][:].rearrange("p (c i t) -> p c t i", i=4, t=PACK),
-                                 q_raw[m][:].rearrange("p t (c i) -> p c t i", i=4), ACT.Copy)
+                                 q_raw[:, :, m * P:(m + 1) * P].rearrange("p t (c i) -> p c t i", i=4), ACT.Copy)
 
         last_term = late.tile([P, 2, P], F32, name="last_term", align_bytes=256, offset=0)
         u_woven = late.tile([P, len(WOVEN), P * PACK], BF16, name="u_woven", align_bytes=256, offset=8 * P)
@@ -230,7 +228,7 @@ def tile_attend_pre_rotate_f_topk_kernel(tc, qT, kT, cT, wT, mg, offs, offs2, ou
         quantize_u(3)
         quantize_u(1)
 
-        sig = sb.tile([P, q_tiles, SLOTS], F32, name="sig", align_bytes=256)
+        sig = sb.tile([P, q_tiles, SLOTS], F32, name="sig", tag="apart", align_bytes=256)
         score = {}
         for i, j in enumerate(FINISH):
             cols = slice(j * P, (j + 1) * P)

@@ -174,8 +174,8 @@ def tile_attend_pre_rotate_f_topk_kernel(tc, qT, kT, cT, wT, mg, offs, offs2, ou
             terms2[j] = term2_23[:, :, (j - 2) * P:(j - 1) * P]
 
         picked = {j: sb.tile([P, P], F32, name="picked3_%d" % j, align_bytes=256) for j in range(GROUPS)}
-        for j in (0, 2, 3, 1):
-            gather = vector_gather if j == 0 else scalar_gather
+        for j in (0, 3, 2, 1):
+            gather = vector_gather if j in (0, 3) else scalar_gather
             gather(picked[j][:], k_plane[3][:], entries(ent_list, j * P, (j + 1) * P))
         terms3 = {0: product(nc.gpsimd, "term3_0", factors[1][:, 1:3, :P], picked[0][:])}
         for j in (2, 3):

from contextlib import ExitStack

import concourse.mybir as mybir
from concourse.masks import make_identity

F32 = mybir.dt.float32
BF16 = mybir.dt.bfloat16
U32 = mybir.dt.uint32
U16 = mybir.dt.uint16
U8 = mybir.dt.uint8
FP8X4 = mybir.dt.float8_e4m3fn_x4
ALU = mybir.AluOpType
ACT = mybir.ActivationFunctionType

P = 128
PACK = 4
PAIRS = PACK // 2
D, NQ, SLOTS, ENTITIES, RELATIONS = 512, 256, 512, 2048, 1024
HALF = SLOTS // 2
GROUPS = SLOTS // P
PER_COLUMN = 16
FLOPS = 2 * D * NQ * SLOTS
BYTES = 4 * (D * ENTITIES + D * RELATIONS + D * NQ + NQ + NQ * SLOTS) + 2 * 2 * P * SLOTS // PER_COLUMN

COS, SIN, NEG_COS = 0, 1, 2
FINISH = (0, 2, 3, 1)
WOVEN = (2, 3)
SCORE_BANKS = [(0, 4), (5, 6), (7, 2), (3, 1)]
PIECES = [(1, 0, 128), (1, 128, 320), (1, 320, 512), (0, 0, 192), (0, 192, 384), (0, 384, 512)]
TWICE_FLOOR = 2.0 ** -59


def tile_attend_pre_rotate_f_topk_kernel(tc, qT, kT, cT, wT, mg, offs, offs2, out):
    nc = tc.nc
    q_tiles = NQ // P

    with ExitStack() as ctx:
        sb = ctx.enter_context(tc.tile_pool(name="sb", bufs=1))
        late = ctx.enter_context(tc.tile_pool(name="late", bufs=1))
        ps = ctx.enter_context(tc.psum_pool(name="ps", bufs=1))

        ent_list = sb.tile([P, SLOTS // PER_COLUMN], U16, name="ent_list")
        rel_list = sb.tile([P, SLOTS // PER_COLUMN], U16, name="rel_list")
        k_plane = [sb.tile([P, ENTITIES], F32, name="k%d" % t, align_bytes=256) for t in range(PACK)]
        c_table = sb.tile([P, PAIRS, RELATIONS], F32, name="c_table", align_bytes=256)
        w_table = sb.tile([P, PAIRS, RELATIONS], F32, name="w_table", align_bytes=256)
        k_rows = kT.rearrange("(p t) n -> p t n", t=PACK)
        q_raw = late.tile([P, PACK, NQ], F32, name="q_raw", align_bytes=256, offset=0)
        margin_row = sb.tile([P, NQ], F32, name="margin_row")
        neg_margin = sb.tile([P, q_tiles], F32, name="neg_margin")
        floor = sb.tile([P, 1], F32, name="floor")

        nc.gpsimd.memset(margin_row[:], 0.0)
        nc.scalar.dma_start(margin_row[0:1, :], mg[0].rearrange("q o -> o q"))
        nc.sync.dma_start(w_table[:], wT.rearrange("(p t) n -> p t n", t=PACK)[:, 1:3, :])
        nc.sync.dma_start(rel_list[:], offs2)
        nc.sync.dma_start(c_table[:], cT.rearrange("(p t) n -> p t n", t=PACK)[:, 1:3, :])
        nc.sync.dma_start(ent_list[:], offs)
        for t in range(PACK):
            nc.sync.dma_start(k_plane[t][:], k_rows[:, t, :])
        nc.sync.dma_start(q_raw[:], qT[0].rearrange("(p t) n -> p t n", t=PACK))

        zero = sb.tile([P, 1], F32, name="zero")
        nc.gpsimd.memset(zero[:], 0.0)
        one_half = sb.tile([P, 1], F32, name="one_half")
        nc.scalar.activation(one_half[:], zero[:], ACT.Sigmoid)
        nc.scalar.activation(floor[:], one_half[:], ACT.Copy, scale=TWICE_FLOOR)

        ident = sb.tile([P, P], F32, name="ident")
        make_identity(nc, ident[:])

        def vector_gather(target, window, entries):
            nc.vector.tensor_copy(target, window.indirect(entries))

        def scalar_gather(target, window, entries):
            nc.scalar.activation(target, window.indirect(entries), ACT.Copy)

        def entries(offsets, lo, hi):
            return offsets[:, lo // PER_COLUMN:hi // PER_COLUMN]

        def product(engine, name, rows, picked):
            width = picked.shape[1]
            term = sb.tile([P, 2, width], F32, name=name, tag=name, align_bytes=256)
            engine.tensor_tensor(term[:], rows, picked.unsqueeze(1).to_broadcast([P, 2, width]), ALU.mult)
            return term

        def whole_lines(h, words):
            return words[:, h, :].rearrange("p (c i e) -> p c e i", i=2, e=2)

        def in_place(h, slots):
            return slots.rearrange("p (c i h e) -> p h c e i", i=2, h=PAIRS, e=2)[:, h]

        def pair_sum(engine, target, first, second):
            engine.tensor_tensor(target, first.rearrange("p e (c i) -> p c e i", i=2),
                                 second.rearrange("p e (c i) -> p c e i", i=2), ALU.subtract)

        def turn(name, row, bank):
            across = ps.tile([P, GROUPS - 1, P], F32, name="across_" + name, tag="bank%d" % bank)
            for j in range(1, GROUPS):
                nc.tensor.transpose(across[:, j - 1, :], row[:, j * P:(j + 1) * P], ident[:])
            return across

        def hold(name, across, sign, places, on_vector=False):
            landed = sb.tile([P, GROUPS - 1, P], F32, name="landed_" + name)
            if on_vector:
                nc.vector.tensor_scalar(landed[:], across[:], sign, None, ALU.mult)
            else:
                nc.scalar.activation(landed[:], across[:], ACT.Copy, scale=sign)
            for j, place in places:
                nc.tensor.transpose(place, landed[:, j - 1, :], ident[:])

        def upper(tile, e):
            return [(j, tile[:, e, (j - 2) * P:(j - 1) * P]) for j in (2, 3)]

        factors = [sb.tile([P, 3, SLOTS], F32, name="factors%d" % h, align_bytes=256) for h in range(PAIRS)]
        odd0_1 = ps.tile([P, 2, P], F32, name="odd0_1", tag="bank6")
        odd0_23 = ps.tile([P, 2, HALF], F32, name="odd0_23", tag="bank7")
        held1 = ps.tile([P, 3, P], F32, name="held1", tag="bank1")
        held_cw = ps.tile([P, 2, HALF], F32, name="held_cw", tag="bank3")
        held_wc = ps.tile([P, 2, HALF], F32, name="held_wc", tag="bank2")

        vector_gather(factors[0][:, SIN, :], w_table[:, 0, :], rel_list[:])
        scalar_gather(factors[1][:, SIN, :], w_table[:, 1, :], rel_list[:])
        w_across = [turn("w%d" % h, factors[h][:, SIN, :], 4 + h) for h in range(PAIRS)]
        hold("w0", w_across[0], 1.0, [(1, odd0_1[:, 0, :])] + upper(odd0_23, 0), on_vector=True)
        hold("w1", w_across[1], 1.0, [(1, held1[:, SIN, :])] + upper(held_cw, 1) + upper(held_wc, 0))
        vector_gather(factors[0][:, COS, :], c_table[:, 0, :], rel_list[:])
        scalar_gather(factors[1][:, COS, :], c_table[:, 1, :], rel_list[:])
        for h in range(PAIRS):
            nc.gpsimd.tensor_scalar(factors[h][:, NEG_COS, :P], factors[h][:, COS, :P], -1.0, 0.0, ALU.mult, ALU.add)
        c0_across = turn("c0", factors[0][:, COS, :], 0)
        c_across = turn("c1", factors[1][:, COS, :], 4)
        hold("neg_c0", c0_across, -1.0, [(1, odd0_1[:, 1, :])] + upper(odd0_23, 1), on_vector=True)

        def shared_gather(t):
            halves = [sb.tile([P, HALF], F32, name="picked%d_%d" % (t, s), align_bytes=256) for s in range(2)]
            vector_gather(halves[0][:], k_plane[t][:], entries(ent_list, 0, HALF))
            scalar_gather(halves[1][:], k_plane[t][:], entries(ent_list, HALF, SLOTS))
            return halves

        halves = shared_gather(0)
        term0 = [product(nc.vector, "term0_%d" % s, factors[0][:, 0:2, s * HALF:(s + 1) * HALF], halves[s][:])
                 for s in (1, 0)][::-1]

        hold("c1", c_across, 1.0, [(1, held1[:, COS, :])] + upper(held_cw, 0))
        hold("neg_c1", c_across, -1.0, [(1, held1[:, NEG_COS, :])] + upper(held_wc, 1))
        margin_turned = ps.tile([P, q_tiles, P], F32, name="margin_turned", tag="bank5")
        for m in range(q_tiles):
            nc.tensor.transpose(margin_turned[:, m, :], margin_row[:, m * P:(m + 1) * P], ident[:])
        nc.scalar.activation(neg_margin[:], margin_turned[:, :, 0], ACT.Copy, scale=-1.0)

        halves = shared_gather(1)
        term1_0 = product(nc.gpsimd, "term1_0", factors[0][:, 1:3, :P], halves[0][:, :P])
        term1_23 = product(nc.vector, "term1_23", odd0_23[:], halves[1][:])
        term1_1 = product(nc.vector, "term1_1", odd0_1[:], halves[0][:, P:])

        apart = sb.tile([P, PAIRS, HALF * 2], BF16, name="apart", tag="apart", align_bytes=256)
        u_last = sb.tile([P, P * PACK], BF16, name="u_last", tag="u_last", align_bytes=256)
        pair_sum(nc.vector, whole_lines(0, apart), term0[1][:], term1_23[:])
        pair_sum(nc.vector, in_place(0, u_last[:]), term0[0][:, :, P:], term1_1[:])
        u_first = sb.tile([P, P * PACK], BF16, name="u_first", tag="term1_1", align_bytes=256)
        pair_sum(nc.gpsimd, in_place(0, u_first[:]), term0[0][:, :, :P], term1_0[:])
        words = {2: apart[:, :, :2 * P], 3: apart[:, :, 2 * P:]}

        parts = {lo: sb.tile([P, hi - lo], F32, name="picked2_%d" % lo, align_bytes=256)
                 for lo, hi in ((0, P), (P, HALF), (HALF, SLOTS))}
        scalar_gather(parts[HALF][:], k_plane[2][:], entries(ent_list, HALF, SLOTS))
        scalar_gather(parts[P][:], k_plane[2][:], entries(ent_list, P, HALF))
        scalar_gather(parts[0][:], k_plane[2][:], entries(ent_list, 0, P))
        term2_23 = product(nc.vector, "term2_23", held_cw[:], parts[HALF][:])
        terms2 = {0: product(nc.gpsimd, "term2_0", factors[1][:, 0:2, :P], parts[0][:])[:],
                  1: product(nc.vector, "term2_1", held1[:, 0:2, :], parts[P][:])[:]}
        for j in (2, 3):
            terms2[j] = term2_23[:, :, (j - 2) * P:(j - 1) * P]

        picked = {j: sb.tile([P, P], F32, name="picked3_%d" % j, align_bytes=256) for j in range(GROUPS)}
        for j in (0, 3, 2, 1):
            gather = vector_gather if j in (0, 3) else scalar_gather
            gather(picked[j][:], k_plane[3][:], entries(ent_list, j * P, (j + 1) * P))
        terms3 = {0: product(nc.gpsimd, "term3_0", factors[1][:, 1:3, :P], picked[0][:])}
        for j in (2, 3):
            terms3[j] = product(nc.vector, "term3_%d" % j, held_wc[:, :, (j - 2) * P:(j - 1) * P], picked[j][:])

        q_bf = [sb.tile([P, P * PACK], BF16, name="q_bf%d" % m, align_bytes=256) for m in range(q_tiles)]
        q_codes = sb.tile([P, NQ], U32, name="q_codes", align_bytes=256)
        q_scales = sb.tile([P, NQ], U8, name="q_scales", align_bytes=256)
        u_codes = sb.tile([P, SLOTS], U32, name="u_codes", tag="codes", align_bytes=256)
        u_scales = sb.tile([P, SLOTS], U8, name="u_scales", align_bytes=256)
        for m in range(q_tiles):
            nc.scalar.activation(q_bf[m][:].rearrange("p (c i t) -> p c t i", i=4, t=PACK),
                                 q_raw[:, :, m * P:(m + 1) * P].rearrange("p t (c i) -> p c t i", i=4), ACT.Copy)

        last_term = late.tile([P, 2, P], F32, name="last_term", align_bytes=256, offset=0)
        u_woven = late.tile([P, len(WOVEN), P * PACK], BF16, name="u_woven", align_bytes=256, offset=8 * P)
        u = {j: u_woven[:, i, :] for i, j in enumerate(WOVEN)}
        u[0] = u_first[:]
        u[1] = u_last[:]

        def weave(j):
            nc.scalar.copy(u[j].bitcast(F32).rearrange("p (n h) -> p n h", h=PAIRS),
                           words[j].bitcast(F32).rearrange("p h n -> p n h"))

        def quantize_u(j):
            cols = slice(j * P, (j + 1) * P)
            nc.vector.quantize_mx(u_codes[:, cols].bitcast(FP8X4), u_scales[:, cols], u[j])

        def last_sum(j):
            target = whole_lines(1, words[j]) if j in WOVEN else in_place(1, u[j])
            pair_sum(nc.vector, target, terms2[j], terms3[j][:])

        def quantize_q(m):
            nc.vector.quantize_mx(q_codes[:, m * P:(m + 1) * P].bitcast(FP8X4), q_scales[:, m * P:(m + 1) * P],
                                  q_bf[m][:])

        last_sum(2)
        weave(2)
        last_sum(0)
        quantize_q(0)
        quantize_u(0)
        last_sum(3)
        weave(3)
        quantize_q(1)
        nc.vector.tensor_tensor(last_term[:], held1[:, 1:3, :], picked[1][:].unsqueeze(1).to_broadcast([P, 2, P]),
                                ALU.mult)
        terms3[1] = last_term
        quantize_u(2)
        last_sum(1)
        quantize_u(3)
        quantize_u(1)

        sig = sb.tile([P, q_tiles, SLOTS], F32, name="sig", tag="apart", align_bytes=256)
        score = {}
        for i, j in enumerate(FINISH):
            cols = slice(j * P, (j + 1) * P)
            for m in range(q_tiles):
                rows = slice(m * P, (m + 1) * P)
                score[j, m] = ps.tile([P, P], F32, name="score%d_%d" % (j, m), tag="bank%d" % SCORE_BANKS[i][m])
                nc.tensor.matmul_mx(score[j, m][:], lhsT=q_codes[:, rows].bitcast(FP8X4), lhsT_scale=q_scales[:, rows],
                                    rhs=u_codes[:, cols].bitcast(FP8X4), rhs_scale=u_scales[:, cols],
                                    start=True, stop=True)
                nc.scalar.activation(sig[:, m, cols], score[j, m][:], ACT.Sigmoid, bias=neg_margin[:, m:m + 1])

        v = sb.tile([P, q_tiles, SLOTS], F32, name="v", tag="u_last", align_bytes=256)
        log_sig = sb.tile([P, q_tiles, SLOTS], F32, name="log_sig", tag="codes", align_bytes=256)
        result = sb.tile([P, q_tiles, SLOTS], F32, name="result", align_bytes=256)
        for m in reversed(range(q_tiles)):
            for j in FINISH:
                nc.vector.tensor_scalar(v[:, m, j * P:(j + 1) * P], score[j, m][:], neg_margin[:, m:m + 1], -1.0,
                                        ALU.add, ALU.mult)
        for m, lo, hi in PIECES:
            nc.scalar.activation(log_sig[:, m, lo:hi], sig[:, m, lo:hi], ACT.Ln, bias=floor[:])
            nc.vector.scalar_tensor_tensor(result[:, m, lo:hi], log_sig[:, m, lo:hi], -1.0, v[:, m, lo:hi],
                                           ALU.mult, ALU.max)
            nc.sync.dma_start(out[0, m * P:(m + 1) * P, lo:hi], result[:, m, lo:hi])
